import numpy as np, ml_dtypes
CORES = [35,38,43,46]
N = 4
import mx_ref
BF = ml_dtypes.bfloat16
def gcols(t, e):
    v = np.concatenate([t.reshape(8, 16, -1, 4), np.zeros((8, 16, 1, 4), BF)], axis=2)
    return np.ascontiguousarray(np.stack([v[g][:, e[g]] for g in range(8)])).reshape(128, -1)
def tile(rs):
    return np.stack(rs, axis=2).reshape(128, -1).astype(BF)
def cut(t, i, w=512):
    return t[:, w * i:w * i + w]
def pick(q, e):
    c = np.concatenate([q[0].reshape(128, -1, 4), np.zeros((128, 1, 4), np.uint8)], axis=1); s = np.concatenate([q[1], np.ones((16, 1), np.uint8)], axis=1)
    return (np.ascontiguousarray(c[:, e].reshape(128, -1)), np.ascontiguousarray(s[:, e]))
def join(*qs):
    return (np.concatenate([q[0] for q in qs], axis=1), np.concatenate([q[1] for q in qs], axis=1))
def put(q, e, v):
    c, s = q[0].reshape(128, -1, 4).copy(), q[1].copy(); c[:, e] = v[0].reshape(128, -1, 4); s[:, e] = v[1]
    return (c.reshape(128, -1), s)
def pk(c, s):
    return (np.ascontiguousarray(c), mx_ref.live(s))
def emit(q):
    return q[0], q[1]
def packed(v, rng):
    q = [mx_ref.quantize(np.ascontiguousarray(v[r])) for r in range(N)]
    return np.stack([a for a, b in q]), np.stack([mx_ref.plane(b, rng) for a, b in q])
def values_of_codes():
    e, c = np.zeros((128, 128, 4), np.float32), np.zeros((128, 2, 4), np.uint8)
    e[np.arange(128), np.arange(128), 0] = 1
    c[:127, :, 0] = np.arange(256).reshape(2, 128).T[:127]
    return mx_ref.matmul(mx_ref.quantize(e.reshape(128, 512).astype(BF)), (c.reshape(128, 8), np.full((16, 2), 127, np.uint8))).T.reshape(-1).astype(np.float64)
CODE_VALUE, SCALE_VALUE = values_of_codes(), 2.0 ** (np.arange(256) - 127.0)
def decode(q):
    return (CODE_VALUE[q[0]].reshape(16, 8, -1, 4) * SCALE_VALUE[q[1]][:, None, :, None] + 0.0).reshape(128, -1).astype(np.float32)
def f(rng, *shape):
    return mx_ref.flush((rng.standard_normal(shape, dtype=np.float32) * np.exp2(rng.integers(-2, 3, shape[:-1] + (1,)))).astype(BF))
def wide(rng, *shape, cols=0):
    v = rng.standard_normal(shape, dtype=np.float32) * np.exp2(rng.integers(-12, 13, shape)).astype(np.float32)
    if cols: v *= np.repeat(np.exp2(rng.integers(-cols, cols + 1, shape[:-2] + (1, shape[-1] // 4))) * (rng.random(shape[:-2] + (1, shape[-1] // 4)) > 0.0625), 4, axis=-1).astype(np.float32)
    return mx_ref.flush(v.astype(BF))
C, K, R = 384, 48, 2
def partner(r, t):
    return r ^ (1 << t)
def highest(p):
    return np.argsort(-(p[::16] + np.float32(0.0)), axis=1, kind="stable")[:, :K]
def warp(own, other):
    n = len(own)
    rows, i = np.arange(n), np.argsort(own, axis=1)
    a, b = np.take_along_axis(own, i, axis=1), np.take_along_axis(other, i, axis=1)
    length, back = np.ones((n, K), np.int64), np.full((n, K), -1)
    for j in range(1, K):
        l = np.where(b[:, :j] < b[:, j:j + 1], length[:, :j], 0)
        best = np.argmax(l, axis=1)
        length[:, j] = 1 + l[rows, best]
        back[:, j] = np.where(l[rows, best] > 0, best, -1)
    on = np.zeros((n, K), bool)
    e = np.argmax(length, axis=1)
    for j in range(K):
        on[rows[e >= 0], e[e >= 0]] = True
        e = np.where(e >= 0, back[rows, e], -1)
    w, p = np.zeros((n, C), np.int64), np.arange(C)
    for k in range(n):
        c, d = a[k][on[k]], b[k][on[k]]
        i = np.searchsorted(c, p, side="right") - 1
        w[k] = np.where(i < 0, np.maximum(0, d[0] - c[0] + p), np.minimum(d[i] + p - c[i], np.append(d[1:] - 1, C - 1)[i]))
    return w
def clear(v):
    v = v.astype(np.float32)
    v[np.abs(v) < np.float32(2.0 ** -16)] = 0
    return v.astype(BF)
def numbers_of(rng):
    return {"x": clear(f(rng, N, 128, 4 * C)), "u": np.array(f(rng, N, 128, 512)), "v": np.array(f(rng, N, 128, 512))}
def weights(rng, w):
    c, p = packed(w, rng)
    return {"wc": c, "ws": p}
def quiet(rng, a, b):
    w = np.array(f(rng, N, 128, 2048)).reshape(N, 8, 16, 4, 8, 16, 4)
    w[:, :, 0] = 0
    w[:, :, :, :, :, :a] = 0
    w[:, :, :, :, :, b:] = 0
    return weights(rng, w.reshape(N, 128, 2048))
def signs(rng):
    return np.stack([rng.permutation(8) % 2 * 2.0 - 1.0 for r in range(N)])
def planted(d, rng, s, m, unit, k):
    x = d["x"].astype(np.float32).reshape(N, 8, 16, C, 4)
    g = ((s[..., None] >> np.arange(8)) & 1) * 2.0 ** np.arange(8) * unit[:, None, None, None]
    x[:, :, 0] = 0
    x[:, :, 0, :, 0] = m
    x[:, :, 8] = g[..., :4]
    x[:, :, 9] = g[..., 4:]
    x[:, :, 10:] = rng.integers(4, 8, (N, 8, 6, C, 4)) * rng.choice([-8.0, 8.0], (N, 8, 6, C, 4)) * unit[:, None, None, None, None]
    u = d["u"].reshape(N, 128, 128, 4)
    k = k.astype(np.float32).astype(BF)
    u[:, :, ::16] = 0
    for h in range(0, 128, 16):
        u[:, h, h, 0] = k
        u[:, h + 8:h + 10, h] = k[:, None, None]
    return {"x": x.reshape(N, 128, 4 * C).astype(BF), "u": u.reshape(N, 128, 512), "v": d["v"], **quiet(rng, 1, 8)}
def patterns(rng):
    i = np.arange(K)
    return np.stack([i, i[::-1], i + 7 - 2 * (i % 8), K - 8 - i + 2 * (i % 8), i ^ 1, rng.permutation(K), (i - 1) % K, (i + K // 2) % K])
def setup_inputs(rng):
    return {**numbers_of(rng), **weights(rng, f(rng, N, 128, 2048))}
def setup_inputs_ties(rng):
    d = numbers_of(rng)
    o = rng.permutation(N)
    x = d["x"].reshape(N, 8, 16, C, 4)
    for r in range(N):
        n = 1 if o[r] == 0 else (3, 9, 24)[o[r] % 3]
        a = x[r][:, :8, :n].copy()
        if n > 1: a[:, :, 2] = 0
        x[r][:, :8] = a[:, :, rng.permutation(C) % n]
        if o[r] == 1: x[r] = 0
    u = d["u"].reshape(N, 8, 16, 8, 16, 4)
    for h in range(8):
        a = u[:, h, :8, h, 0].copy()
        u[:, :, :, h, 0] = 0
        u[:, h, :8, h, 0] = a
    return {"x": x.reshape(N, 128, 4 * C), "u": u.reshape(N, 128, 512), "v": d["v"], **quiet(rng, 8, 16)}
def setup_inputs_near(rng):
    d = numbers_of(rng)
    s = (np.argsort(rng.random((N, 8, C)), axis=2) + 1) // 2
    tiny = (np.arange(N) // 2 + int(rng.integers(2))) % 2 == 0
    m = np.repeat((signs(rng) * ~tiny[:, None])[:, :, None], C, axis=2)
    for r in range(N):
        m[r, rng.permutation(8)[:4], rng.integers(0, C, 4)] = 2.0 ** 30 * rng.choice([-1.0, 1.0], 4)
    return planted(d, rng, s, m, np.where(tiny, 2.0 ** -29, 2.0 ** -23), np.where(tiny, 2.0 ** -30, 1.0))
def setup_inputs_chains(rng):
    d = numbers_of(rng)
    s, m = np.zeros((N, 8, C), np.int64), -1.0 * rng.integers(1, 8, (N, 8, C))
    for o in range(0, N, 4):
        k, to = rng.permutation(8), patterns(rng)
        for g in range(8):
            a, b, t = rng.permutation(K), rng.permutation(K), to[k[g]]
            four = (a, a, t[a], t[a]) if (k[g] + o // 4) % 2 == 0 else (a, t[a], b, t[b])
            for i in range(4):
                e = (np.arange(K), np.arange(C - K, C), np.sort(rng.permutation(C)[:K]))[(k[g] + i) % 3]
                m[o + i, g, e] = 0
                s[o + i, g, e[four[i]]] = K - np.arange(K)
    return planted(d, rng, s, m, np.full(N, 2.0 ** -23), np.ones(N))
def setup_inputs_huge(rng):
    d = numbers_of(rng)
    x = 2.0 ** 30 * (0.6 + 0.4 * rng.random((N, 128, C, 4)))
    c = np.stack([rng.permutation(C) % 2 * 2.0 - 1.0 for r in range(N)])
    c[rng.permutation(N) < N // 2] = 1
    x *= c[:, None, :, None]
    u = d["u"].reshape(N, 128, 128, 4)
    a = 2.0 ** 30 * (1 - 0.25 * rng.random((N, 128, 8, 4))) * signs(rng)[:, None, :, None]
    u[:, :, ::16] = a.astype(np.float32).astype(BF)
    w = np.zeros((N, 128, 4, 128, 4), np.float32)
    i = np.arange(128)
    for b in range(4): w[:, i, b, i, b] = -16
    return {"x": x.astype(np.float32).reshape(N, 128, 4 * C).astype(BF), "u": u.reshape(N, 128, 512), "v": d["v"], **weights(rng, w.reshape(N, 128, 2048).astype(BF))}
def setup_inputs_spread(rng):
    d = setup_inputs(rng)
    d["x"] = clear(wide(rng, N, 128, 4 * C, cols=6))
    return d
def check_inputs(d):
    b = []
    for k in ("x", "u", "v"):
        a = np.abs(d[k].astype(np.float32))
        if not (np.isfinite(a).all() and ((a == 0) | (a >= 2.0 ** -30) & (a <= 2.0 ** 30)).all()): b.append("a value of " + k)
    return b
def reference(x, u, v, wc, ws):
    qu = [mx_ref.quantize(u[r]) for r in range(N)]
    lay = [pk(wc[r], ws[r]) for r in range(N)]
    now = [x[r] for r in range(N)]
    y, oq = np.zeros((N, 128, C), np.float32), np.zeros((N, 8, R * C), np.float32)
    oc, osc = np.zeros((N, 128, 4 * C), np.uint8), np.zeros((N, 16, C), np.uint8)
    for t in range(R):
        state = [mx_ref.quantize(now[r]) for r in range(N)]
        top = [highest(mx_ref.matmul(qu[r], state[r])) for r in range(N)]
        held = decode(join(*state)).astype(BF)
        for r in range(N):
            e = partner(r, t)
            q = warp(top[r], top[e])
            oq[r, :, C * t:C * t + C] = q
            came = gcols(cut(held, e, 4 * C), q)
            mid = ((now[r].astype(np.float32) + came.astype(np.float32)) * np.float32(0.5)).astype(BF)
            g, z = mid.astype(np.float32), mx_ref.quantize(mid)
            now[r] = tile([g[:, b::4] + np.maximum(mx_ref.matmul(pick(lay[r], np.arange(128 * b, 128 * b + 128)), z), np.float32(0.0)) * np.float32(0.015625) for b in range(4)])
    for r in range(N):
        z = mx_ref.quantize(now[r])
        y[r] = mx_ref.matmul(mx_ref.quantize(v[r]), z)
        oc[r], osc[r] = emit(z)
    return {"y": y, "oq": oq, "oc": oc, "osc": osc}

@@ -1,0 +1,420 @@
+from concourse.mybir import dt, AxisListType, AluOpType as A, ActivationFunctionType as F
+
+C, K, R = 384, 48, 2
+W = 194
+H = C // 2
+F32, BF, U16, I32, Q4, U8 = "float32", "bfloat16", "uint16", "int32", "float8_e4m3fn_x4", "uint8"
+SCRATCH = {}
+for _n, _w, _d in [
+    ("x0", 4 * C, BF), ("x1", 4 * C, BF), ("x2", 4 * C, BF), ("xh", 4 * C, BF), ("gg", 4 * C, BF), ("yh", 4 * C, BF),
+    ("rl", 4 * C, F32), ("ub", 512, BF), ("vb", 512, BF), ("eb", 516, BF), ("one", 520, BF),
+    ("t0", C, Q4), ("t1", C, Q4), ("t2", C, Q4), ("s0", C, U8), ("s1", C, U8), ("s2", C, U8),
+    ("lt0", C, Q4), ("lt1", C, Q4), ("ls0", C, U8), ("ls1", C, U8), ("zq", C, Q4), ("zs", C, U8),
+    ("uq", 128, Q4), ("us", 128, U8), ("up", 128, Q4), ("ups", 128, U8), ("vq", 128, Q4), ("vs", 128, U8),
+    ("wq", 512, Q4), ("wsp", 512, U8), ("eq", 512, Q4), ("es", 512, U8),
+    ("iot", 128, F32), ("c16", 144, F32), ("c4", C, F32), ("pi", 4, I32), ("pj", 16, I32), ("col", 32, F32), ("i16", 8, F32),
+    ("dm", 144, F32), ("sg", 144, F32), ("rs3", H, BF), ("dw", C, BF), ("clr", 96, F32),
+    ("uo", 8, U16), ("so", 6, U16), ("ipo", 4, U16),
+    ("psb", C, F32), ("m3", C, F32), ("ma", 144, F32), ("mh", 144, F32), ("junk", C, BF),
+    ("rk", 10, F32), ("rko", 10, U16), ("sel", 128, BF), ("pos", 128, BF), ("cn", C, F32), ("co", 4, U16),
+    ("cand", 144, F32), ("crow", 144, BF), ("h0", 144, BF), ("h1", 144, BF), ("lh0", K, BF), ("lh1", K, BF),
+    ("oa", 96, F32), ("oh", 96, F32), ("pn", 4, F32), ("po", 4, U16), ("krow", K, F32), ("kw", 6, U16),
+    ("arow", 96, F32), ("ao", 10, U16),
+    ("ba", K, F32), ("bh", K, F32), ("brow", 96, F32), ("sn", 4, F32), ("fo", 10, U16), ("lo", 6, U16),
+    ("fc", 64, F32), ("val", 160, BF), ("tab", 16 * W, BF), ("fout", 17 * W, BF),
+    ("lr", 96, F32), ("cr", K, F32), ("l4", K, F32), ("cl", K, F32), ("pm", 56, F32), ("on", K, F32),
+    ("bz", K, F32), ("dl", K, F32), ("nn", K, F32), ("od", K, F32), ("d1", K, F32), ("pv", 144, BF),
+    ("pw", 1200, BF), ("cap", C, BF), ("qr", C, BF), ("qh", C, BF), ("qo", 96, U16),
+    ("oq0", C, F32), ("oq1", C, F32), ("ysb", C, F32),
+]:
+    SCRATCH[_n] = ("sbuf", [128, _w], _d)
+SCRATCH["tb8"] = ("sbuf", [128, 8, 144], BF)
+SCRATCH["tb9"] = ("sbuf", [128, 9, 160], BF)
+for _i in range(8):
+    SCRATCH["ps%d" % _i] = ("psum", [128, 512], F32)
+SEMAPHORES = ["v", "a", "p", "g"] + ["d%d" % _i for _i in range(40)] + ["rt0", "rt1", "rh0", "rh1"]
+
+
+def rank_program(g, core, T, topo):
+    rank = T.rank_of(core)
+    if rank is None:
+        return
+    ops = []
+
+    def V(name, a=0, b=None, s=1):
+        b = T[name].shape[1] if b is None else b
+        if s == 1:
+            return (T[name][:, a:b], (name, a, b))
+        if s > 1:
+            return (T[name][:, a:b:s], (name, a, b, s))
+        return (T[name][:, a:(b if b >= 0 else None):s], (name, b + 1, a + 1))
+
+    def IND(win, off):
+        return (win[0].indirect(off[0]), win[1], off[1])
+
+    def regs(vs):
+        return [r for x in vs if isinstance(x, tuple) for r in x[1:]]
+
+    def ap(x):
+        return x[0] if isinstance(x, tuple) else x
+
+    def op(q, fn, writes, reads, kind="c", n=1, arrive=None):
+        ops.append({"q": q, "fn": fn, "w": regs(writes), "r": regs(reads), "kind": kind, "n": n, "arrive": arrive})
+
+    def tt(o, a, b, f):
+        op("v", lambda: g.vector.tensor_tensor(o[0], a[0], b[0], f), [o], [a, b])
+
+    def ts(o, a, s1, f0, s2=None, f1=None):
+        if f1 is None:
+            op("v", lambda: g.vector.tensor_scalar(o[0], a[0], ap(s1), None, f0), [o], [a, s1])
+        else:
+            op("v", lambda: g.vector.tensor_scalar(o[0], a[0], ap(s1), ap(s2), f0, f1), [o], [a, s1, s2])
+
+    def cp(o, a):
+        op("v", lambda: g.vector.tensor_copy(o[0], a[0]), [o], [a])
+
+    def scat(win, off, a):
+        op("v", lambda: g.vector.tensor_copy(win[0].indirect(off[0]), a[0]), [win], [a, off])
+
+    def scan(o, d0, d1, init, f0, f1):
+        op("v", lambda: g.vector.tensor_tensor_scan(o[0], d0[0], d1[0], ap(init), f0, f1), [o], [d0, d1, init])
+
+    def ms(o, c):
+        op("v", lambda: g.vector.memset(o[0], c), [o], [])
+
+    def act(o, a, f, bias=0.0, scale=1.0, acc=None):
+        if acc is None:
+            op("a", lambda: g.scalar.activation(o[0], a[0], f, bias=ap(bias), scale=scale), [o], [a, bias])
+        else:
+            op("a", lambda: g.scalar.activation(o[0], a[0], f, bias=ap(bias), scale=scale, accum_out=acc[0]), [o, acc], [a, bias])
+
+    def quant(q, s, a):
+        op("v", lambda: g.vector.quantize_mx(q[0], s[0], a[0]), [q, s], [a])
+
+    def mm(o, wq, ws, xq, xs):
+        op("p", lambda: g.tensor.matmul_mx(o[0], wq[0], ws[0], xq[0], xs[0], True, True), [o], [wq, ws, xq, xs])
+
+    def iota(o, pat, base=0, cm=0):
+        if SCRATCH[o[1][0]][2] == I32:
+            op("g", lambda: g.iota(o[0], pat, base, cm), [o], [])
+        else:
+            op("g", lambda: g.iota(o[0], pat, base, cm, allow_small_or_imprecise_dtypes=True), [o], [])
+
+    eng = {"v": g.vector, "a": g.scalar, "p": g.tensor, "g": g, "s": g.sync}
+
+    def dma(q, o, a, writes, reads):
+        op(q, lambda: eng[q].dma_start(o, a), writes, reads, kind="d", n=16)
+
+    def send(t, land, src, sem, codes=False):
+        dst = T.cores[rank ^ (1 << t)]
+        rid, pid = topo.addr(dst)[:2]
+        m = topo.mask(core, dst)
+        o, a = (land[0].bitcast(dt.uint8), src[0].bitcast(dt.uint8)) if codes else (land[0], src[0])
+        op("g", lambda s: g.remote_dma(o, a, T.sem[sem], s, pid, rid, m), [], [src], kind="r", n=len(topo.engines(core, dst)))
+
+    def arrive(t, sem, lands, calls):
+        src = T.cores[rank ^ (1 << t)]
+        op(None, None, lands, [], kind="x", n=calls * len(topo.engines(src, core)), arrive=sem)
+
+    def col(i):
+        return V("col", i, i + 1)
+
+    def wrap(h, a, row, n):
+        tt(V(a, 0, n), row, V("dm", 0, n), A.add)
+        scan(V(h, 0, n), V("sg", 0, n), V(a, 0, n), 0.0, A.add, A.max)
+
+    def count(out, row, n, bias):
+        for k in range(3):
+            act(V("junk", 128 * k, 128 * k + n), row, F.Sign, bias=bias(k), scale=-1.0, acc=V(out, k, k + 1))
+
+    def ranks(name, a, s, n):
+        row = lambda i, j: V(name, a + s * i, a + s * (j - 1) + 1, s)
+        nb, w = n // 16, n + 16
+        tb = "tb%d" % nb
+        seg = lambda k, i, j: (T[tb][:, k, i:j], (tb, w * k + i, w * k + j))
+        scan(V("mh", 0, n), V("sg", 0, n), V("ma", 0, n), 0.0, A.add, A.max)
+        for k in range(nb):
+            e, m = 16 * k + 16, V("mh", 16 * k + 15, 16 * k + 16)
+            ts(seg(k, 0, e), row(0, e), m, A.is_ge)
+            if e < n:
+                ts(seg(k, e, n), row(e, n), m, A.is_gt)
+            if k in (0, 2, 4, 6):
+                z = k + 2 if k < 6 else nb
+                tt((T[tb][:, k:z, n:w],) + tuple((tb, w * i + n, w * i + w) for i in range(k, z)), row(16 * k, 16 * z), V("mh", 16 * k, 16 * z), A.not_equal)
+            if k + 1 < nb:
+                act(seg(k, 0, w), seg(k, 0, w), F.Identity, acc=V("rk", k, k + 1))
+        last, out = seg(nb - 1, 0, w), V("rk", nb - 1, nb)
+        op("v", lambda: g.vector.tensor_reduce(out[0], last[0], AxisListType.X, A.add), [out], [last])
+        ts(V("rko", 0, nb), V("rk", 0, nb), -16.0, A.add)
+
+    def table_fill(i, j):
+        for k in range(i, j):
+            act(V("tab", 520 * k, min(520 * k + 520, 16 * W)), V("one", 0, min(520, 16 * W - 520 * k)), F.Copy, scale=0.0)
+
+    plain = (1024.0, 0.0, 4.0)
+
+    small = [
+        lambda: ts(V("col", 12, 15), V("col", 1, 4), -1.5, A.add, 1.0 / 3.0, A.mult),
+        lambda: cp(V("pj", 4, 7), V("col", 12, 15)),
+        lambda: ts(V("col", 16, 19), V("pj", 4, 7), -47.0, A.mult),
+        lambda: ts(V("col", 20, 23), V("col", 1, 4), -0.5, A.add, 16.0, A.mult),
+        lambda: tt(V("col", 24, 27), V("col", 16, 19), V("col", 20, 23), A.add),
+        lambda: cp(V("ipo", 0, 3), V("col", 24, 27)),
+        lambda: ms(V("clr", 0, 16), 1.0),
+        lambda: ms(V("clr", 16, 48), 0.0),
+        lambda: ms(V("clr", 48, 80), -1.0),
+        lambda: ms(V("clr", 80, 96), 0.0),
+        lambda: ms(V("pm", 0, 1), 0.0),
+    ]
+
+    dma("a", T.ub[:], T.u[:], [V("ub")], [])
+    dma("s", T.x0[:, 0:4 * H], T.x[:, 0:4 * H], [V("x0", 0, 4 * H)], [])
+    dma("a", T.x0[:, 4 * H:4 * C], T.x[:, 4 * H:4 * C], [V("x0", 4 * H, 4 * C)], [])
+    iota(V("pi", 0, 1), [[0, 1]], 0, 1)
+    iota(V("i16"), [[16, 8]])
+    ms(V("one"), 1.0)
+    op("g", lambda: g.affine_select(T.eb[:], T.one[:, 0:516], [[-1, 516]], A.is_equal, 0.0, 3, 4), [V("eb")], [V("one")])
+    iota(V("c16"), [[0, 9], [1, 16]])
+    iota(V("iot"), [[1, 128]])
+    iota(V("c4"), [[0, 96], [1, 4]])
+    table_fill(0, 4)
+    ms(V("rs3"), 0.0)
+    ts(V("pi", 1, 2), V("pi", 0, 1), 15, A.bitwise_and)
+    ms(V("rs3", 0, H, 3), -1e29)
+    cp(col(0), V("pi", 1, 2))
+    cp(V("uo"), V("i16"))
+    for k in range(3):
+        ms(V("pw", 400 * k, 400 * k + 400), plain[k])
+    ts(V("col", 1, 4), V("i16", 0, 3), col(0), A.add, 0.5, A.add)
+    for b in range(4):
+        quant(V("eq", 128 * b, 128 * b + 128), V("es", 128 * b, 128 * b + 128), V("eb", 3 - b, 515 - b))
+    ts(V("dm"), V("c16"), col(0), A.not_equal, -1e29, A.mult)
+    ts(V("sg"), V("c16"), 0.0, A.is_equal, -3e29, A.mult)
+    ts(V("pj", 0, 1), V("pi", 1, 2), 2, A.arith_shift_right)
+    ts(V("pj", 1, 2), V("pi", 1, 2), 3, A.bitwise_and)
+    ts(col(11), col(0), 3.0, A.mult)
+    cp(V("col", 4, 6), V("pj", 0, 2))
+    quant(V("uq"), V("us"), V("ub"))
+    op("v", lambda: g.vector.tensor_copy(T.up[:, 0:128].bitcast(dt.uint32), T.uq[:, 0:128].bitcast(dt.uint32).indirect(T.uo[:, 0:8])),
+       [V("up")], [V("uq"), V("uo")])
+    op("a", lambda: g.scalar.activation(T.ups[:, 0:128], T.us[:, 0:128].indirect(T.uo[:, 0:8]), F.Copy), [V("ups")], [V("us"), V("uo")])
+    for h in range(2):
+        quant(V("t0", H * h, H * h + H), V("s0", H * h, H * h + H), V("x0", 4 * H * h, 4 * H * h + 4 * H))
+    table_fill(4, 5)
+    dma("s", T.wq[:].bitcast(dt.uint8), T.wc[:], [V("wq")], [V("x0")])
+    dma("s", T.wsp[:], T.ws[:], [V("wsp")], [V("x0")])
+    dma("s", T.vb[:], T.v[:], [V("vb")], [V("x0")])
+
+    for t in range(R):
+        tq, sq, hb, lh, xs = "t%d" % t, "s%d" % t, "h%d" % t, "lh%d" % t, "x%d" % t
+        send(t, V("lt%d" % t), V(tq), "rt%d" % t, codes=True)
+        send(t, V("ls%d" % t), V(sq), "rt%d" % t)
+        for i in (0, 2, 1, 3) if t == 0 else range(4):
+            h = i // 2
+            mm(V("ps%d" % i, 0, H), V("up"), V("ups"), V(tq, H * h, H * h + H), V(sq, H * h, H * h + H))
+        for h in range(2):
+            scan(V("m3", H * h, H * h + H), V("rs3"), V("ps%d" % (2 * h), 0, H), 0.0, A.add, A.max)
+            tt(V("ma", 64 * h, 64 * h + 64), V("m3", H * h + 2, H * h + H, 3), V("dm", 0, 64), A.add)
+            for i in range(3):
+                act(V("psb", 128 * i + 64 * h, 128 * i + 64 * h + 64), V("ps%d" % (2 * h + 1), i, H, 3), F.Copy)
+        ranks("m3", 2, 3, 128)
+        ts(V("sel"), IND(V("iot"), V("rko", 0, 8)), float(K), A.is_lt)
+        scan(V("pos"), V("sel"), V("sel"), 0.0, A.add, A.max)
+        for k in range(2):
+            act(V("junk", 128 * k, 128 * k + 128), V("pos"), F.Sign, bias=col(1 + k), scale=-1.0, acc=V("cn", 128 * k + 127, 128 * k + 128))
+        ts(V("junk", 256, C), V("pos"), col(3), A.is_le)
+        if t == 0:
+            ts(V("so", 3, 6), V("col", 1, 4), -0.5, A.add)
+        scan(V("cn", 256, C), V("junk", 256, C), V("junk", 256, C), -128.0, A.add, A.add)
+        if t == 0:
+            ts(V("so", 0, 3), V("iot", 0, 3), col(11), A.add)
+        ts(V("co", 0, 3), V("cn", 127, C, 128), 0.5, A.mult, 64.0, A.add)
+        for i in range(3):
+            tt(V("ma", i, 144, 3), IND(V("psb", 128 * i, 128 * i + 128), V("co", 0, 3)), V("dm", i, 144, 3), A.add)
+            act(V("cand", i, 144, 3), IND(V("psb", 128 * i, 128 * i + 128), V("co", 0, 3)), F.Copy)
+        for i in range(3):
+            act(V("crow", i, 144, 3), IND(V("iot"), V("co", 0, 3)), F.Copy, bias=float(i - H), scale=3.0)
+        ranks("cand", 0, 1, 144)
+        if t == 0:
+            table_fill(5, 6)
+        scat(V(hb), V("rko", 0, 9), V("crow"))
+        send(t, V(lh), V(hb, 0, K), "rh%d" % t)
+        wrap("oh", "oa", V(hb, 0, K), K)
+        count("pn", V(hb, 0, K), K, lambda k: V("oh", 16 * k + 15, 16 * k + 16))
+        for h in range(2):
+            act(V("xh", 4 * H * h, 4 * H * h + 4 * H), V(xs, 4 * H * h, 4 * H * h + 4 * H), F.Copy, scale=0.5)
+        if t == 0:
+            ts(col(7), col(0), float(W), A.mult, 48.0, A.add)
+            ts(col(8), col(0), float(W), A.mult, 47.0, A.add)
+            ts(col(9), col(0), float(-W), A.mult, 15.0 * W + 146.0, A.add)
+            ts(col(10), col(0), float(-W), A.mult, 15.0 * W + 145.0, A.add)
+            ms(V("val", 0, 96), 1.0)
+            ms(V("val", 96, 160), -1.0)
+            ms(V("fout", 0, W), 0.0)
+            ms(V("tab", 96, 16 * W, W), -100.0)
+        else:
+            quant(V("vq"), V("vs"), V("vb"))
+        ts(V("po", 0, 3), V("pn", 0, 3), 47.0, A.add, 0.5, A.mult)
+        scat(V("krow"), V("po", 0, 3), V("iot", 0, K))
+        wrap("oh", "oa", IND(V("krow"), V("so")), 96)
+        cp(V("kw"), V("oh", 15, 96, 16))
+        cp(V("arow"), IND(V(hb, 0, K), V("kw")))
+        wrap("oh", "oa", V("arow", K, 96), K)
+        for i in range(3):
+            ts(V("ao", 3 * i, 3 * i + 3), V("oh", 15, K, 16), H + 400.0 * i, A.add)
+        arrive(t, "rh%d" % t, [V(lh)], 1)
+        act(V("brow"), IND(V(lh), V("kw")), F.Copy)
+        wrap("bh", "ba", IND(V(lh), V("kw", 0, 3)), K)
+        count("sn", V(lh), K, lambda k: V("bh", 16 * k + 15, 16 * k + 16))
+        tt(V("fc", 0, 32), V("brow", 0, 32), V("brow", 16, 48), A.is_gt)
+        tt(V("fc", 32, 48), V("brow", 0, 16), V("brow", 32, 48), A.is_gt)
+        tt(V("fc", 48, 64), V("fc", 32, 48), V("fc", 0, 16), A.subtract)
+        tt(V("val", 112, 128), V("fc", 48, 64), V("fc", 16, 32), A.subtract)
+        tt(V("val", 128, 144), V("fc", 48, 64), V("fc", 16, 32), A.subtract)
+        ts(V("fo", 0, 3), V("sn", 0, 3), col(7), A.add)
+        ts(V("fo", 3, 6), V("sn", 0, 3), -1.0, A.mult, col(9), A.add)
+        ts(V("fo", 6, 8), V("sn", 0, 2), col(8), A.add)
+        ts(V("fo", 8, 10), V("sn", 1, 3), -1.0, A.mult, col(10), A.add)
+        scat(V("tab"), V("fo"), V("val"))
+        arrive(t, "rt%d" % t, [V("lt%d" % t), V("ls%d" % t)], 2)
+        act(V("bz"), V("brow", K, 96), F.Copy, bias=2048.0, scale=4.0)
+        for b in range(4):
+            mm(V("ps%d" % b, 0, C), V("eq", 128 * b, 128 * b + 128), V("es", 128 * b, 128 * b + 128), V("lt%d" % t), V("ls%d" % t))
+            act(V("yh", b, 4 * C, 4), V("ps%d" % b, 0, C), F.Copy, scale=0.5)
+        if t == 0:
+            act(V("c4"), V("c4"), F.Abs, bias=col(4), scale=-1.0)
+            act(V("dw"), V("c4"), F.Relu, bias=4096.0, scale=-4096.0)
+        else:
+            for k in range(3):
+                act(V("pw", 400 * k, 400 * k + 400), V("one", 0, 400), F.Copy, scale=plain[k])
+        for s in range(16):
+            scan(V("fout", W * s + W, W * s + 2 * W), V("fout", W * s, W * s + W), V("tab", W * s, W * s + W), 0.0, A.max, A.add)
+            if s == 0:
+                ts(V("lo", 1, 5), V("fo", 1, 5), float(W), A.add)
+            if s == 1:
+                cp(V("lo", 0, 6, 5), V("fo", 0, 6, 5))
+            if s == 2:
+                tt(V("d1"), V("brow", K, 96), V("arow", K, 96), A.subtract)
+            if s == 3:
+                ts(V("dl"), V("d1"), -1.0 - H, A.add, 1.0 / 512.0, A.mult)
+            if t == 0 and 4 <= s < 15:
+                small[s - 4]()
+        tt(V("lr"), IND(V("fout"), V("lo")), V("clr"), A.add)
+        act(V("l4"), IND(V("lr", 0, K), V("ipo", 0, 3)), F.Copy, scale=2048.0 + 131072.0)
+        ts(V("cr"), IND(V("lr", K, 96), V("ipo", 0, 3)), V("fout", 16 * W + 95, 16 * W + 96), A.subtract, 131072.0, A.mult)
+        if t == 0:
+            ts(col(6), col(5), 4.0 * H, A.add)
+        tt(V("cl"), V("cr"), V("l4"), A.add)
+        scan(V("pm", 1, K + 1), V("cl"), V("cl"), 0.0, A.max, A.max)
+        tt(V("on"), V("pm", 1, K + 1), V("pm", 0, K), A.subtract)
+        tt(V("pv", 0, K), V("bz"), V("on"), A.subtract)
+        act(V("pv", K, 96), V("on"), F.Copy, scale=-1.0 / 512.0)
+        ts(V("pv", 96, 144), V("on"), 4.0, A.add)
+        act(V("nn"), V("on"), F.Copy, bias=1.0, scale=-1.0 / 2048.0)
+        scat(V("pw"), V("ao", 0, 9), V("pv"))
+        tt(V("od"), V("on"), V("dl"), A.mult)
+        scan(V("cap", C - 1, -1, -1), V("pw", 400 + C, 400, -1), V("pw", C - 1, -1, -1), 4.0 * (C - 1 - H), A.add, A.min)
+        scan(V("d1", K - 1, -1, -1), V("nn", K - 1, -1, -1), V("od", K - 1, -1, -1), 0.0, A.mult, A.add)
+        scan(V("qr"), V("pw", 800, 800 + C), V("cap"), V("d1", 0, 1), A.add, A.min)
+        scan(V("qh"), V("dw"), V("qr"), 0.0, A.add, A.min)
+        ts(V("qo"), V("qh", 3, C, 4), col(6), A.add, col(5), A.max)
+        act(V("oq%d" % t), V("qr"), F.Relu, bias=float(H), scale=0.25)
+        dma("s", T.oq[:, C * t:C * t + C], T["oq%d" % t][0:128:16, :], [], [V("oq%d" % t)])
+        if t + 1 < R:
+            table_fill(0, 3)
+        xn, tn, sn = "x%d" % (t + 1), "t%d" % (t + 1), "s%d" % (t + 1)
+        for h in range(2):
+            a, e = 4 * H * h, 4 * H * h + 4 * H
+            tt(V("gg", a, e), IND(V("yh"), V("qo", K * h, K * h + K)), V("xh", a, e), A.add)
+            quant(V("zq", H * h, H * h + H), V("zs", H * h, H * h + H), V("gg", a, e))
+            for b in range(4):
+                ps = V("ps%d" % (4 * h + b), 0, H)
+                mm(ps, V("wq", 128 * b, 128 * b + 128), V("wsp", 128 * b, 128 * b + 128), V("zq", H * h, H * h + H), V("zs", H * h, H * h + H))
+                act(V("rl", a + b, e, 4), ps, F.Relu, scale=0.015625)
+        if t + 1 < R:
+            table_fill(3, 6)
+            act(V("tab", 96, 16 * W, W), V("one", 0, 16), F.Copy, scale=-100.0)
+            for c0, c1 in ((0, H), (H, C)):
+                tt(V(xn, 4 * c0, 4 * c1), V("gg", 4 * c0, 4 * c1), V("rl", 4 * c0, 4 * c1), A.add)
+                quant(V(tn, c0, c1), V(sn, c0, c1), V(xn, 4 * c0, 4 * c1))
+            continue
+        tt(V(xn, 0, 4 * H), V("gg", 0, 4 * H), V("rl", 0, 4 * H), A.add)
+        for h, (a, c0, c1) in enumerate(((H, 0, 256), (256, 256, C))):
+            tt(V(xn, 4 * a, 4 * c1), V("gg", 4 * a, 4 * c1), V("rl", 4 * a, 4 * c1), A.add)
+            quant(V(tn, c0, c1), V(sn, c0, c1), V(xn, 4 * c0, 4 * c1))
+            mm(V("ps%d" % h, 0, c1 - c0), V("vq"), V("vs"), V(tn, c0, c1), V(sn, c0, c1))
+            dma("s", T.oc[:, 4 * c0:4 * c1], T[tn][:, c0:c1].bitcast(dt.uint8), [], [V(tn, c0, c1)])
+            if h == 0:
+                act(V("ysb", c0, c1), V("ps0", 0, c1 - c0), F.Copy)
+            else:
+                for k in range(4):
+                    dma("a" if k % 2 else "s", T.osc[4 * k:4 * k + 4, :], T[sn][32 * k:32 * k + 4, :], [], [V(sn)])
+                cp(V("ysb", c0, c1), V("ps1", 0, c1 - c0))
+            dma("a", T.y[:, c0:c1], T.ysb[:, c0:c1], [], [V("ysb", c0, c1)])
+
+    emit(ops, eng, T)
+
+
+def emit(ops, eng, T):
+    def bank(x):
+        return x[0].startswith("ps") and x[0][2:].isdigit()
+
+    def apart(x, y):
+        return len(x) > 3 and len(y) > 3 and x[3] == y[3] and (x[1] - y[1]) % x[3] != 0
+
+    def hit(x, y):
+        return x[0] == y[0] and (bank(x) or (x[1] < y[2] and y[1] < x[2] and not apart(x, y)))
+
+    deps = []
+    for i, o in enumerate(ops):
+        d = set()
+        for j in range(i):
+            p = ops[j]
+            if any(hit(x, y) for x in o["r"] for y in p["w"]) or any(hit(x, y) for x in o["w"] for y in p["w"] + p["r"]):
+                d.add(j)
+            elif p["q"] != o["q"] and any(bank(x) and hit(x, y) for x in o["r"] for y in p["r"]):
+                d.add(j)
+        deps.append(d)
+    known, done_at, waits = {q: set() for q in eng}, [], []
+    for i, o in enumerate(ops):
+        q = o["q"]
+        if q is None:
+            done_at.append({i})
+            waits.append([])
+            continue
+        need = []
+        for j in sorted(deps[i], reverse=True):
+            if j not in known[q]:
+                need.append(j)
+                known[q] |= done_at[j]
+        waits.append(need)
+        mine = set(known[q]) | {i}
+        if o["kind"] == "c":
+            mine |= {j for j in range(i) if ops[j]["q"] == q and ops[j]["kind"] == "c"}
+        done_at.append(mine)
+    target = {j for w in waits for j in w}
+    count, token, nd = {q: 0 for q in eng}, {}, 0
+    for i, o in enumerate(ops):
+        q = o["q"]
+        if q is None:
+            token[i] = (T.sem[o["arrive"]], o["n"])
+            continue
+        for j in waits[i]:
+            eng[q].wait_ge(*token[j])
+        if o["kind"] == "c":
+            ins = o["fn"]()
+            if i in target:
+                count[q] += 1
+                ins.then_inc(T.sem[q], 1)
+                token[i] = (T.sem[q], count[q])
+        else:
+            s = T.sem["d%d" % nd]
+            nd += 1
+            token[i] = (s, o["n"])
+            if o["kind"] == "d":
+                o["fn"]().then_inc(s, 16)
+            else:
+                o["fn"](s)
+    for i, o in enumerate(ops):
+        if o["kind"] in "dr" and i not in target:
+            eng["g" if o["kind"] == "r" else o["q"]].wait_ge(*token[i])

@@ -1,7 +1,7 @@
 from concourse.mybir import dt, AxisListType, AluOpType as A, ActivationFunctionType as F
 
 C, K, R = 384, 48, 2
-W = 194
+W = 192
 H = C // 2
 F32, BF, U16, I32, Q4, U8 = "float32", "bfloat16", "uint16", "int32", "float8_e4m3fn_x4", "uint8"
 SCRATCH = {}
@@ -13,16 +13,16 @@ for _n, _w, _d in [
     ("uq", 128, Q4), ("us", 128, U8), ("up", 128, Q4), ("ups", 128, U8), ("vq", 128, Q4), ("vs", 128, U8),
     ("wq", 512, Q4), ("wsp", 512, U8), ("eq", 512, Q4), ("es", 512, U8),
     ("iot", 128, F32), ("c16", 144, F32), ("c4", C, F32), ("pi", 4, I32), ("pj", 16, I32), ("col", 32, F32), ("i16", 8, F32),
-    ("dm", 144, F32), ("sg", 144, F32), ("rs3", H, BF), ("dw", C, BF), ("clr", 96, F32),
-    ("uo", 8, U16), ("so", 6, U16), ("ipo", 4, U16),
+    ("dm", 144, F32), ("sg", 144, F32), ("rs3", H, BF), ("dw", C, BF),
+    ("uo", 8, U16), ("so", 6, U16),
     ("psb", C, F32), ("m3", C, F32), ("ma", 144, F32), ("mh", 144, F32), ("junk", C, BF),
     ("rk", 10, F32), ("rko", 10, U16), ("sel", 128, BF), ("pos", 128, BF), ("cn", C, F32), ("co", 4, U16),
     ("cand", 144, F32), ("crow", 144, BF), ("h0", 144, BF), ("h1", 144, BF), ("lh0", K, BF), ("lh1", K, BF),
     ("oa", 96, F32), ("oh", 96, F32), ("pn", 4, F32), ("po", 4, U16), ("krow", K, F32), ("kw", 6, U16),
     ("arow", 96, F32), ("ao", 10, U16),
-    ("ba", K, F32), ("bh", K, F32), ("brow", 96, F32), ("sn", 4, F32), ("fo", 10, U16), ("lo", 6, U16),
+    ("ba", K, F32), ("bh", K, F32), ("brow", 96, F32), ("sn", 4, F32), ("fo", 10, U16), ("lo", 12, U16),
     ("fc", 64, F32), ("val", 160, BF), ("tab", 16 * W, BF), ("fout", 17 * W, BF),
-    ("lr", 96, F32), ("cr", K, F32), ("l4", K, F32), ("cl", K, F32), ("pm", 56, F32), ("on", K, F32),
+    ("cr", K, F32), ("l4", K, F32), ("cl", K, F32), ("pm", 56, F32), ("on", K, F32),
     ("bz", K, F32), ("dl", K, F32), ("nn", K, F32), ("od", K, F32), ("d1", K, F32), ("pv", 144, BF),
     ("pw", 1200, BF), ("cap", C, BF), ("qr", C, BF), ("qh", C, BF), ("qo", 96, U16),
     ("oq0", C, F32), ("oq1", C, F32), ("ysb", C, F32),
@@ -119,9 +119,12 @@ def rank_program(g, core, T, topo):
     def col(i):
         return V("col", i, i + 1)
 
+    def hold(h, a, i, j):
+        scan(V(h, i, j), V("sg", 0, j - i), V(a, i, j), 0.0, A.add, A.max)
+
     def wrap(h, a, row, n):
         tt(V(a, 0, n), row, V("dm", 0, n), A.add)
-        scan(V(h, 0, n), V("sg", 0, n), V(a, 0, n), 0.0, A.add, A.max)
+        hold(h, a, 0, n)
 
     def count(out, row, n, bias):
         for k in range(3):
@@ -132,7 +135,6 @@ def rank_program(g, core, T, topo):
         nb, w = n // 16, n + 16
         tb = "tb%d" % nb
         seg = lambda k, i, j: (T[tb][:, k, i:j], (tb, w * k + i, w * k + j))
-        scan(V("mh", 0, n), V("sg", 0, n), V("ma", 0, n), 0.0, A.add, A.max)
         for k in range(nb):
             e, m = 16 * k + 16, V("mh", 16 * k + 15, 16 * k + 16)
             ts(seg(k, 0, e), row(0, e), m, A.is_ge)
@@ -149,23 +151,24 @@ def rank_program(g, core, T, topo):
 
     def table_fill(i, j):
         for k in range(i, j):
-            act(V("tab", 520 * k, min(520 * k + 520, 16 * W)), V("one", 0, min(520, 16 * W - 520 * k)), F.Copy, scale=0.0)
+            act(V("tab", 512 * k, 512 * k + 512), V("one", 0, 512), F.Copy, scale=0.0)
+
+    def scores(t, i):
+        h = i // 2
+        mm(V("ps%d" % i, 0, H), V("up"), V("ups"), V("t%d" % t, H * h, H * h + H), V("s%d" % t, H * h, H * h + H))
+
+    def top(h):
+        scan(V("m3", H * h, H * h + H), V("rs3"), V("ps%d" % (2 * h), 0, H), 0.0, A.add, A.max)
+        for i in range(3):
+            act(V("psb", 128 * i + 64 * h, 128 * i + 64 * h + 64), V("ps%d" % (2 * h + 1), i, H, 3), F.Copy)
+
+    def mask(h):
+        tt(V("ma", 64 * h, 64 * h + 64), V("m3", H * h + 2, H * h + H, 3), V("dm", 0, 64), A.add)
+
+    def layer_sum(xn, a, e):
+        tt(V(xn, 4 * a, 4 * e), V("gg", 4 * a, 4 * e), V("rl", 4 * a, 4 * e), A.add)
 
     plain = (1024.0, 0.0, 4.0)
-
-    small = [
-        lambda: ts(V("col", 12, 15), V("col", 1, 4), -1.5, A.add, 1.0 / 3.0, A.mult),
-        lambda: cp(V("pj", 4, 7), V("col", 12, 15)),
-        lambda: ts(V("col", 16, 19), V("pj", 4, 7), -47.0, A.mult),
-        lambda: ts(V("col", 20, 23), V("col", 1, 4), -0.5, A.add, 16.0, A.mult),
-        lambda: tt(V("col", 24, 27), V("col", 16, 19), V("col", 20, 23), A.add),
-        lambda: cp(V("ipo", 0, 3), V("col", 24, 27)),
-        lambda: ms(V("clr", 0, 16), 1.0),
-        lambda: ms(V("clr", 16, 48), 0.0),
-        lambda: ms(V("clr", 48, 80), -1.0),
-        lambda: ms(V("clr", 80, 96), 0.0),
-        lambda: ms(V("pm", 0, 1), 0.0),
-    ]
 
     dma("a", T.ub[:], T.u[:], [V("ub")], [])
     dma("s", T.x0[:, 0:4 * H], T.x[:, 0:4 * H], [V("x0", 0, 4 * H)], [])
@@ -186,37 +189,46 @@ def rank_program(g, core, T, topo):
     for k in range(3):
         ms(V("pw", 400 * k, 400 * k + 400), plain[k])
     ts(V("col", 1, 4), V("i16", 0, 3), col(0), A.add, 0.5, A.add)
-    for b in range(4):
-        quant(V("eq", 128 * b, 128 * b + 128), V("es", 128 * b, 128 * b + 128), V("eb", 3 - b, 515 - b))
-    ts(V("dm"), V("c16"), col(0), A.not_equal, -1e29, A.mult)
-    ts(V("sg"), V("c16"), 0.0, A.is_equal, -3e29, A.mult)
     ts(V("pj", 0, 1), V("pi", 1, 2), 2, A.arith_shift_right)
     ts(V("pj", 1, 2), V("pi", 1, 2), 3, A.bitwise_and)
     ts(col(11), col(0), 3.0, A.mult)
+    for b in range(4):
+        quant(V("eq", 128 * b, 128 * b + 128), V("es", 128 * b, 128 * b + 128), V("eb", 3 - b, 515 - b))
     cp(V("col", 4, 6), V("pj", 0, 2))
+    ts(V("dm"), V("c16"), col(0), A.not_equal, -1e29, A.mult)
+    ts(V("sg"), V("c16"), 0.0, A.is_equal, -3e29, A.mult)
     quant(V("uq"), V("us"), V("ub"))
+    ts(col(6), col(5), 4.0 * H, A.add)
     op("v", lambda: g.vector.tensor_copy(T.up[:, 0:128].bitcast(dt.uint32), T.uq[:, 0:128].bitcast(dt.uint32).indirect(T.uo[:, 0:8])),
        [V("up")], [V("uq"), V("uo")])
     op("a", lambda: g.scalar.activation(T.ups[:, 0:128], T.us[:, 0:128].indirect(T.uo[:, 0:8]), F.Copy), [V("ups")], [V("us"), V("uo")])
     for h in range(2):
         quant(V("t0", H * h, H * h + H), V("s0", H * h, H * h + H), V("x0", 4 * H * h, 4 * H * h + 4 * H))
     table_fill(4, 5)
-    dma("s", T.wq[:].bitcast(dt.uint8), T.wc[:], [V("wq")], [V("x0")])
-    dma("s", T.wsp[:], T.ws[:], [V("wsp")], [V("x0")])
-    dma("s", T.vb[:], T.v[:], [V("vb")], [V("x0")])
 
     for t in range(R):
-        tq, sq, hb, lh, xs = "t%d" % t, "s%d" % t, "h%d" % t, "lh%d" % t, "x%d" % t
-        send(t, V("lt%d" % t), V(tq), "rt%d" % t, codes=True)
-        send(t, V("ls%d" % t), V(sq), "rt%d" % t)
-        for i in (0, 2, 1, 3) if t == 0 else range(4):
-            h = i // 2
-            mm(V("ps%d" % i, 0, H), V("up"), V("ups"), V(tq, H * h, H * h + H), V(sq, H * h, H * h + H))
-        for h in range(2):
-            scan(V("m3", H * h, H * h + H), V("rs3"), V("ps%d" % (2 * h), 0, H), 0.0, A.add, A.max)
-            tt(V("ma", 64 * h, 64 * h + 64), V("m3", H * h + 2, H * h + H, 3), V("dm", 0, 64), A.add)
-            for i in range(3):
-                act(V("psb", 128 * i + 64 * h, 128 * i + 64 * h + 64), V("ps%d" % (2 * h + 1), i, H, 3), F.Copy)
+        tq, sq, hb, lh, xs, lt = "t%d" % t, "s%d" % t, "h%d" % t, "lh%d" % t, "x%d" % t, "lt%d" % t
+        send(t, V(lt, 0, H), V(tq, 0, H), "rt%d" % t, codes=True)
+        if t == 0:
+            send(t, V("ls%d" % t), V(sq), "rt%d" % t)
+            for i in (0, 2, 1, 3):
+                scores(t, i)
+            top(0)
+            top(1)
+            mask(0)
+        else:
+            scores(t, 0)
+            scores(t, 1)
+            top(0)
+            quant(V(tq, H, C), V(sq, H, C), V(xs, 4 * H, 4 * C))
+            send(t, V("ls%d" % t), V(sq), "rt%d" % t)
+            scores(t, 2)
+            scores(t, 3)
+            mask(0)
+            top(1)
+        hold("mh", "ma", 0, 64)
+        mask(1)
+        hold("mh", "ma", 64, 128)
         ranks("m3", 2, 3, 128)
         ts(V("sel"), IND(V("iot"), V("rko", 0, 8)), float(K), A.is_lt)
         scan(V("pos"), V("sel"), V("sel"), 0.0, A.add, A.max)
@@ -234,11 +246,14 @@ def rank_program(g, core, T, topo):
             act(V("cand", i, 144, 3), IND(V("psb", 128 * i, 128 * i + 128), V("co", 0, 3)), F.Copy)
         for i in range(3):
             act(V("crow", i, 144, 3), IND(V("iot"), V("co", 0, 3)), F.Copy, bias=float(i - H), scale=3.0)
+        hold("mh", "ma", 0, 64)
+        hold("mh", "ma", 64, 144)
         ranks("cand", 0, 1, 144)
         if t == 0:
             table_fill(5, 6)
         scat(V(hb), V("rko", 0, 9), V("crow"))
         send(t, V(lh), V(hb, 0, K), "rh%d" % t)
+        send(t, V(lt, H, C), V(tq, H, C), "rt%d" % t, codes=True)
         wrap("oh", "oa", V(hb, 0, K), K)
         count("pn", V(hb, 0, K), K, lambda k: V("oh", 16 * k + 15, 16 * k + 16))
         for h in range(2):
@@ -246,23 +261,22 @@ def rank_program(g, core, T, topo):
         if t == 0:
             ts(col(7), col(0), float(W), A.mult, 48.0, A.add)
             ts(col(8), col(0), float(W), A.mult, 47.0, A.add)
-            ts(col(9), col(0), float(-W), A.mult, 15.0 * W + 146.0, A.add)
-            ts(col(10), col(0), float(-W), A.mult, 15.0 * W + 145.0, A.add)
+            ts(col(9), col(0), float(-W), A.mult, 15.0 * W + 144.0, A.add)
+            ts(col(10), col(0), float(-W), A.mult, 15.0 * W + 143.0, A.add)
             ms(V("val", 0, 96), 1.0)
             ms(V("val", 96, 160), -1.0)
             ms(V("fout", 0, W), 0.0)
-            ms(V("tab", 96, 16 * W, W), -100.0)
         else:
             quant(V("vq"), V("vs"), V("vb"))
         ts(V("po", 0, 3), V("pn", 0, 3), 47.0, A.add, 0.5, A.mult)
         scat(V("krow"), V("po", 0, 3), V("iot", 0, K))
         wrap("oh", "oa", IND(V("krow"), V("so")), 96)
         cp(V("kw"), V("oh", 15, 96, 16))
-        cp(V("arow"), IND(V(hb, 0, K), V("kw")))
-        wrap("oh", "oa", V("arow", K, 96), K)
-        for i in range(3):
-            ts(V("ao", 3 * i, 3 * i + 3), V("oh", 15, K, 16), H + 400.0 * i, A.add)
         arrive(t, "rh%d" % t, [V(lh)], 1)
+        if t == 0:
+            dma("s", T.wq[:].bitcast(dt.uint8), T.wc[:], [V("wq")], [V(lh)])
+            dma("s", T.wsp[:], T.ws[:], [V("wsp")], [V(lh)])
+            dma("s", T.vb[:], T.v[:], [V("vb")], [V(lh)])
         act(V("brow"), IND(V(lh), V("kw")), F.Copy)
         wrap("bh", "ba", IND(V(lh), V("kw", 0, 3)), K)
         count("sn", V(lh), K, lambda k: V("bh", 16 * k + 15, 16 * k + 16))
@@ -276,45 +290,51 @@ def rank_program(g, core, T, topo):
         ts(V("fo", 6, 8), V("sn", 0, 2), col(8), A.add)
         ts(V("fo", 8, 10), V("sn", 1, 3), -1.0, A.mult, col(10), A.add)
         scat(V("tab"), V("fo"), V("val"))
-        arrive(t, "rt%d" % t, [V("lt%d" % t), V("ls%d" % t)], 2)
+        arrive(t, "rt%d" % t, [V(lt), V("ls%d" % t)], 3)
         act(V("bz"), V("brow", K, 96), F.Copy, bias=2048.0, scale=4.0)
-        for b in range(4):
-            mm(V("ps%d" % b, 0, C), V("eq", 128 * b, 128 * b + 128), V("es", 128 * b, 128 * b + 128), V("lt%d" % t), V("ls%d" % t))
-            act(V("yh", b, 4 * C, 4), V("ps%d" % b, 0, C), F.Copy, scale=0.5)
         if t == 0:
             act(V("c4"), V("c4"), F.Abs, bias=col(4), scale=-1.0)
             act(V("dw"), V("c4"), F.Relu, bias=4096.0, scale=-4096.0)
         else:
             for k in range(3):
                 act(V("pw", 400 * k, 400 * k + 400), V("one", 0, 400), F.Copy, scale=plain[k])
+        for b in range(4):
+            mm(V("ps%d" % b, 0, C), V("eq", 128 * b, 128 * b + 128), V("es", 128 * b, 128 * b + 128), V(lt), V("ls%d" % t))
+            act(V("yh", b, 4 * C, 4), V("ps%d" % b, 0, C), F.Copy, scale=0.5)
+        between = [
+            lambda: cp(V("arow"), IND(V(hb, 0, K), V("kw"))),
+            lambda: tt(V("oa", 0, K), V("arow", K, 96), V("dm", 0, K), A.add),
+            lambda: hold("oh", "oa", 0, K),
+            lambda: ts(V("ao", 0, 3), V("oh", 15, K, 16), float(H), A.add),
+            lambda: ts(V("ao", 3, 6), V("oh", 15, K, 16), H + 400.0, A.add),
+            lambda: ts(V("ao", 6, 9), V("oh", 15, K, 16), H + 800.0, A.add),
+            lambda: ts(V("lo", 2, 10, 2), V("fo", 1, 5), float(W), A.add),
+            lambda: cp(V("lo", 0, 11, 10), V("fo", 0, 6, 5)),
+            lambda: tt(V("d1"), V("brow", K, 96), V("arow", K, 96), A.subtract),
+            lambda: ts(V("dl"), V("d1"), -1.0 - H, A.add, 1.0 / 512.0, A.mult),
+        ]
         for s in range(16):
-            scan(V("fout", W * s + W, W * s + 2 * W), V("fout", W * s, W * s + W), V("tab", W * s, W * s + W), 0.0, A.max, A.add)
-            if s == 0:
-                ts(V("lo", 1, 5), V("fo", 1, 5), float(W), A.add)
-            if s == 1:
-                cp(V("lo", 0, 6, 5), V("fo", 0, 6, 5))
-            if s == 2:
-                tt(V("d1"), V("brow", K, 96), V("arow", K, 96), A.subtract)
-            if s == 3:
-                ts(V("dl"), V("d1"), -1.0 - H, A.add, 1.0 / 512.0, A.mult)
-            if t == 0 and 4 <= s < 15:
-                small[s - 4]()
-        tt(V("lr"), IND(V("fout"), V("lo")), V("clr"), A.add)
-        act(V("l4"), IND(V("lr", 0, K), V("ipo", 0, 3)), F.Copy, scale=2048.0 + 131072.0)
-        ts(V("cr"), IND(V("lr", K, 96), V("ipo", 0, 3)), V("fout", 16 * W + 95, 16 * W + 96), A.subtract, 131072.0, A.mult)
-        if t == 0:
-            ts(col(6), col(5), 4.0 * H, A.add)
+            for a in (W * s, W * s + 2 * K):
+                scan(V("fout", a + W, a + W + 2 * K), V("fout", a, a + 2 * K), V("tab", a, a + 2 * K), 0.0, A.max, A.add)
+            if s < len(between):
+                between[s]()
+        big = 131072.0
+        ts(V("pm", 0, 1), V("fout", 16 * W + 95, 16 * W + 96), big, A.mult)
+        for k in range(3):
+            act(V("l4", k, K, 3), IND(V("fout"), V("lo", 2 * k, 2 * k + 1)), F.Copy, scale=2048.0 + big,
+                bias=(2048.0 + big if k == 0 else 0.0) - (big if k != 2 else 0.0))
+            ts(V("cr", k, K, 3), IND(V("fout"), V("lo", 6 + 2 * k, 7 + 2 * k)), big, A.mult)
         tt(V("cl"), V("cr"), V("l4"), A.add)
-        scan(V("pm", 1, K + 1), V("cl"), V("cl"), 0.0, A.max, A.max)
+        scan(V("pm", 1, K + 1), V("cl"), V("cl"), V("pm", 0, 1), A.max, A.max)
         tt(V("on"), V("pm", 1, K + 1), V("pm", 0, K), A.subtract)
         tt(V("pv", 0, K), V("bz"), V("on"), A.subtract)
         act(V("pv", K, 96), V("on"), F.Copy, scale=-1.0 / 512.0)
         ts(V("pv", 96, 144), V("on"), 4.0, A.add)
         act(V("nn"), V("on"), F.Copy, bias=1.0, scale=-1.0 / 2048.0)
-        scat(V("pw"), V("ao", 0, 9), V("pv"))
         tt(V("od"), V("on"), V("dl"), A.mult)
-        scan(V("cap", C - 1, -1, -1), V("pw", 400 + C, 400, -1), V("pw", C - 1, -1, -1), 4.0 * (C - 1 - H), A.add, A.min)
+        scat(V("pw"), V("ao", 0, 9), V("pv"))
         scan(V("d1", K - 1, -1, -1), V("nn", K - 1, -1, -1), V("od", K - 1, -1, -1), 0.0, A.mult, A.add)
+        scan(V("cap", C - 1, -1, -1), V("pw", 400 + C, 400, -1), V("pw", C - 1, -1, -1), 4.0 * (C - 1 - H), A.add, A.min)
         scan(V("qr"), V("pw", 800, 800 + C), V("cap"), V("d1", 0, 1), A.add, A.min)
         scan(V("qh"), V("dw"), V("qr"), 0.0, A.add, A.min)
         ts(V("qo"), V("qh", 3, C, 4), col(6), A.add, col(5), A.max)
@@ -331,16 +351,16 @@ def rank_program(g, core, T, topo):
                 ps = V("ps%d" % (4 * h + b), 0, H)
                 mm(ps, V("wq", 128 * b, 128 * b + 128), V("wsp", 128 * b, 128 * b + 128), V("zq", H * h, H * h + H), V("zs", H * h, H * h + H))
                 act(V("rl", a + b, e, 4), ps, F.Relu, scale=0.015625)
+        layer_sum(xn, 0, H)
         if t + 1 < R:
             table_fill(3, 6)
-            act(V("tab", 96, 16 * W, W), V("one", 0, 16), F.Copy, scale=-100.0)
-            for c0, c1 in ((0, H), (H, C)):
-                tt(V(xn, 4 * c0, 4 * c1), V("gg", 4 * c0, 4 * c1), V("rl", 4 * c0, 4 * c1), A.add)
-                quant(V(tn, c0, c1), V(sn, c0, c1), V(xn, 4 * c0, 4 * c1))
+            layer_sum(xn, H, 224)
+            quant(V(tn, 0, H), V(sn, 0, H), V(xn, 0, 4 * H))
+            layer_sum(xn, 224, C)
             continue
-        tt(V(xn, 0, 4 * H), V("gg", 0, 4 * H), V("rl", 0, 4 * H), A.add)
-        for h, (a, c0, c1) in enumerate(((H, 0, 256), (256, 256, C))):
-            tt(V(xn, 4 * a, 4 * c1), V("gg", 4 * a, 4 * c1), V("rl", 4 * a, 4 * c1), A.add)
+        layer_sum(xn, H, 256)
+        for h, (a, e, c0, c1) in enumerate(((256, 280, 0, 256), (280, C, 256, C))):
+            layer_sum(xn, a, e)
             quant(V(tn, c0, c1), V(sn, c0, c1), V(xn, 4 * c0, 4 * c1))
             mm(V("ps%d" % h, 0, c1 - c0), V("vq"), V("vs"), V(tn, c0, c1), V(sn, c0, c1))
             dma("s", T.oc[:, 4 * c0:4 * c1], T[tn][:, c0:c1].bitcast(dt.uint8), [], [V(tn, c0, c1)])

@@ -1,8 +1,10 @@
 from concourse.mybir import dt, AxisListType, AluOpType as A, ActivationFunctionType as F
 
 C, K, R = 384, 48, 2
-W = 192
+W = 2 * K
 H = C // 2
+NC = 3 * K
+BIG = 131072.0
 F32, BF, U16, I32, Q4, U8 = "float32", "bfloat16", "uint16", "int32", "float8_e4m3fn_x4", "uint8"
 SCRATCH = {}
 for _n, _w, _d in [
@@ -12,19 +14,20 @@ for _n, _w, _d in [
     ("lt0", C, Q4), ("lt1", C, Q4), ("ls0", C, U8), ("ls1", C, U8), ("zq", C, Q4), ("zs", C, U8),
     ("uq", 128, Q4), ("us", 128, U8), ("up", 128, Q4), ("ups", 128, U8), ("vq", 128, Q4), ("vs", 128, U8),
     ("wq", 512, Q4), ("wsp", 512, U8), ("eq", 512, Q4), ("es", 512, U8),
-    ("iot", 128, F32), ("c16", 144, F32), ("c4", C, F32), ("pi", 4, I32), ("pj", 16, I32), ("col", 32, F32), ("i16", 8, F32),
-    ("dm", 144, F32), ("sg", 144, F32), ("rs3", H, BF), ("dw", C, BF),
-    ("uo", 8, U16), ("so", 6, U16),
-    ("psb", C, F32), ("m3", C, F32), ("ma", 144, F32), ("mh", 144, F32), ("junk", C, BF),
-    ("rk", 10, F32), ("rko", 10, U16), ("sel", 128, BF), ("pos", 128, BF), ("cn", C, F32), ("co", 4, U16),
-    ("cand", 144, F32), ("crow", 144, BF), ("h0", 144, BF), ("h1", 144, BF), ("lh0", K, BF), ("lh1", K, BF),
-    ("oa", 96, F32), ("oh", 96, F32), ("pn", 4, F32), ("po", 4, U16), ("krow", K, F32), ("kw", 6, U16),
-    ("arow", 96, F32), ("ao", 10, U16),
-    ("ba", K, F32), ("bh", K, F32), ("brow", 96, F32), ("sn", 4, F32), ("fo", 10, U16), ("lo", 12, U16),
-    ("fc", 64, F32), ("val", 160, BF), ("tab", 16 * W, BF), ("fout", 17 * W, BF),
-    ("cr", K, F32), ("l4", K, F32), ("cl", K, F32), ("pm", 56, F32), ("on", K, F32),
-    ("bz", K, F32), ("dl", K, F32), ("nn", K, F32), ("od", K, F32), ("d1", K, F32), ("pv", 144, BF),
-    ("pw", 1200, BF), ("cap", C, BF), ("qr", C, BF), ("qh", C, BF), ("qo", 96, U16),
+    ("iot", NC, F32), ("c16", NC, F32), ("c4", C, BF), ("pi", 4, I32), ("pj", 16, I32), ("col", 32, F32), ("i16", 8, F32),
+    ("dm", NC, F32), ("sg", NC, F32), ("rs3", H, BF), ("dw", C, BF), ("flg", NC, BF), ("uo", 8, U16),
+    ("psb", C, F32), ("m3", C, F32), ("ma", NC, F32), ("mh", NC, F32), ("junk", 3 * NC, BF),
+    ("rk", 10, F32), ("rko", 10, U16), ("sel", NC, BF), ("pos", NC, BF), ("cn", 3 * NC, F32), ("co", 4, U16),
+    ("cand", NC, F32), ("crow", NC, BF), ("h0", NC, BF), ("h1", NC, BF), ("lh0", K, BF), ("lh1", K, BF),
+    ("rr", NC, BF), ("eo", 4, U16), ("en", 4, U16), ("cm", 4, F32),
+    ("oa", K, F32), ("oh", K, F32), ("kw", 4, U16), ("a4", K, F32), ("ao", 10, U16),
+    ("ba", K, F32), ("bh", K, F32), ("brow", K, F32), ("sn", 4, F32), ("fo", 12, U16), ("lo", 8, U16),
+    ("fc", 64, BF), ("fs", 64, BF), ("val", 4 * NC, BF),
+    ("tf0", 16 * W, BF), ("tf1", 16 * W, BF), ("tm0", 16 * W, BF), ("tm1", 16 * W, BF), ("ff", 17 * W, BF), ("fm", 17 * W, BF),
+    ("l4", K, F32), ("cl", K, F32), ("pm", 56, F32), ("on", K, F32),
+    ("bz", K, F32), ("dl", K, F32), ("nn", K, F32), ("od", K, F32), ("d1", K, F32), ("pv", NC, BF),
+    ("pa0", 800, BF), ("pa1", 800, BF), ("pb0", 400, BF), ("pb1", 400, BF),
+    ("cap", C, BF), ("qr", C, BF), ("qh", C, BF), ("qo", 96, U16),
     ("oq0", C, F32), ("oq1", C, F32), ("ysb", C, F32),
 ]:
     SCRATCH[_n] = ("sbuf", [128, _w], _d)
@@ -100,6 +103,9 @@ def rank_program(g, core, T, topo):
         else:
             op("g", lambda: g.iota(o[0], pat, base, cm, allow_small_or_imprecise_dtypes=True), [o], [])
 
+    def gfill(name, a, b, c):
+        iota(V(name, a, b), [[0, b - a]], int(c))
+
     eng = {"v": g.vector, "a": g.scalar, "p": g.tensor, "g": g, "s": g.sync}
 
     def dma(q, o, a, writes, reads):
@@ -119,43 +125,66 @@ def rank_program(g, core, T, topo):
     def col(i):
         return V("col", i, i + 1)
 
+    spare = []
+
+    def slot(n=1):
+        for _ in range(n):
+            if spare:
+                spare.pop(0)()
+
     def hold(h, a, i, j):
         scan(V(h, i, j), V("sg", 0, j - i), V(a, i, j), 0.0, A.add, A.max)
 
-    def wrap(h, a, row, n):
-        tt(V(a, 0, n), row, V("dm", 0, n), A.add)
-        hold(h, a, 0, n)
+    def count(out, row, n, bias, ks):
+        for k in ks:
+            act(V("junk", NC * k, NC * k + n), row, F.Sign, bias=bias(k), scale=-1.0, acc=out(k))
 
-    def count(out, row, n, bias):
-        for k in range(3):
-            act(V("junk", 128 * k, 128 * k + n), row, F.Sign, bias=bias(k), scale=-1.0, acc=V(out, k, k + 1))
+    def invert(out, n, c0):
+        count(lambda k: V("cn", NC * k + n - 1, NC * k + n), V("pos", 0, n), n, lambda k: col(c0 + k), (0, 1))
+        j = V("junk", 2 * NC, 2 * NC + n)
+        ts(j, V("pos", 0, n), col(c0 + 2), A.is_le)
+        slot()
+        scan(V("cn", 2 * NC, 2 * NC + n), j, j, float(-n), A.add, A.add)
+        slot()
+        ts(out, V("cn", n - 1, 3 * NC, NC), 0.5, A.mult, n / 2.0, A.add)
 
-    def ranks(name, a, s, n):
+    def ranker(name, a, s, n):
         row = lambda i, j: V(name, a + s * i, a + s * (j - 1) + 1, s)
         nb, w = n // 16, n + 16
         tb = "tb%d" % nb
         seg = lambda k, i, j: (T[tb][:, k, i:j], (tb, w * k + i, w * k + j))
-        for k in range(nb):
-            e, m = 16 * k + 16, V("mh", 16 * k + 15, 16 * k + 16)
-            ts(seg(k, 0, e), row(0, e), m, A.is_ge)
-            if e < n:
-                ts(seg(k, e, n), row(e, n), m, A.is_gt)
-            if k in (0, 2, 4, 6):
-                z = k + 2 if k < 6 else nb
-                tt((T[tb][:, k:z, n:w],) + tuple((tb, w * i + n, w * i + w) for i in range(k, z)), row(16 * k, 16 * z), V("mh", 16 * k, 16 * z), A.not_equal)
-            if k + 1 < nb:
-                act(seg(k, 0, w), seg(k, 0, w), F.Identity, acc=V("rk", k, k + 1))
-        last, out = seg(nb - 1, 0, w), V("rk", nb - 1, nb)
-        op("v", lambda: g.vector.tensor_reduce(out[0], last[0], AxisListType.X, A.add), [out], [last])
-        ts(V("rko", 0, nb), V("rk", 0, nb), -16.0, A.add)
+        m = lambda k: V("mh", 16 * k + 15, 16 * k + 16)
 
-    def table_fill(i, j):
-        for k in range(i, j):
-            act(V("tab", 512 * k, 512 * k + 512), V("one", 0, 512), F.Copy, scale=0.0)
+        def ge(k):
+            ts(seg(k, 0, 16 * k + 16), row(0, 16 * k + 16), m(k), A.is_ge)
 
-    def scores(t, i):
-        h = i // 2
-        mm(V("ps%d" % i, 0, H), V("up"), V("ups"), V("t%d" % t, H * h, H * h + H), V("s%d" % t, H * h, H * h + H))
+        def fix(k, z):
+            tt((T[tb][:, k:z, n:w],) + tuple((tb, w * i + n, w * i + w) for i in range(k, z)), row(16 * k, 16 * z), V("mh", 16 * k, 16 * z), A.not_equal)
+
+        def gt(k):
+            ts(seg(k, 16 * k + 16, n), row(16 * k + 16, n), m(k), A.is_gt)
+            act(seg(k, 0, w), seg(k, 0, w), F.Identity, acc=V("rk", k, k + 1))
+
+        def rest(k0):
+            for k in range(k0, nb):
+                ge(k)
+                if k % 2 == 0 and k <= 6:
+                    fix(k, k + 2 if k < 6 else nb)
+                if k + 1 < nb:
+                    gt(k)
+            slot()
+            last, out = seg(nb - 1, 0, w), V("rk", nb - 1, nb)
+            op("v", lambda: g.vector.tensor_reduce(out[0], last[0], AxisListType.X, A.add), [out], [last])
+            slot()
+            ts(V("rko", 0, nb), V("rk", 0, nb), -16.0, A.add)
+        return ge, fix, gt, rest
+
+    def quant_state(t, a, e):
+        quant(V("t%d" % t, a, e), V("s%d" % t, a, e), V("x%d" % t, 4 * a, 4 * e))
+
+    def scores(t, h):
+        for i in (2 * h, 2 * h + 1):
+            mm(V("ps%d" % i, 0, H), V("up"), V("ups"), V("t%d" % t, H * h, H * h + H), V("s%d" % t, H * h, H * h + H))
 
     def top(h):
         scan(V("m3", H * h, H * h + H), V("rs3"), V("ps%d" % (2 * h), 0, H), 0.0, A.add, A.max)
@@ -165,203 +194,266 @@ def rank_program(g, core, T, topo):
     def mask(h):
         tt(V("ma", 64 * h, 64 * h + 64), V("m3", H * h + 2, H * h + H, 3), V("dm", 0, 64), A.add)
 
-    def layer_sum(xn, a, e):
-        tt(V(xn, 4 * a, 4 * e), V("gg", 4 * a, 4 * e), V("rl", 4 * a, 4 * e), A.add)
+    def layer_sum(xn, b, a, e):
+        tt(V(xn, 4 * a + b, 4 * e, 4), V("gg", 4 * a + b, 4 * e, 4), V("rl", 4 * a + b, 4 * e, 4), A.add)
 
-    plain = (1024.0, 0.0, 4.0)
+    def mix(a, e):
+        tt(V("gg", 4 * a, 4 * e), IND(V("yh"), V("qo", a // 4, e // 4)), V("xh", 4 * a, 4 * e), A.add)
+
+    def layer(h):
+        quant(V("zq", H * h, H * h + H), V("zs", H * h, H * h + H), V("gg", 4 * H * h, 4 * H * h + 4 * H))
+        for b in range(4):
+            ps = V("ps%d" % (4 * h + b), 0, H)
+            mm(ps, V("wq", 128 * b, 128 * b + 128), V("wsp", 128 * b, 128 * b + 128), V("zq", H * h, H * h + H), V("zs", H * h, H * h + H))
+            act(V("rl", 4 * H * h + b, 4 * H * h + 4 * H, 4), ps, F.Relu, scale=0.015625)
+
+    ge1, fix1, gt1, rest1 = ranker("m3", 2, 3, 128)
+    ge2, fix2, gt2, rest2 = ranker("cand", 0, 1, NC)
 
     dma("a", T.ub[:], T.u[:], [V("ub")], [])
     dma("s", T.x0[:, 0:4 * H], T.x[:, 0:4 * H], [V("x0", 0, 4 * H)], [])
     dma("a", T.x0[:, 4 * H:4 * C], T.x[:, 4 * H:4 * C], [V("x0", 4 * H, 4 * C)], [])
     iota(V("pi", 0, 1), [[0, 1]], 0, 1)
     iota(V("i16"), [[16, 8]])
+    iota(V("c16"), [[0, 9], [1, 16]])
+    iota(V("iot"), [[1, NC]])
     ms(V("one"), 1.0)
     op("g", lambda: g.affine_select(T.eb[:], T.one[:, 0:516], [[-1, 516]], A.is_equal, 0.0, 3, 4), [V("eb")], [V("one")])
-    iota(V("c16"), [[0, 9], [1, 16]])
-    iota(V("iot"), [[1, 128]])
     iota(V("c4"), [[0, 96], [1, 4]])
-    table_fill(0, 4)
+    for name, k in (("tf0", 0), ("tf0", 1), ("tf0", 2), ("tm0", 0)):
+        act(V(name, 512 * k, 512 * k + 512), V("one", 0, 512), F.Copy, scale=0.0)
     ms(V("rs3"), 0.0)
     ts(V("pi", 1, 2), V("pi", 0, 1), 15, A.bitwise_and)
+    ms(V("fs"), 1.0)
     ms(V("rs3", 0, H, 3), -1e29)
-    cp(col(0), V("pi", 1, 2))
     cp(V("uo"), V("i16"))
-    for k in range(3):
-        ms(V("pw", 400 * k, 400 * k + 400), plain[k])
-    ts(V("col", 1, 4), V("i16", 0, 3), col(0), A.add, 0.5, A.add)
+    cp(col(0), V("pi", 1, 2))
     ts(V("pj", 0, 1), V("pi", 1, 2), 2, A.arith_shift_right)
     ts(V("pj", 1, 2), V("pi", 1, 2), 3, A.bitwise_and)
-    ts(col(11), col(0), 3.0, A.mult)
-    for b in range(4):
-        quant(V("eq", 128 * b, 128 * b + 128), V("es", 128 * b, 128 * b + 128), V("eb", 3 - b, 515 - b))
-    cp(V("col", 4, 6), V("pj", 0, 2))
+    ms(V("fs", 0, 64, 4), 0.0)
+    ms(V("fs", 3, 64, 4), -BIG)
+    ms(V("fc"), BIG)
     ts(V("dm"), V("c16"), col(0), A.not_equal, -1e29, A.mult)
     ts(V("sg"), V("c16"), 0.0, A.is_equal, -3e29, A.mult)
+    ts(V("col", 1, 4), V("i16", 0, 3), col(0), A.add, 0.5, A.add)
+    ts(col(11), col(0), 3.0, A.mult, 0.5, A.add)
+    cp(V("col", 4, 6), V("pj", 0, 2))
+    ts(col(7), col(0), float(W), A.mult, 48.0, A.add)
+    ts(col(8), col(0), float(W), A.mult, 47.0, A.add)
+    ts(col(9), col(0), float(-W), A.mult, 15.0 * W + 48.0, A.add)
+    ts(col(10), col(0), float(-W), A.mult, 15.0 * W + 47.0, A.add)
+    ts(V("col", 12, 15), V("iot", 0, 3), col(11), A.add)
+    ts(V("flg"), V("iot"), float(K), A.is_lt)
     quant(V("uq"), V("us"), V("ub"))
     ts(col(6), col(5), 4.0 * H, A.add)
+    ms(V("val"), BIG)
     op("v", lambda: g.vector.tensor_copy(T.up[:, 0:128].bitcast(dt.uint32), T.uq[:, 0:128].bitcast(dt.uint32).indirect(T.uo[:, 0:8])),
        [V("up")], [V("uq"), V("uo")])
     op("a", lambda: g.scalar.activation(T.ups[:, 0:128], T.us[:, 0:128].indirect(T.uo[:, 0:8]), F.Copy), [V("ups")], [V("us"), V("uo")])
-    for h in range(2):
-        quant(V("t0", H * h, H * h + H), V("s0", H * h, H * h + H), V("x0", 4 * H * h, 4 * H * h + 4 * H))
-    table_fill(4, 5)
+    spare += [
+        lambda: ms(V("val", 192, 384), -BIG),
+        lambda: ms(V("ff", 0, W), 0.0),
+        lambda: ms(V("fm", 0, W), 0.0),
+        lambda: ms(V("pa0", 0, 400), 1024.0),
+        lambda: ms(V("pa0", 400, 800), 0.0),
+        lambda: ms(V("pb0"), 4.0),
+        lambda: ts(V("dw"), V("c4"), col(4), A.is_equal, 4096.0, A.mult),
+    ] + [(lambda b: lambda: quant(V("eq", 128 * b, 128 * b + 128), V("es", 128 * b, 128 * b + 128), V("eb", 3 - b, 515 - b)))(b) for b in range(4)]
+    quant_state(0, 0, H)
+    send(0, V("lt0", 0, H), V("t0", 0, H), "rt0", codes=True)
+    scores(0, 0)
+    quant_state(0, H, C)
+    send(0, V("ls0"), V("s0"), "rt0")
+    gfill("tm0", 512, 16 * W, 0)
+    scores(0, 1)
+    top(0)
+    slot()
+    mask(0)
+    top(1)
+    hold("mh", "ma", 0, 64)
+    slot()
+    mask(1)
+    ge1(0)
+    fix1(0, 2)
+    gt1(0)
+    hold("mh", "ma", 64, 128)
+    for k in (1, 2, 3):
+        ge1(k)
+        if k == 2:
+            fix1(2, 4)
+        gt1(k)
 
     for t in range(R):
-        tq, sq, hb, lh, xs, lt = "t%d" % t, "s%d" % t, "h%d" % t, "lh%d" % t, "x%d" % t, "lt%d" % t
-        send(t, V(lt, 0, H), V(tq, 0, H), "rt%d" % t, codes=True)
-        if t == 0:
-            send(t, V("ls%d" % t), V(sq), "rt%d" % t)
-            for i in (0, 2, 1, 3):
-                scores(t, i)
-            top(0)
-            top(1)
-            mask(0)
-        else:
-            scores(t, 0)
-            scores(t, 1)
-            top(0)
-            quant(V(tq, H, C), V(sq, H, C), V(xs, 4 * H, 4 * C))
-            send(t, V("ls%d" % t), V(sq), "rt%d" % t)
-            scores(t, 2)
-            scores(t, 3)
-            mask(0)
-            top(1)
-        hold("mh", "ma", 0, 64)
-        mask(1)
-        hold("mh", "ma", 64, 128)
-        ranks("m3", 2, 3, 128)
-        ts(V("sel"), IND(V("iot"), V("rko", 0, 8)), float(K), A.is_lt)
-        scan(V("pos"), V("sel"), V("sel"), 0.0, A.add, A.max)
-        for k in range(2):
-            act(V("junk", 128 * k, 128 * k + 128), V("pos"), F.Sign, bias=col(1 + k), scale=-1.0, acc=V("cn", 128 * k + 127, 128 * k + 128))
-        ts(V("junk", 256, C), V("pos"), col(3), A.is_le)
-        if t == 0:
-            ts(V("so", 3, 6), V("col", 1, 4), -0.5, A.add)
-        scan(V("cn", 256, C), V("junk", 256, C), V("junk", 256, C), -128.0, A.add, A.add)
-        if t == 0:
-            ts(V("so", 0, 3), V("iot", 0, 3), col(11), A.add)
-        ts(V("co", 0, 3), V("cn", 127, C, 128), 0.5, A.mult, 64.0, A.add)
+        tq, hb, lh, xs, lt = "t%d" % t, "h%d" % t, "lh%d" % t, "x%d" % t, "lt%d" % t
+        tf, tm, pa, pb = "tf%d" % t, "tm%d" % t, "pa%d" % t, "pb%d" % t
+        rest1(4)
+        slot()
+        ts(V("sel", 0, 128), IND(V("iot"), V("rko", 0, 8)), float(K), A.is_lt)
+        slot()
+        scan(V("pos", 0, 128), V("sel", 0, 128), V("sel", 0, 128), 0.0, A.add, A.max)
+        slot()
+        invert(V("co", 0, 3), 128, 1)
+        slot()
         for i in range(3):
-            tt(V("ma", i, 144, 3), IND(V("psb", 128 * i, 128 * i + 128), V("co", 0, 3)), V("dm", i, 144, 3), A.add)
-            act(V("cand", i, 144, 3), IND(V("psb", 128 * i, 128 * i + 128), V("co", 0, 3)), F.Copy)
+            tt(V("ma", i, NC, 3), IND(V("psb", 128 * i, 128 * i + 128), V("co", 0, 3)), V("dm", i, NC, 3), A.add)
+            act(V("cand", i, NC, 3), IND(V("psb", 128 * i, 128 * i + 128), V("co", 0, 3)), F.Copy)
         for i in range(3):
-            act(V("crow", i, 144, 3), IND(V("iot"), V("co", 0, 3)), F.Copy, bias=float(i - H), scale=3.0)
+            act(V("crow", i, NC, 3), IND(V("iot"), V("co", 0, 3)), F.Copy, bias=float(i - H), scale=3.0)
+        slot()
         hold("mh", "ma", 0, 64)
-        hold("mh", "ma", 64, 144)
-        ranks("cand", 0, 1, 144)
-        if t == 0:
-            table_fill(5, 6)
+        hold("mh", "ma", 64, NC)
+        slot()
+        rest2(0)
+        slot()
         scat(V(hb), V("rko", 0, 9), V("crow"))
         send(t, V(lh), V(hb, 0, K), "rh%d" % t)
         send(t, V(lt, H, C), V(tq, H, C), "rt%d" % t, codes=True)
-        wrap("oh", "oa", V(hb, 0, K), K)
-        count("pn", V(hb, 0, K), K, lambda k: V("oh", 16 * k + 15, 16 * k + 16))
-        for h in range(2):
-            act(V("xh", 4 * H * h, 4 * H * h + 4 * H), V(xs, 4 * H * h, 4 * H * h + 4 * H), F.Copy, scale=0.5)
-        if t == 0:
-            ts(col(7), col(0), float(W), A.mult, 48.0, A.add)
-            ts(col(8), col(0), float(W), A.mult, 47.0, A.add)
-            ts(col(9), col(0), float(-W), A.mult, 15.0 * W + 144.0, A.add)
-            ts(col(10), col(0), float(-W), A.mult, 15.0 * W + 143.0, A.add)
-            ms(V("val", 0, 96), 1.0)
-            ms(V("val", 96, 160), -1.0)
-            ms(V("fout", 0, W), 0.0)
-        else:
-            quant(V("vq"), V("vs"), V("vb"))
-        ts(V("po", 0, 3), V("pn", 0, 3), 47.0, A.add, 0.5, A.mult)
-        scat(V("krow"), V("po", 0, 3), V("iot", 0, K))
-        wrap("oh", "oa", IND(V("krow"), V("so")), 96)
-        cp(V("kw"), V("oh", 15, 96, 16))
+        if t + 1 < R:
+            gfill("tf1", 0, 16 * W, 0)
+            gfill("tm1", 0, 16 * W, 0)
+            gfill("pa1", 0, 400, 1024)
+            gfill("pa1", 400, 800, 0)
+            gfill("pb1", 0, 400, 4)
+        act(V("sel"), IND(V("flg"), V("rko", 0, 9)), F.Copy)
+        act(V("rr"), IND(V("iot"), V("rko", 0, 9)), F.Copy)
+        scan(V("pos"), V("sel"), V("sel"), 0.0, A.add, A.max)
+        slot()
+        invert(V("eo", 0, 3), NC, 12)
+        slot()
+        tt(V("oa"), IND(V("rr"), V("eo", 0, 3)), V("dm", 0, K), A.add)
+        slot()
+        hold("oh", "oa", 0, K)
+        slot(len(spare))
+        cp(V("kw", 0, 3), V("oh", 15, K, 16))
         arrive(t, "rh%d" % t, [V(lh)], 1)
         if t == 0:
             dma("s", T.wq[:].bitcast(dt.uint8), T.wc[:], [V("wq")], [V(lh)])
             dma("s", T.wsp[:], T.ws[:], [V("wsp")], [V(lh)])
             dma("s", T.vb[:], T.v[:], [V("vb")], [V(lh)])
-        act(V("brow"), IND(V(lh), V("kw")), F.Copy)
-        wrap("bh", "ba", IND(V(lh), V("kw", 0, 3)), K)
-        count("sn", V(lh), K, lambda k: V("bh", 16 * k + 15, 16 * k + 16))
-        tt(V("fc", 0, 32), V("brow", 0, 32), V("brow", 16, 48), A.is_gt)
-        tt(V("fc", 32, 48), V("brow", 0, 16), V("brow", 32, 48), A.is_gt)
-        tt(V("fc", 48, 64), V("fc", 32, 48), V("fc", 0, 16), A.subtract)
-        tt(V("val", 112, 128), V("fc", 48, 64), V("fc", 16, 32), A.subtract)
-        tt(V("val", 128, 144), V("fc", 48, 64), V("fc", 16, 32), A.subtract)
-        ts(V("fo", 0, 3), V("sn", 0, 3), col(7), A.add)
-        ts(V("fo", 3, 6), V("sn", 0, 3), -1.0, A.mult, col(9), A.add)
-        ts(V("fo", 6, 8), V("sn", 0, 2), col(8), A.add)
-        ts(V("fo", 8, 10), V("sn", 1, 3), -1.0, A.mult, col(10), A.add)
-        scat(V("tab"), V("fo"), V("val"))
-        arrive(t, "rt%d" % t, [V(lt), V("ls%d" % t)], 3)
-        act(V("bz"), V("brow", K, 96), F.Copy, bias=2048.0, scale=4.0)
-        if t == 0:
-            act(V("c4"), V("c4"), F.Abs, bias=col(4), scale=-1.0)
-            act(V("dw"), V("c4"), F.Relu, bias=4096.0, scale=-4096.0)
-        else:
-            for k in range(3):
-                act(V("pw", 400 * k, 400 * k + 400), V("one", 0, 400), F.Copy, scale=plain[k])
-        for b in range(4):
-            mm(V("ps%d" % b, 0, C), V("eq", 128 * b, 128 * b + 128), V("es", 128 * b, 128 * b + 128), V(lt), V("ls%d" % t))
-            act(V("yh", b, 4 * C, 4), V("ps%d" % b, 0, C), F.Copy, scale=0.5)
-        between = [
-            lambda: cp(V("arow"), IND(V(hb, 0, K), V("kw"))),
-            lambda: tt(V("oa", 0, K), V("arow", K, 96), V("dm", 0, K), A.add),
-            lambda: hold("oh", "oa", 0, K),
-            lambda: ts(V("ao", 0, 3), V("oh", 15, K, 16), float(H), A.add),
-            lambda: ts(V("ao", 3, 6), V("oh", 15, K, 16), H + 400.0, A.add),
-            lambda: ts(V("ao", 6, 9), V("oh", 15, K, 16), H + 800.0, A.add),
-            lambda: ts(V("lo", 2, 10, 2), V("fo", 1, 5), float(W), A.add),
-            lambda: cp(V("lo", 0, 11, 10), V("fo", 0, 6, 5)),
-            lambda: tt(V("d1"), V("brow", K, 96), V("arow", K, 96), A.subtract),
-            lambda: ts(V("dl"), V("d1"), -1.0 - H, A.add, 1.0 / 512.0, A.mult),
-        ]
-        for s in range(16):
-            for a in (W * s, W * s + 2 * K):
-                scan(V("fout", a + W, a + W + 2 * K), V("fout", a, a + 2 * K), V("tab", a, a + 2 * K), 0.0, A.max, A.add)
-            if s < len(between):
-                between[s]()
-        big = 131072.0
-        ts(V("pm", 0, 1), V("fout", 16 * W + 95, 16 * W + 96), big, A.mult)
+        act(V("brow"), IND(V(lh), V("kw", 0, 3)), F.Copy)
+        tt(V("ba"), IND(V(lh), V("kw", 0, 3)), V("dm", 0, K), A.add)
+        hold("bh", "ba", 0, K)
+        count(lambda k: V("sn", k, k + 1), V(lh), K, lambda k: V("bh", 16 * k + 15, 16 * k + 16), (0, 1, 2))
         for k in range(3):
-            act(V("l4", k, K, 3), IND(V("fout"), V("lo", 2 * k, 2 * k + 1)), F.Copy, scale=2048.0 + big,
-                bias=(2048.0 + big if k == 0 else 0.0) - (big if k != 2 else 0.0))
-            ts(V("cr", k, K, 3), IND(V("fout"), V("lo", 6 + 2 * k, 7 + 2 * k)), big, A.mult)
-        tt(V("cl"), V("cr"), V("l4"), A.add)
+            n = (k + 1) % 3
+            tt(V("fc", k, 64, 4), V("brow", 16 * k, 16 * k + 16), V("brow", 16 * n, 16 * n + 16), A.is_gt)
+        scan(V("val", 256, 320), V("fs"), V("fc"), 0.0, A.mult, A.add)
+        ts(V("fo", 0, 3), V("sn", 0, 3), col(7), A.add)
+        ts(V("fo", 3, 5), V("sn", 0, 2), col(8), A.add)
+        ts(V("fo", 6, 8), V("sn", 1, 3), -1.0, A.mult, col(10), A.add)
+        ts(V("fo", 8, 11), V("sn", 0, 3), -1.0, A.mult, col(9), A.add)
+        scat(V(tf), V("fo", 0, 5), V("val", 3, 320, 4))
+        scat(V(tm), V("fo", 6, 11), V("val", 259, 4 * NC, 4))
+        count(lambda k: V("cm", k, k + 1), V("pos"), NC, lambda k: col(1 + k), (0, 1, 2))
+        for k in range(3):
+            act(V("bz", k, K, 3), V("brow", 16 * k, 16 * k + 16), F.Copy, bias=2048.0, scale=4.0)
+        for h in range(2):
+            act(V("xh", 4 * H * h, 4 * H * h + 4 * H), V(xs, 4 * H * h, 4 * H * h + 4 * H), F.Copy, scale=0.5)
+
+        def unpack():
+            act(V("a4"), IND(V("crow"), V("en", 0, 3)), F.Copy, bias=2048.0 + 4.0 * (H + 1), scale=4.0)
+            arrive(t, "rt%d" % t, [V(lt), V("ls%d" % t)], 3)
+            for b in range(4):
+                mm(V("ps%d" % b, 0, C), V("eq", 128 * b, 128 * b + 128), V("es", 128 * b, 128 * b + 128), V(lt), V("ls%d" % t))
+                act(V("yh", b, 4 * C, 4), V("ps%d" % b, 0, C), F.Copy, scale=0.5)
+
+        def length(k, win, off):
+            ts(V("l4", k, K, 3), IND(win, off), 1.0 + 2048.0 / BIG, A.mult, (2048.0, -BIG, 0.0)[k], A.add)
+
+        def both(k, off):
+            tt(V("cl", k, K, 3), IND(V("fm"), off), V("l4", k, K, 3), A.add)
+
+        between = {
+            0: lambda: ts(V("lo", 0, 4, 2), V("fo", 1, 3), float(W), A.add),
+            1: lambda: ts(V("lo", 4, 8, 2), V("fo", 8, 10), float(W), A.add),
+            2: lambda: (ts(V("en", 0, 3), V("cm", 0, 3), 0.5, A.mult, NC / 2.0, A.add), unpack()),
+            3: lambda: tt(V("oa"), IND(V("crow"), V("en", 0, 3)), V("dm", 0, K), A.add),
+            4: lambda: hold("oh", "oa", 0, K),
+            5: lambda: ts(V("ao", 0, 3), V("oh", 15, K, 16), float(H), A.add),
+            6: lambda: ts(V("ao", 3, 6), V("oh", 15, K, 16), H + 400.0, A.add),
+            7: lambda: ts(V("ao", 6, 9), V("oh", 15, K, 16), float(H), A.add),
+            9: lambda: quant(V("vq"), V("vs"), V("vb")) if t + 1 == R else None,
+            11: lambda: tt(V("d1"), V("bz"), V("a4"), A.subtract),
+            12: lambda: ts(V("dl"), V("d1"), 1.0 / 2048.0, A.mult),
+            15: lambda: length(0, V("ff", 0, 16 * W), V("fo", 0, 1)),
+        }
+        for s in range(16):
+            a = W * s
+            for f, tab in (("ff", tf), ("fm", tm)):
+                scan(V(f, a + W, a + 2 * W), V(f, a, a + W), V(tab, a, a + W), 0.0, A.max, A.add)
+            if s in between:
+                between[s]()
+        length(1, V("ff"), V("lo", 0, 1))
+        length(2, V("ff"), V("lo", 2, 3))
+        cp(V("pm", 0, 1), V("ff", 17 * W - 1, 17 * W))
+        both(0, V("lo", 4, 5))
+        both(1, V("lo", 6, 7))
+        both(2, V("fo", 10, 11))
         scan(V("pm", 1, K + 1), V("cl"), V("cl"), V("pm", 0, 1), A.max, A.max)
         tt(V("on"), V("pm", 1, K + 1), V("pm", 0, K), A.subtract)
         tt(V("pv", 0, K), V("bz"), V("on"), A.subtract)
         act(V("pv", K, 96), V("on"), F.Copy, scale=-1.0 / 512.0)
-        ts(V("pv", 96, 144), V("on"), 4.0, A.add)
         act(V("nn"), V("on"), F.Copy, bias=1.0, scale=-1.0 / 2048.0)
         tt(V("od"), V("on"), V("dl"), A.mult)
-        scat(V("pw"), V("ao", 0, 9), V("pv"))
+        ts(V("pv", 96, NC), V("on"), 4.0, A.add)
+        scat(V(pa), V("ao", 0, 6), V("pv", 0, 96))
         scan(V("d1", K - 1, -1, -1), V("nn", K - 1, -1, -1), V("od", K - 1, -1, -1), 0.0, A.mult, A.add)
-        scan(V("cap", C - 1, -1, -1), V("pw", 400 + C, 400, -1), V("pw", C - 1, -1, -1), 4.0 * (C - 1 - H), A.add, A.min)
-        scan(V("qr"), V("pw", 800, 800 + C), V("cap"), V("d1", 0, 1), A.add, A.min)
-        scan(V("qh"), V("dw"), V("qr"), 0.0, A.add, A.min)
-        ts(V("qo"), V("qh", 3, C, 4), col(6), A.add, col(5), A.max)
+        scat(V(pb), V("ao", 6, 9), V("pv", 96, NC))
+        scan(V("cap", C - 1, -1, -1), V(pa, 400 + C, 400, -1), V(pa, C - 1, -1, -1), 4.0 * (C - 1 - H), A.add, A.min)
+
+        scan(V("qr"), V(pb, 0, C), V("cap"), V("d1", 0, 1), A.add, A.min)
+        for a in (0, H):
+            scan(V("qh", a, a + H), V("dw", a, a + H), V("qr", a, a + H), 0.0, A.add, A.min)
+        for h in range(2):
+            ts(V("qo", K * h, K * h + K), V("qh", H * h + 3, H * h + H, 4), col(6), A.add, col(5), A.max)
         act(V("oq%d" % t), V("qr"), F.Relu, bias=float(H), scale=0.25)
         dma("s", T.oq[:, C * t:C * t + C], T["oq%d" % t][0:128:16, :], [], [V("oq%d" % t)])
-        if t + 1 < R:
-            table_fill(0, 3)
         xn, tn, sn = "x%d" % (t + 1), "t%d" % (t + 1), "s%d" % (t + 1)
-        for h in range(2):
-            a, e = 4 * H * h, 4 * H * h + 4 * H
-            tt(V("gg", a, e), IND(V("yh"), V("qo", K * h, K * h + K)), V("xh", a, e), A.add)
-            quant(V("zq", H * h, H * h + H), V("zs", H * h, H * h + H), V("gg", a, e))
-            for b in range(4):
-                ps = V("ps%d" % (4 * h + b), 0, H)
-                mm(ps, V("wq", 128 * b, 128 * b + 128), V("wsp", 128 * b, 128 * b + 128), V("zq", H * h, H * h + H), V("zs", H * h, H * h + H))
-                act(V("rl", a + b, e, 4), ps, F.Relu, scale=0.015625)
-        layer_sum(xn, 0, H)
+        mix(0, H)
+        mix(H, H + 24)
+        layer(0)
+        mix(H + 24, C)
+        layer_sum(xn, 0, 0, H)
+        layer(1)
+        for b in (1, 2, 3):
+            layer_sum(xn, b, 0, H)
         if t + 1 < R:
-            table_fill(3, 6)
-            layer_sum(xn, H, 224)
-            quant(V(tn, 0, H), V(sn, 0, H), V(xn, 0, 4 * H))
-            layer_sum(xn, 224, C)
+            layer_sum(xn, 0, H, C)
+            quant_state(t + 1, 0, H)
+            send(t + 1, V("lt%d" % (t + 1), 0, H), V(tn, 0, H), "rt%d" % (t + 1), codes=True)
+            scores(t + 1, 0)
+            layer_sum(xn, 1, H, C)
+            layer_sum(xn, 2, H, 256)
+            top(0)
+            layer_sum(xn, 2, 256, C)
+            mask(0)
+            layer_sum(xn, 3, H, C)
+            hold("mh", "ma", 0, 64)
+            quant_state(t + 1, H, C)
+            send(t + 1, V("ls%d" % (t + 1)), V(sn), "rt%d" % (t + 1))
+            scores(t + 1, 1)
+            ge1(0)
+            fix1(0, 2)
+            ge1(1)
+            ge1(2)
+            top(1)
+            ge1(3)
+            fix1(2, 4)
+            mask(1)
+            gt1(0)
+            gt1(1)
+            hold("mh", "ma", 64, 128)
+            gt1(2)
+            gt1(3)
             continue
-        layer_sum(xn, H, 256)
-        for h, (a, e, c0, c1) in enumerate(((256, 280, 0, 256), (280, C, 256, C))):
-            layer_sum(xn, a, e)
-            quant(V(tn, c0, c1), V(sn, c0, c1), V(xn, 4 * c0, 4 * c1))
+        for b in range(4):
+            layer_sum(xn, b, H, 256)
+        layer_sum(xn, 0, 256, C)
+        for h, (c0, c1) in enumerate(((0, 256), (256, C))):
+            if h:
+                for b in (1, 2, 3):
+                    layer_sum(xn, b, c0, c1)
+            quant_state(t + 1, c0, c1)
             mm(V("ps%d" % h, 0, c1 - c0), V("vq"), V("vs"), V(tn, c0, c1), V(sn, c0, c1))
             dma("s", T.oc[:, 4 * c0:4 * c1], T[tn][:, c0:c1].bitcast(dt.uint8), [], [V(tn, c0, c1)])
             if h == 0:

@@ -3,7 +3,10 @@ from concourse.mybir import dt, AxisListType, AluOpType as A, ActivationFunction
 C, K, R = 384, 48, 2
 W = 2 * K
 H = C // 2
+M = 240
+PIECE = ((0, M), (M, C))
 NC = 3 * K
+STEP = 512.0
 BIG = 131072.0
 F32, BF, U16, I32, Q4, U8 = "float32", "bfloat16", "uint16", "int32", "float8_e4m3fn_x4", "uint8"
 SCRATCH = {}
@@ -15,19 +18,19 @@ for _n, _w, _d in [
     ("uq", 128, Q4), ("us", 128, U8), ("up", 128, Q4), ("ups", 128, U8), ("vq", 128, Q4), ("vs", 128, U8),
     ("wq", 512, Q4), ("wsp", 512, U8), ("eq", 512, Q4), ("es", 512, U8),
     ("iot", NC, F32), ("c16", NC, F32), ("c4", C, BF), ("pi", 4, I32), ("pj", 16, I32), ("col", 32, F32), ("i16", 8, F32),
-    ("dm", NC, F32), ("sg", NC, F32), ("rs3", H, BF), ("dw", C, BF), ("flg", NC, BF), ("uo", 8, U16),
-    ("psb", C, F32), ("m3", C, F32), ("ma", NC, F32), ("mh", NC, F32), ("junk", 3 * NC, BF),
+    ("dm", NC, F32), ("sg", NC, F32), ("rs3", M, BF), ("dw", C, BF), ("flg", NC, BF), ("uo", 8, U16),
+    ("psb", C, F32), ("m3", C, F32), ("ma", NC, F32), ("mh", NC, F32), ("junk", 480, BF),
     ("rk", 10, F32), ("rko", 10, U16), ("sel", NC, BF), ("pos", NC, BF), ("cn", 3 * NC, F32), ("co", 4, U16),
     ("cand", NC, F32), ("crow", NC, BF), ("h0", NC, BF), ("h1", NC, BF), ("lh0", K, BF), ("lh1", K, BF),
-    ("rr", NC, BF), ("eo", 4, U16), ("en", 4, U16), ("cm", 4, F32),
+    ("rr", NC, BF), ("eo", 4, U16), ("cm", 4, F32),
     ("oa", K, F32), ("oh", K, F32), ("kw", 4, U16), ("a4", K, F32), ("ao", 10, U16),
-    ("ba", K, F32), ("bh", K, F32), ("brow", K, F32), ("sn", 4, F32), ("fo", 12, U16), ("lo", 8, U16),
-    ("fc", 64, BF), ("fs", 64, BF), ("val", 4 * NC, BF),
+    ("ba", K, F32), ("bh", K, F32), ("brow", K, F32), ("sn", 4, F32), ("fo", 12, U16), ("lf", 8, F32), ("lo", 8, U16),
+    ("fc", 64, BF), ("fs", 64, BF), ("fl", 64, BF), ("val", 160, BF), ("cv", K, F32),
     ("tf0", 16 * W, BF), ("tf1", 16 * W, BF), ("tm0", 16 * W, BF), ("tm1", 16 * W, BF), ("ff", 17 * W, BF), ("fm", 17 * W, BF),
     ("l4", K, F32), ("cl", K, F32), ("pm", 56, F32), ("on", K, F32),
     ("bz", K, F32), ("dl", K, F32), ("nn", K, F32), ("od", K, F32), ("d1", K, F32), ("pv", NC, BF),
     ("pa0", 800, BF), ("pa1", 800, BF), ("pb0", 400, BF), ("pb1", 400, BF),
-    ("cap", C, BF), ("qr", C, BF), ("qh", C, BF), ("qo", 96, U16),
+    ("cap", C, BF), ("qf", H, BF), ("qr", C, BF), ("qh", C, BF), ("qo", 96, U16),
     ("oq0", C, F32), ("oq1", C, F32), ("ysb", C, F32),
 ]:
     SCRATCH[_n] = ("sbuf", [128, _w], _d)
@@ -82,6 +85,9 @@ def rank_program(g, core, T, topo):
     def scan(o, d0, d1, init, f0, f1):
         op("v", lambda: g.vector.tensor_tensor_scan(o[0], d0[0], d1[0], ap(init), f0, f1), [o], [d0, d1, init])
 
+    def reduce(o, a, f, size=False):
+        op("v", lambda: g.vector.tensor_reduce(o[0], a[0], AxisListType.X, f, apply_absolute_value=size), [o], [a])
+
     def ms(o, c):
         op("v", lambda: g.vector.memset(o[0], c), [o], [])
 
@@ -135,18 +141,20 @@ def rank_program(g, core, T, topo):
     def hold(h, a, i, j):
         scan(V(h, i, j), V("sg", 0, j - i), V(a, i, j), 0.0, A.add, A.max)
 
-    def count(out, row, n, bias, ks):
+    def count(out, row, n, bias, ks, scale=-1.0):
         for k in ks:
-            act(V("junk", NC * k, NC * k + n), row, F.Sign, bias=bias(k), scale=-1.0, acc=out(k))
+            act(V("junk", NC * k, NC * k + n), row, F.Sign, bias=bias(k), scale=scale, acc=out(k))
 
-    def invert(out, n, c0):
-        count(lambda k: V("cn", NC * k + n - 1, NC * k + n), V("pos", 0, n), n, lambda k: col(c0 + k), (0, 1))
-        j = V("junk", 2 * NC, 2 * NC + n)
-        ts(j, V("pos", 0, n), col(c0 + 2), A.is_le)
+    def invert(out, n):
+        sel = V("sel", 0, n)
+        scan(V("pos", 0, n), sel, sel, 0.0, A.add, A.min)
+        scan(V("cn", 0, n), sel, V("one", 0, n), col(7), A.add, A.add)
+        count(lambda k: V("cm", k, k + 1), V("pos", 0, n), n, lambda k: col(1 + k), (0, 1), 1.0 / STEP)
         slot()
-        scan(V("cn", 2 * NC, 2 * NC + n), j, j, float(-n), A.add, A.add)
+        reduce(V("cm", 2, 3), V("cn", 0, n), A.min, True)
         slot()
-        ts(out, V("cn", n - 1, 3 * NC, NC), 0.5, A.mult, n / 2.0, A.add)
+        cp(V(out, 2, 3), V("cm", 2, 3))
+        ts(V(out, 0, 2), V("cm", 0, 2), 0.5, A.mult, n / 2.0, A.add)
 
     def ranker(name, a, s, n):
         row = lambda i, j: V(name, a + s * i, a + s * (j - 1) + 1, s)
@@ -155,44 +163,48 @@ def rank_program(g, core, T, topo):
         seg = lambda k, i, j: (T[tb][:, k, i:j], (tb, w * k + i, w * k + j))
         m = lambda k: V("mh", 16 * k + 15, 16 * k + 16)
 
-        def ge(k):
-            ts(seg(k, 0, 16 * k + 16), row(0, 16 * k + 16), m(k), A.is_ge)
+        def low(k, scalar=False):
+            if scalar:
+                act(seg(k, 0, 16 * k + 16), row(0, 16 * k + 16), F.Sign, bias=m(k), scale=-1.0)
+            else:
+                ts(seg(k, 0, 16 * k + 16), row(0, 16 * k + 16), m(k), A.is_lt)
 
         def fix(k, z):
-            tt((T[tb][:, k:z, n:w],) + tuple((tb, w * i + n, w * i + w) for i in range(k, z)), row(16 * k, 16 * z), V("mh", 16 * k, 16 * z), A.not_equal)
+            tt((T[tb][:, k:z, n:w],) + tuple((tb, w * i + n, w * i + w) for i in range(k, z)), row(16 * k, 16 * z), V("mh", 16 * k, 16 * z), A.is_equal)
 
-        def gt(k):
-            ts(seg(k, 16 * k + 16, n), row(16 * k + 16, n), m(k), A.is_gt)
-            act(seg(k, 0, w), seg(k, 0, w), F.Identity, acc=V("rk", k, k + 1))
+        def high(k):
+            ts(seg(k, 16 * k + 16, n), row(16 * k + 16, n), m(k), A.is_le)
 
-        def rest(k0):
-            for k in range(k0, nb):
-                ge(k)
-                if k % 2 == 0 and k <= 6:
-                    fix(k, k + 2 if k < 6 else nb)
-                if k + 1 < nb:
-                    gt(k)
+        def total(k):
+            act(seg(k, 0, w), seg(k, 0, w), F.Relu, acc=V("rk", k, k + 1))
+
+        def close(k):
+            reduce(V("rk", k, k + 1), seg(k, 0, w), A.add)
+            reduce(V("rk", nb - 1, nb), seg(nb - 1, 0, w), A.add)
             slot()
-            last, out = seg(nb - 1, 0, w), V("rk", nb - 1, nb)
-            op("v", lambda: g.vector.tensor_reduce(out[0], last[0], AxisListType.X, A.add), [out], [last])
-            slot()
-            ts(V("rko", 0, nb), V("rk", 0, nb), -16.0, A.add)
-        return ge, fix, gt, rest
+            ts(V("rko", 0, nb), V("rk", 0, nb), -1.0, A.mult, float(n), A.add)
+        return low, fix, high, total, close
 
     def quant_state(t, a, e):
         quant(V("t%d" % t, a, e), V("s%d" % t, a, e), V("x%d" % t, 4 * a, 4 * e))
 
     def scores(t, h):
+        a, e = PIECE[h]
         for i in (2 * h, 2 * h + 1):
-            mm(V("ps%d" % i, 0, H), V("up"), V("ups"), V("t%d" % t, H * h, H * h + H), V("s%d" % t, H * h, H * h + H))
+            mm(V("ps%d" % i, 0, e - a), V("up"), V("ups"), V("t%d" % t, a, e), V("s%d" % t, a, e))
 
     def top(h):
-        scan(V("m3", H * h, H * h + H), V("rs3"), V("ps%d" % (2 * h), 0, H), 0.0, A.add, A.max)
+        a, e = PIECE[h]
+        scan(V("m3", a, e), V("rs3", 0, e - a), V("ps%d" % (2 * h), 0, e - a), 0.0, A.add, A.max)
+
+    def planes(h):
+        a, e = PIECE[h]
         for i in range(3):
-            act(V("psb", 128 * i + 64 * h, 128 * i + 64 * h + 64), V("ps%d" % (2 * h + 1), i, H, 3), F.Copy)
+            act(V("psb", 128 * i + a // 3, 128 * i + e // 3), V("ps%d" % (2 * h + 1), i, e - a, 3), F.Copy)
 
     def mask(h):
-        tt(V("ma", 64 * h, 64 * h + 64), V("m3", H * h + 2, H * h + H, 3), V("dm", 0, 64), A.add)
+        a, e = PIECE[h]
+        tt(V("ma", a // 3, e // 3), V("m3", a + 2, e, 3), V("dm", 0, (e - a) // 3), A.add)
 
     def layer_sum(xn, b, a, e):
         tt(V(xn, 4 * a + b, 4 * e, 4), V("gg", 4 * a + b, 4 * e, 4), V("rl", 4 * a + b, 4 * e, 4), A.add)
@@ -201,18 +213,50 @@ def rank_program(g, core, T, topo):
         tt(V("gg", 4 * a, 4 * e), IND(V("yh"), V("qo", a // 4, e // 4)), V("xh", 4 * a, 4 * e), A.add)
 
     def layer(h):
-        quant(V("zq", H * h, H * h + H), V("zs", H * h, H * h + H), V("gg", 4 * H * h, 4 * H * h + 4 * H))
+        a, e = H * h, H * h + H
+        quant(V("zq", a, e), V("zs", a, e), V("gg", 4 * a, 4 * e))
         for b in range(4):
-            ps = V("ps%d" % (4 * h + b), 0, H)
-            mm(ps, V("wq", 128 * b, 128 * b + 128), V("wsp", 128 * b, 128 * b + 128), V("zq", H * h, H * h + H), V("zs", H * h, H * h + H))
-            act(V("rl", 4 * H * h + b, 4 * H * h + 4 * H, 4), ps, F.Relu, scale=0.015625)
+            ps = V("ps%d" % (4 * h + b), 0, e - a)
+            mm(ps, V("wq", 128 * b, 128 * b + 128), V("wsp", 128 * b, 128 * b + 128), V("zq", a, e), V("zs", a, e))
+            act(V("rl", 4 * a + b, 4 * e, 4), ps, F.Relu, scale=0.015625)
 
-    ge1, fix1, gt1, rest1 = ranker("m3", 2, 3, 128)
-    ge2, fix2, gt2, rest2 = ranker("cand", 0, 1, NC)
+    low1, fix1, high1, total1, close1 = ranker("m3", 2, 3, 128)
+    low2, fix2, high2, total2, close2 = ranker("cand", 0, 1, NC)
+
+    TB9 = lambda k: (T.tb9[:, k, :], ("tb9", 160 * k, 160 * k + 160))
+
+    def rank_triples(late):
+        for k in (2, 3, 4):
+            low1(k, True)
+        if late:
+            top(1)
+        else:
+            mask(1)
+        low1(0)
+        fix1(0, 2)
+        low1(1)
+        if late:
+            mask(1)
+        for k in range(5):
+            high1(k)
+            if k == 1:
+                fix1(2, 5)
+                hold("mh", "ma", M // 3, 128)
+            if k == 3:
+                low1(5, True)
+            total1(k)
+        fix1(5, 8)
+        high1(5)
+        total1(5)
+        low1(6)
+        high1(6)
+        low1(7)
+        planes(1)
+        close1(6)
 
     dma("a", T.ub[:], T.u[:], [V("ub")], [])
-    dma("s", T.x0[:, 0:4 * H], T.x[:, 0:4 * H], [V("x0", 0, 4 * H)], [])
-    dma("a", T.x0[:, 4 * H:4 * C], T.x[:, 4 * H:4 * C], [V("x0", 4 * H, 4 * C)], [])
+    dma("s", T.x0[:, 0:4 * M], T.x[:, 0:4 * M], [V("x0", 0, 4 * M)], [])
+    dma("a", T.x0[:, 4 * M:4 * C], T.x[:, 4 * M:4 * C], [V("x0", 4 * M, 4 * C)], [])
     iota(V("pi", 0, 1), [[0, 1]], 0, 1)
     iota(V("i16"), [[16, 8]])
     iota(V("c16"), [[0, 9], [1, 16]])
@@ -225,7 +269,7 @@ def rank_program(g, core, T, topo):
     ms(V("rs3"), 0.0)
     ts(V("pi", 1, 2), V("pi", 0, 1), 15, A.bitwise_and)
     ms(V("fs"), 1.0)
-    ms(V("rs3", 0, H, 3), -1e29)
+    ms(V("rs3", 0, M, 3), -1e29)
     cp(V("uo"), V("i16"))
     cp(col(0), V("pi", 1, 2))
     ts(V("pj", 0, 1), V("pi", 1, 2), 2, A.arith_shift_right)
@@ -236,14 +280,13 @@ def rank_program(g, core, T, topo):
     ts(V("dm"), V("c16"), col(0), A.not_equal, -1e29, A.mult)
     ts(V("sg"), V("c16"), 0.0, A.is_equal, -3e29, A.mult)
     ts(V("col", 1, 4), V("i16", 0, 3), col(0), A.add, 0.5, A.add)
-    ts(col(11), col(0), 3.0, A.mult, 0.5, A.add)
     cp(V("col", 4, 6), V("pj", 0, 2))
-    ts(col(7), col(0), float(W), A.mult, 48.0, A.add)
-    ts(col(8), col(0), float(W), A.mult, 47.0, A.add)
-    ts(col(9), col(0), float(-W), A.mult, 15.0 * W + 48.0, A.add)
-    ts(col(10), col(0), float(-W), A.mult, 15.0 * W + 47.0, A.add)
-    ts(V("col", 12, 15), V("iot", 0, 3), col(11), A.add)
-    ts(V("flg"), V("iot"), float(K), A.is_lt)
+    ts(col(7), col(0), STEP, A.mult, 33.0 * STEP - 1.0, A.add)
+    ts(col(11), col(0), -1.0, A.add)
+    ts(V("pj", 8, 11), V("col", 1, 4), 0.5, A.add, 1.0 / 3.0, A.mult)
+    ts(V("pj", 12, 15), V("col", 1, 4), -0.5, A.add, 1.0 / 3.0, A.mult)
+    ts(V("flg"), V("iot"), float(K), A.is_lt, -STEP, A.mult)
+    ts(V("pj", 4, 7), V("iot", 0, 3), col(11), A.add, 1.0 / 3.0, A.mult)
     quant(V("uq"), V("us"), V("ub"))
     ts(col(6), col(5), 4.0 * H, A.add)
     ms(V("val"), BIG)
@@ -251,48 +294,41 @@ def rank_program(g, core, T, topo):
        [V("up")], [V("uq"), V("uo")])
     op("a", lambda: g.scalar.activation(T.ups[:, 0:128], T.us[:, 0:128].indirect(T.uo[:, 0:8]), F.Copy), [V("ups")], [V("us"), V("uo")])
     spare += [
-        lambda: ms(V("val", 192, 384), -BIG),
-        lambda: ms(V("ff", 0, W), 0.0),
-        lambda: ms(V("fm", 0, W), 0.0),
+        lambda: (ts(V("col", 8, 11), V("pj", 8, 11), float(W), A.mult, 48.0, A.add),
+                 ts(V("col", 12, 15), V("pj", 12, 15), float(-W), A.mult, 16.0 * W + 48.0, A.add)),
+        lambda: [ts(V("col", 20 + i, 26, 2), V("pj", 4, 7), float(W), A.mult, 47.0 + i, A.add) for i in range(2)],
+        lambda: [ts(V("col", 26 + i, 32, 2), V("pj", 4, 7), float(-W), A.mult, 5.0 * W + 47.0 + i, A.add) for i in range(2)],
+        lambda: (ms(V("ff", 0, W), 0.0), ms(V("fm", 0, W), 0.0)),
+        lambda: [ms(V("cv", k, K, 3), c) for k, c in enumerate((2048.0, -BIG, 0.0))],
+        lambda: (ms(V("val", 16, 64, 3), -BIG), ms(V("val", 18, 64, 3), 0.0)),
+        lambda: (ms(V("val", 96, NC, 3), 0.0), ms(V("val", 98, NC, 3), -BIG)),
         lambda: ms(V("pa0", 0, 400), 1024.0),
         lambda: ms(V("pa0", 400, 800), 0.0),
         lambda: ms(V("pb0"), 4.0),
         lambda: ts(V("dw"), V("c4"), col(4), A.is_equal, 4096.0, A.mult),
     ] + [(lambda b: lambda: quant(V("eq", 128 * b, 128 * b + 128), V("es", 128 * b, 128 * b + 128), V("eb", 3 - b, 515 - b)))(b) for b in range(4)]
-    quant_state(0, 0, H)
-    send(0, V("lt0", 0, H), V("t0", 0, H), "rt0", codes=True)
+    quant_state(0, 0, M)
+    send(0, V("lt0", 0, M), V("t0", 0, M), "rt0", codes=True)
     scores(0, 0)
-    quant_state(0, H, C)
+    quant_state(0, M, C)
     send(0, V("ls0"), V("s0"), "rt0")
     gfill("tm0", 512, 16 * W, 0)
     scores(0, 1)
     top(0)
+    planes(0)
     slot()
     mask(0)
     top(1)
-    hold("mh", "ma", 0, 64)
-    slot()
-    mask(1)
-    ge1(0)
-    fix1(0, 2)
-    gt1(0)
-    hold("mh", "ma", 64, 128)
-    for k in (1, 2, 3):
-        ge1(k)
-        if k == 2:
-            fix1(2, 4)
-        gt1(k)
+    hold("mh", "ma", 0, M // 3)
 
     for t in range(R):
         tq, hb, lh, xs, lt = "t%d" % t, "h%d" % t, "lh%d" % t, "x%d" % t, "lt%d" % t
         tf, tm, pa, pb = "tf%d" % t, "tm%d" % t, "pa%d" % t, "pb%d" % t
-        rest1(4)
+        rank_triples(t > 0)
         slot()
-        ts(V("sel", 0, 128), IND(V("iot"), V("rko", 0, 8)), float(K), A.is_lt)
+        ts(V("sel", 0, 128), IND(V("iot"), V("rko", 0, 8)), float(K), A.is_lt, -STEP, A.mult)
         slot()
-        scan(V("pos", 0, 128), V("sel", 0, 128), V("sel", 0, 128), 0.0, A.add, A.max)
-        slot()
-        invert(V("co", 0, 3), 128, 1)
+        invert("co", 128)
         slot()
         for i in range(3):
             tt(V("ma", i, NC, 3), IND(V("psb", 128 * i, 128 * i + 128), V("co", 0, 3)), V("dm", i, NC, 3), A.add)
@@ -300,14 +336,34 @@ def rank_program(g, core, T, topo):
         for i in range(3):
             act(V("crow", i, NC, 3), IND(V("iot"), V("co", 0, 3)), F.Copy, bias=float(i - H), scale=3.0)
         slot()
-        hold("mh", "ma", 0, 64)
         hold("mh", "ma", 64, NC)
+        hold("mh", "ma", 0, 64)
         slot()
-        rest2(0)
+        for k in (8, 7, 6, 5):
+            low2(k, True)
+        fix2(6, 9)
+        high2(7)
+        high2(6)
+        fix2(3, 6)
+        high2(5)
+        for k in (8, 7, 6, 5):
+            total2(k)
+        for k in (4, 3):
+            low2(k)
+            high2(k)
+            total2(k)
+        fix2(0, 3)
+        for k in range(3):
+            low2(k)
+            high2(k)
+        for k in range(3):
+            scan(V("junk", 160 * k, 160 * k + 160), TB9(k), TB9(k), 0.0, A.add, A.add)
+        ts(V("rko", 3, 9), V("rk", 3, 9), -1.0, A.mult, float(NC), A.add)
+        ts(V("rko", 0, 3), V("junk", 159, 480, 160), -0.5, A.mult, float(NC), A.add)
         slot()
         scat(V(hb), V("rko", 0, 9), V("crow"))
         send(t, V(lh), V(hb, 0, K), "rh%d" % t)
-        send(t, V(lt, H, C), V(tq, H, C), "rt%d" % t, codes=True)
+        send(t, V(lt, M, C), V(tq, M, C), "rt%d" % t, codes=True)
         if t + 1 < R:
             gfill("tf1", 0, 16 * W, 0)
             gfill("tm1", 0, 16 * W, 0)
@@ -316,11 +372,10 @@ def rank_program(g, core, T, topo):
             gfill("pb1", 0, 400, 4)
         act(V("sel"), IND(V("flg"), V("rko", 0, 9)), F.Copy)
         act(V("rr"), IND(V("iot"), V("rko", 0, 9)), F.Copy)
-        scan(V("pos"), V("sel"), V("sel"), 0.0, A.add, A.max)
-        slot()
-        invert(V("eo", 0, 3), NC, 12)
+        invert("eo", NC)
         slot()
         tt(V("oa"), IND(V("rr"), V("eo", 0, 3)), V("dm", 0, K), A.add)
+        act(V("a4"), IND(V("crow"), V("eo", 0, 3)), F.Copy, bias=2048.0 + 4.0 * (H + 1), scale=4.0)
         slot()
         hold("oh", "oa", 0, K)
         slot(len(spare))
@@ -333,62 +388,67 @@ def rank_program(g, core, T, topo):
         act(V("brow"), IND(V(lh), V("kw", 0, 3)), F.Copy)
         tt(V("ba"), IND(V(lh), V("kw", 0, 3)), V("dm", 0, K), A.add)
         hold("bh", "ba", 0, K)
-        count(lambda k: V("sn", k, k + 1), V(lh), K, lambda k: V("bh", 16 * k + 15, 16 * k + 16), (0, 1, 2))
+        count(lambda k: V("sn", k, k + 1), V(lh), K, lambda k: V("bh", 16 * k + 15, 16 * k + 16), (0, 2, 1))
         for k in range(3):
-            n = (k + 1) % 3
-            tt(V("fc", k, 64, 4), V("brow", 16 * k, 16 * k + 16), V("brow", 16 * n, 16 * n + 16), A.is_gt)
-        scan(V("val", 256, 320), V("fs"), V("fc"), 0.0, A.mult, A.add)
-        ts(V("fo", 0, 3), V("sn", 0, 3), col(7), A.add)
-        ts(V("fo", 3, 5), V("sn", 0, 2), col(8), A.add)
-        ts(V("fo", 6, 8), V("sn", 1, 3), -1.0, A.mult, col(10), A.add)
-        ts(V("fo", 8, 11), V("sn", 0, 3), -1.0, A.mult, col(9), A.add)
-        scat(V(tf), V("fo", 0, 5), V("val", 3, 320, 4))
-        scat(V(tm), V("fo", 6, 11), V("val", 259, 4 * NC, 4))
-        count(lambda k: V("cm", k, k + 1), V("pos"), NC, lambda k: col(1 + k), (0, 1, 2))
-        for k in range(3):
-            act(V("bz", k, K, 3), V("brow", 16 * k, 16 * k + 16), F.Copy, bias=2048.0, scale=4.0)
+            tt(V("fc", k, 64, 4), V("brow", k, K, 3), V("brow", (k + 1) % 3, K, 3), A.is_gt)
+        scan(V("fl"), V("fs"), V("fc"), 0.0, A.mult, A.add)
+
+        def slots(m, c, out, later=0.0):
+            i = 20 + 6 * m + 2 * c
+            ts(out, V("col", i, i + 2), V("sn", c, c + 1), A.subtract if m else A.add, later, A.add)
+
+        def table(name, a, e, i, v):
+            scat(V(name, W * a, W * e), V("fo", i, i + 2), V("val", v, v + 32))
+
+        slots(0, 0, V("fo", 1, -1, -1))
+        slots(1, 2, V("fo", 10, 12))
+        for a in (16, 96):
+            cp(V("val", a + 1, a + K, 3), V("fl", 3, 64, 4))
+        slots(0, 1, V("fo", 2, 6, 2))
+        slots(1, 1, V("fo", 7, 10, 2))
+        table(tf, 0, 6, 0, 0)
+        table(tm, 0, 6, 10, 128)
+        slots(0, 2, V("fo", 3, 6, 2), 5.0 * W)
+        act(V("bz"), V("brow"), F.Copy, bias=2048.0, scale=4.0)
         for h in range(2):
             act(V("xh", 4 * H * h, 4 * H * h + 4 * H), V(xs, 4 * H * h, 4 * H * h + 4 * H), F.Copy, scale=0.5)
+        arrive(t, "rt%d" % t, [V(lt), V("ls%d" % t)], 3)
+        for b in range(4):
+            mm(V("ps%d" % b, 0, C), V("eq", 128 * b, 128 * b + 128), V("es", 128 * b, 128 * b + 128), V(lt), V("ls%d" % t))
+            act(V("yh", b, 4 * C, 4), V("ps%d" % b, 0, C), F.Copy, scale=0.5)
 
-        def unpack():
-            act(V("a4"), IND(V("crow"), V("en", 0, 3)), F.Copy, bias=2048.0 + 4.0 * (H + 1), scale=4.0)
-            arrive(t, "rt%d" % t, [V(lt), V("ls%d" % t)], 3)
-            for b in range(4):
-                mm(V("ps%d" % b, 0, C), V("eq", 128 * b, 128 * b + 128), V("es", 128 * b, 128 * b + 128), V(lt), V("ls%d" % t))
-                act(V("yh", b, 4 * C, 4), V("ps%d" % b, 0, C), F.Copy, scale=0.5)
-
-        def length(k, win, off):
-            ts(V("l4", k, K, 3), IND(win, off), 1.0 + 2048.0 / BIG, A.mult, (2048.0, -BIG, 0.0)[k], A.add)
-
-        def both(k, off):
-            tt(V("cl", k, K, 3), IND(V("fm"), off), V("l4", k, K, 3), A.add)
+        def where(k):
+            ts(V("ao", 3 * k, 3 * k + 3), V("mh", 15, K, 16), H + 400.0 * (k % 2), A.add)
 
         between = {
-            0: lambda: ts(V("lo", 0, 4, 2), V("fo", 1, 3), float(W), A.add),
-            1: lambda: ts(V("lo", 4, 8, 2), V("fo", 8, 10), float(W), A.add),
-            2: lambda: (ts(V("en", 0, 3), V("cm", 0, 3), 0.5, A.mult, NC / 2.0, A.add), unpack()),
-            3: lambda: tt(V("oa"), IND(V("crow"), V("en", 0, 3)), V("dm", 0, K), A.add),
-            4: lambda: hold("oh", "oa", 0, K),
-            5: lambda: ts(V("ao", 0, 3), V("oh", 15, K, 16), float(H), A.add),
-            6: lambda: ts(V("ao", 3, 6), V("oh", 15, K, 16), H + 400.0, A.add),
-            7: lambda: ts(V("ao", 6, 9), V("oh", 15, K, 16), float(H), A.add),
-            9: lambda: quant(V("vq"), V("vs"), V("vb")) if t + 1 == R else None,
-            11: lambda: tt(V("d1"), V("bz"), V("a4"), A.subtract),
-            12: lambda: ts(V("dl"), V("d1"), 1.0 / 2048.0, A.mult),
-            15: lambda: length(0, V("ff", 0, 16 * W), V("fo", 0, 1)),
+            0: lambda: table(tf, 5, 16, 2, 32),
+            1: lambda: table(tm, 5, 16, 6, 96),
+            2: lambda: table(tf, 5, 16, 4, 64),
+            3: lambda: table(tm, 5, 16, 8, 64),
+            4: lambda: tt(V("ma", 0, K), IND(V("crow"), V("eo", 0, 3)), V("dm", 0, K), A.add),
+            5: lambda: (tt(V("lf", 0, 3), V("col", 8, 11), V("sn", 0, 3), A.add), tt(V("lf", 3, 6), V("col", 12, 15), V("sn", 0, 3), A.subtract)),
+            6: lambda: (hold("mh", "ma", 0, K), tt(V("d1"), V("bz"), V("a4"), A.subtract)),
+            7: lambda: (cp(V("lo", 0, 3), V("lf", 0, 3)), cp(V("lo", 4, 5), V("lf", 3, 4))),
+            8: lambda: (cp(V("lo", 6, 8), V("lf", 4, 6)), ts(V("dl"), V("d1"), 1.0 / 2048.0, A.mult)),
+            9: lambda: (where(0), where(1)),
+            10: lambda: (where(2), quant(V("vq"), V("vs"), V("vb")) if t + 1 == R else None),
+            11: lambda: ts(V("l4", 0, 32), IND(V("ff", 0, 12 * W), V("lo", 0, 2)), 1.0 + 2048.0 / BIG, A.mult),
+            12: lambda: tt(V("oa", 16, K), IND(V("fm", 0, 12 * W), V("lo", 6, 8)), V("cv", 16, K), A.add),
+            13: lambda: tt(V("oa", 0, 16), V("l4", 0, 16), V("cv", 0, 16), A.add),
+            14: lambda: tt(V("cl", 16, 32), V("l4", 16, 32), V("oa", 16, 32), A.add),
         }
         for s in range(16):
             a = W * s
             for f, tab in (("ff", tf), ("fm", tm)):
                 scan(V(f, a + W, a + 2 * W), V(f, a, a + W), V(tab, a, a + W), 0.0, A.max, A.add)
+                if s == 0 and tab == tf:
+                    slots(1, 0, V("fo", 6, 10, 2), 5.0 * W)
             if s in between:
                 between[s]()
-        length(1, V("ff"), V("lo", 0, 1))
-        length(2, V("ff"), V("lo", 2, 3))
+        ts(V("l4", 32, K), IND(V("ff"), V("lo", 2, 3)), 1.0 + 2048.0 / BIG, A.mult)
+        tt(V("cl", 0, 16), IND(V("fm"), V("lo", 4, 5)), V("oa", 0, 16), A.add)
         cp(V("pm", 0, 1), V("ff", 17 * W - 1, 17 * W))
-        both(0, V("lo", 4, 5))
-        both(1, V("lo", 6, 7))
-        both(2, V("fo", 10, 11))
+        tt(V("cl", 32, K), V("l4", 32, K), V("oa", 32, K), A.add)
         scan(V("pm", 1, K + 1), V("cl"), V("cl"), V("pm", 0, 1), A.max, A.max)
         tt(V("on"), V("pm", 1, K + 1), V("pm", 0, K), A.subtract)
         tt(V("pv", 0, K), V("bz"), V("on"), A.subtract)
@@ -400,58 +460,46 @@ def rank_program(g, core, T, topo):
         scan(V("d1", K - 1, -1, -1), V("nn", K - 1, -1, -1), V("od", K - 1, -1, -1), 0.0, A.mult, A.add)
         scat(V(pb), V("ao", 6, 9), V("pv", 96, NC))
         scan(V("cap", C - 1, -1, -1), V(pa, 400 + C, 400, -1), V(pa, C - 1, -1, -1), 4.0 * (C - 1 - H), A.add, A.min)
-
-        scan(V("qr"), V(pb, 0, C), V("cap"), V("d1", 0, 1), A.add, A.min)
-        for a in (0, H):
-            scan(V("qh", a, a + H), V("dw", a, a + H), V("qr", a, a + H), 0.0, A.add, A.min)
-        for h in range(2):
-            ts(V("qo", K * h, K * h + K), V("qh", H * h + 3, H * h + H, 4), col(6), A.add, col(5), A.max)
+        for name, e in (("qf", H), ("qr", C)):
+            scan(V(name, 0, e), V(pb, 0, e), V("cap", 0, e), V("d1", 0, 1), A.add, A.min)
+        for name, a, e in (("qf", 0, H), ("qr", H, C)):
+            scan(V("qh", a, e), V("dw", a, e), V(name, a, e), 0.0, A.add, A.min)
+        for a, e in ((0, H), (H, C)):
+            ts(V("qo", a // 4, e // 4), V("qh", a + 3, e, 4), col(6), A.add, col(5), A.max)
         act(V("oq%d" % t), V("qr"), F.Relu, bias=float(H), scale=0.25)
         dma("s", T.oq[:, C * t:C * t + C], T["oq%d" % t][0:128:16, :], [], [V("oq%d" % t)])
         xn, tn, sn = "x%d" % (t + 1), "t%d" % (t + 1), "s%d" % (t + 1)
         mix(0, H)
-        mix(H, H + 24)
+        mix(H, H + 32)
         layer(0)
-        mix(H + 24, C)
+        mix(H + 32, C)
         layer_sum(xn, 0, 0, H)
         layer(1)
         for b in (1, 2, 3):
             layer_sum(xn, b, 0, H)
+        layer_sum(xn, 0, H, C)
+        for b in (1, 2, 3):
+            layer_sum(xn, b, H, M)
+        layer_sum(xn, 1, M, C - 32)
         if t + 1 < R:
-            layer_sum(xn, 0, H, C)
-            quant_state(t + 1, 0, H)
-            send(t + 1, V("lt%d" % (t + 1), 0, H), V(tn, 0, H), "rt%d" % (t + 1), codes=True)
+            quant_state(t + 1, 0, M)
+            send(t + 1, V("lt%d" % (t + 1), 0, M), V(tn, 0, M), "rt%d" % (t + 1), codes=True)
             scores(t + 1, 0)
-            layer_sum(xn, 1, H, C)
-            layer_sum(xn, 2, H, 256)
+            layer_sum(xn, 1, C - 32, C)
+            layer_sum(xn, 2, M, C)
+            layer_sum(xn, 3, M, C)
             top(0)
-            layer_sum(xn, 2, 256, C)
-            mask(0)
-            layer_sum(xn, 3, H, C)
-            hold("mh", "ma", 0, 64)
-            quant_state(t + 1, H, C)
+            quant_state(t + 1, M, C)
             send(t + 1, V("ls%d" % (t + 1)), V(sn), "rt%d" % (t + 1))
             scores(t + 1, 1)
-            ge1(0)
-            fix1(0, 2)
-            ge1(1)
-            ge1(2)
-            top(1)
-            ge1(3)
-            fix1(2, 4)
-            mask(1)
-            gt1(0)
-            gt1(1)
-            hold("mh", "ma", 64, 128)
-            gt1(2)
-            gt1(3)
+            planes(0)
+            mask(0)
+            hold("mh", "ma", 0, M // 3)
             continue
-        for b in range(4):
-            layer_sum(xn, b, H, 256)
-        layer_sum(xn, 0, 256, C)
-        for h, (c0, c1) in enumerate(((0, 256), (256, C))):
+        for h, (c0, c1) in enumerate(PIECE):
             if h:
-                for b in (1, 2, 3):
+                layer_sum(xn, 1, C - 32, C)
+                for b in (2, 3):
                     layer_sum(xn, b, c0, c1)
             quant_state(t + 1, c0, c1)
             mm(V("ps%d" % h, 0, c1 - c0), V("vq"), V("vs"), V(tn, c0, c1), V(sn, c0, c1))

@@ -117,12 +117,12 @@ def rank_program(g, core, T, topo):
     def dma(q, o, a, writes, reads):
         op(q, lambda: eng[q].dma_start(o, a), writes, reads, kind="d", n=16)
 
-    def send(t, land, src, sem, codes=False):
+    def send(t, land, src, sem, codes=False, behind=()):
         dst = T.cores[rank ^ (1 << t)]
         rid, pid = topo.addr(dst)[:2]
         m = topo.mask(core, dst)
         o, a = (land[0].bitcast(dt.uint8), src[0].bitcast(dt.uint8)) if codes else (land[0], src[0])
-        op("g", lambda s: g.remote_dma(o, a, T.sem[sem], s, pid, rid, m), [], [src], kind="r", n=len(topo.engines(core, dst)))
+        op("g", lambda s: g.remote_dma(o, a, T.sem[sem], s, pid, rid, m), list(behind), [src], kind="r", n=len(topo.engines(core, dst)))
 
     def arrive(t, sem, lands, calls):
         src = T.cores[rank ^ (1 << t)]
@@ -146,15 +146,15 @@ def rank_program(g, core, T, topo):
             act(V("junk", NC * k, NC * k + n), row, F.Sign, bias=bias(k), scale=scale, acc=out(k))
 
     def invert(out, n):
-        sel = V("sel", 0, n)
-        scan(V("pos", 0, n), sel, sel, 0.0, A.add, A.min)
-        scan(V("cn", 0, n), sel, V("one", 0, n), col(7), A.add, A.add)
-        count(lambda k: V("cm", k, k + 1), V("pos", 0, n), n, lambda k: col(1 + k), (0, 1), 1.0 / STEP)
+        sel = V("sel", 0, n - 16)
+        scan(V("pos", 0, n - 16), sel, sel, 0.0, A.add, A.min)
+        scan(V("cn", n - 1, 31, -1), V("sel", n - 1, 31, -1), V("one", 0, n - 32), col(7), A.add, A.add)
+        count(lambda k: V("cm", k, k + 1), V("pos", 0, n - 16), n - 16, lambda k: col(1 + k), (0, 1), 1.0 / STEP)
         slot()
-        reduce(V("cm", 2, 3), V("cn", 0, n), A.min, True)
+        reduce(V("cm", 2, 3), V("cn", 32, n), A.min, True)
         slot()
-        cp(V(out, 2, 3), V("cm", 2, 3))
-        ts(V(out, 0, 2), V("cm", 0, 2), 0.5, A.mult, n / 2.0, A.add)
+        ts(V(out, 2, 3), V("cm", 2, 3), -1.0, A.mult, float(n), A.add)
+        ts(V(out, 0, 2), V("cm", 0, 2), 0.5, A.mult, (n - 16) / 2.0, A.add)
 
     def ranker(name, a, s, n):
         row = lambda i, j: V(name, a + s * i, a + s * (j - 1) + 1, s)
@@ -178,12 +178,15 @@ def rank_program(g, core, T, topo):
         def total(k):
             act(seg(k, 0, w), seg(k, 0, w), F.Relu, acc=V("rk", k, k + 1))
 
-        def close(k):
-            reduce(V("rk", k, k + 1), seg(k, 0, w), A.add)
-            reduce(V("rk", nb - 1, nb), seg(nb - 1, 0, w), A.add)
-            slot()
-            ts(V("rko", 0, nb), V("rk", 0, nb), -1.0, A.mult, float(n), A.add)
-        return low, fix, high, total, close
+        def twice(k, i):
+            scan(V("junk", w * i, w * i + w), seg(k, 0, w), seg(k, 0, w), 0.0, A.add, A.add)
+
+        def places(k, z, vector=False):
+            if vector:
+                ts(V("rko", k, z), V("junk", w - 1, w * (z - k), w), -0.5, A.mult, float(n), A.add)
+            else:
+                ts(V("rko", k, z), V("rk", k, z), -1.0, A.mult, float(n), A.add)
+        return low, fix, high, total, twice, places
 
     def quant_state(t, a, e):
         quant(V("t%d" % t, a, e), V("s%d" % t, a, e), V("x%d" % t, 4 * a, 4 * e))
@@ -213,50 +216,51 @@ def rank_program(g, core, T, topo):
         tt(V("gg", 4 * a, 4 * e), IND(V("yh"), V("qo", a // 4, e // 4)), V("xh", 4 * a, 4 * e), A.add)
 
     def layer(h):
-        a, e = H * h, H * h + H
+        a, e = 128 * h, 128 * h + 128
         quant(V("zq", a, e), V("zs", a, e), V("gg", 4 * a, 4 * e))
         for b in range(4):
-            ps = V("ps%d" % (4 * h + b), 0, e - a)
+            ps = V("ps%d" % (4 * (h % 2) + b), 0, e - a)
             mm(ps, V("wq", 128 * b, 128 * b + 128), V("wsp", 128 * b, 128 * b + 128), V("zq", a, e), V("zs", a, e))
             act(V("rl", 4 * a + b, 4 * e, 4), ps, F.Relu, scale=0.015625)
 
-    low1, fix1, high1, total1, close1 = ranker("m3", 2, 3, 128)
-    low2, fix2, high2, total2, close2 = ranker("cand", 0, 1, NC)
+    low1, fix1, high1, total1, twice1, places1 = ranker("m3", 2, 3, 128)
+    low2, fix2, high2, total2, twice2, places2 = ranker("cand", 0, 1, NC)
 
-    TB9 = lambda k: (T.tb9[:, k, :], ("tb9", 160 * k, 160 * k + 160))
-
-    def rank_triples(late):
+    def rank_triples():
         for k in (2, 3, 4):
             low1(k, True)
-        if late:
-            top(1)
-        else:
-            mask(1)
+        top(1)
         low1(0)
         fix1(0, 2)
         low1(1)
-        if late:
-            mask(1)
+        mask(1)
         for k in range(5):
             high1(k)
             if k == 1:
                 fix1(2, 5)
                 hold("mh", "ma", M // 3, 128)
-            if k == 3:
-                low1(5, True)
             total1(k)
         fix1(5, 8)
+        low1(5)
         high1(5)
         total1(5)
         low1(6)
         high1(6)
         low1(7)
+        twice1(6, 0)
+        places1(0, 4)
+        twice1(7, 1)
+        chosen = lambda k, z: (V("sel", 16 * k, 16 * z), IND(V("flg"), V("rko", k, z)))
+        places1(4, 6)
+        places1(6, 8, True)
+        act(*chosen(4, 6), F.Copy)
         planes(1)
-        close1(6)
+        cp(*chosen(0, 4))
+        cp(*chosen(6, 8))
 
-    dma("a", T.ub[:], T.u[:], [V("ub")], [])
+    dma("s", T.ub[:], T.u[:], [V("ub")], [])
     dma("s", T.x0[:, 0:4 * M], T.x[:, 0:4 * M], [V("x0", 0, 4 * M)], [])
-    dma("a", T.x0[:, 4 * M:4 * C], T.x[:, 4 * M:4 * C], [V("x0", 4 * M, 4 * C)], [])
+    dma("s", T.x0[:, 4 * M:4 * C], T.x[:, 4 * M:4 * C], [V("x0", 4 * M, 4 * C)], [])
     iota(V("pi", 0, 1), [[0, 1]], 0, 1)
     iota(V("i16"), [[16, 8]])
     iota(V("c16"), [[0, 9], [1, 16]])
@@ -264,36 +268,37 @@ def rank_program(g, core, T, topo):
     ms(V("one"), 1.0)
     op("g", lambda: g.affine_select(T.eb[:], T.one[:, 0:516], [[-1, 516]], A.is_equal, 0.0, 3, 4), [V("eb")], [V("one")])
     iota(V("c4"), [[0, 96], [1, 4]])
-    for name, k in (("tf0", 0), ("tf0", 1), ("tf0", 2), ("tm0", 0)):
-        act(V(name, 512 * k, 512 * k + 512), V("one", 0, 512), F.Copy, scale=0.0)
+    zero = lambda name, k: act(V(name, 512 * k, 512 * k + 512), V("one", 0, 512), F.Copy, scale=0.0)
+    zero("tf0", 0)
+    zero("tf0", 1)
     ms(V("rs3"), 0.0)
     ts(V("pi", 1, 2), V("pi", 0, 1), 15, A.bitwise_and)
     ms(V("fs"), 1.0)
+    ms(V("fc"), BIG)
     ms(V("rs3", 0, M, 3), -1e29)
     cp(V("uo"), V("i16"))
     cp(col(0), V("pi", 1, 2))
     ts(V("pj", 0, 1), V("pi", 1, 2), 2, A.arith_shift_right)
     ts(V("pj", 1, 2), V("pi", 1, 2), 3, A.bitwise_and)
-    ms(V("fs", 0, 64, 4), 0.0)
-    ms(V("fs", 3, 64, 4), -BIG)
-    ms(V("fc"), BIG)
-    ts(V("dm"), V("c16"), col(0), A.not_equal, -1e29, A.mult)
     ts(V("sg"), V("c16"), 0.0, A.is_equal, -3e29, A.mult)
-    ts(V("col", 1, 4), V("i16", 0, 3), col(0), A.add, 0.5, A.add)
-    cp(V("col", 4, 6), V("pj", 0, 2))
-    ts(col(7), col(0), STEP, A.mult, 33.0 * STEP - 1.0, A.add)
-    ts(col(11), col(0), -1.0, A.add)
-    ts(V("pj", 8, 11), V("col", 1, 4), 0.5, A.add, 1.0 / 3.0, A.mult)
-    ts(V("pj", 12, 15), V("col", 1, 4), -0.5, A.add, 1.0 / 3.0, A.mult)
-    ts(V("flg"), V("iot"), float(K), A.is_lt, -STEP, A.mult)
-    ts(V("pj", 4, 7), V("iot", 0, 3), col(11), A.add, 1.0 / 3.0, A.mult)
+    ts(V("dm"), V("c16"), col(0), A.not_equal, -1e29, A.mult)
     quant(V("uq"), V("us"), V("ub"))
-    ts(col(6), col(5), 4.0 * H, A.add)
-    ms(V("val"), BIG)
+    ts(V("col", 1, 4), V("i16", 0, 3), col(0), A.add, 0.5, A.add)
+    ts(col(7), col(0), -STEP, A.mult, 16.0 * STEP, A.add)
+    ts(col(11), col(0), -1.0, A.add)
     op("v", lambda: g.vector.tensor_copy(T.up[:, 0:128].bitcast(dt.uint32), T.uq[:, 0:128].bitcast(dt.uint32).indirect(T.uo[:, 0:8])),
        [V("up")], [V("uq"), V("uo")])
     op("a", lambda: g.scalar.activation(T.ups[:, 0:128], T.us[:, 0:128].indirect(T.uo[:, 0:8]), F.Copy), [V("ups")], [V("us"), V("uo")])
+    zero("tf0", 2)
+    zero("tm0", 0)
     spare += [
+        lambda: (ts(V("pj", 4, 7), V("iot", 0, 3), col(11), A.add, 1.0 / 3.0, A.mult),
+                 ts(V("pj", 8, 11), V("col", 1, 4), 0.5, A.add, 1.0 / 3.0, A.mult)),
+        lambda: (ts(V("pj", 12, 15), V("col", 1, 4), -0.5, A.add, 1.0 / 3.0, A.mult),
+                 cp(V("col", 4, 6), V("pj", 0, 2)),
+                 ms(V("val"), BIG)),
+        lambda: ts(V("flg"), V("iot"), float(K), A.is_lt, -STEP, A.mult),
+        lambda: (ms(V("fs", 0, 64, 4), 0.0), ms(V("fs", 3, 64, 4), -BIG), ts(col(6), col(5), 4.0 * H, A.add)),
         lambda: (ts(V("col", 8, 11), V("pj", 8, 11), float(W), A.mult, 48.0, A.add),
                  ts(V("col", 12, 15), V("pj", 12, 15), float(-W), A.mult, 16.0 * W + 48.0, A.add)),
         lambda: [ts(V("col", 20 + i, 26, 2), V("pj", 4, 7), float(W), A.mult, 47.0 + i, A.add) for i in range(2)],
@@ -307,26 +312,25 @@ def rank_program(g, core, T, topo):
         lambda: ms(V("pb0"), 4.0),
         lambda: ts(V("dw"), V("c4"), col(4), A.is_equal, 4096.0, A.mult),
     ] + [(lambda b: lambda: quant(V("eq", 128 * b, 128 * b + 128), V("es", 128 * b, 128 * b + 128), V("eb", 3 - b, 515 - b)))(b) for b in range(4)]
+    slot()
     quant_state(0, 0, M)
-    send(0, V("lt0", 0, M), V("t0", 0, M), "rt0", codes=True)
     scores(0, 0)
+    slot()
+    top(0)
     quant_state(0, M, C)
     send(0, V("ls0"), V("s0"), "rt0")
+    send(0, V("lt0", 0, M), V("t0", 0, M), "rt0", codes=True)
     gfill("tm0", 512, 16 * W, 0)
     scores(0, 1)
-    top(0)
     planes(0)
-    slot()
     mask(0)
-    top(1)
+    slot()
     hold("mh", "ma", 0, M // 3)
 
     for t in range(R):
         tq, hb, lh, xs, lt = "t%d" % t, "h%d" % t, "lh%d" % t, "x%d" % t, "lt%d" % t
         tf, tm, pa, pb = "tf%d" % t, "tm%d" % t, "pa%d" % t, "pb%d" % t
-        rank_triples(t > 0)
-        slot()
-        ts(V("sel", 0, 128), IND(V("iot"), V("rko", 0, 8)), float(K), A.is_lt, -STEP, A.mult)
+        rank_triples()
         slot()
         invert("co", 128)
         slot()
@@ -357,13 +361,13 @@ def rank_program(g, core, T, topo):
             low2(k)
             high2(k)
         for k in range(3):
-            scan(V("junk", 160 * k, 160 * k + 160), TB9(k), TB9(k), 0.0, A.add, A.add)
-        ts(V("rko", 3, 9), V("rk", 3, 9), -1.0, A.mult, float(NC), A.add)
-        ts(V("rko", 0, 3), V("junk", 159, 480, 160), -0.5, A.mult, float(NC), A.add)
+            twice2(k, k)
+        places2(3, 9)
+        places2(0, 3, True)
         slot()
         scat(V(hb), V("rko", 0, 9), V("crow"))
         send(t, V(lh), V(hb, 0, K), "rh%d" % t)
-        send(t, V(lt, M, C), V(tq, M, C), "rt%d" % t, codes=True)
+        send(t, V(lt, M, C), V(tq, M, C), "rt%d" % t, codes=True, behind=[V(hb, 0, K)])
         if t + 1 < R:
             gfill("tf1", 0, 16 * W, 0)
             gfill("tm1", 0, 16 * W, 0)
@@ -378,19 +382,21 @@ def rank_program(g, core, T, topo):
         act(V("a4"), IND(V("crow"), V("eo", 0, 3)), F.Copy, bias=2048.0 + 4.0 * (H + 1), scale=4.0)
         slot()
         hold("oh", "oa", 0, K)
-        slot(len(spare))
+        slot()
         cp(V("kw", 0, 3), V("oh", 15, K, 16))
+        slot(2)
         arrive(t, "rh%d" % t, [V(lh)], 1)
         if t == 0:
-            dma("s", T.wq[:].bitcast(dt.uint8), T.wc[:], [V("wq")], [V(lh)])
-            dma("s", T.wsp[:], T.ws[:], [V("wsp")], [V(lh)])
-            dma("s", T.vb[:], T.v[:], [V("vb")], [V(lh)])
+            dma("s", T.wq[:].bitcast(dt.uint8), T.wc[:], [V("wq"), V(tq, M, C)], [])
+            dma("s", T.wsp[:], T.ws[:], [V("wsp")], [])
         act(V("brow"), IND(V(lh), V("kw", 0, 3)), F.Copy)
         tt(V("ba"), IND(V(lh), V("kw", 0, 3)), V("dm", 0, K), A.add)
+        slot()
         hold("bh", "ba", 0, K)
         count(lambda k: V("sn", k, k + 1), V(lh), K, lambda k: V("bh", 16 * k + 15, 16 * k + 16), (0, 2, 1))
         for k in range(3):
             tt(V("fc", k, 64, 4), V("brow", k, K, 3), V("brow", (k + 1) % 3, K, 3), A.is_gt)
+        slot(len(spare))
         scan(V("fl"), V("fs"), V("fc"), 0.0, A.mult, A.add)
 
         def slots(m, c, out, later=0.0):
@@ -468,20 +474,23 @@ def rank_program(g, core, T, topo):
             ts(V("qo", a // 4, e // 4), V("qh", a + 3, e, 4), col(6), A.add, col(5), A.max)
         act(V("oq%d" % t), V("qr"), F.Relu, bias=float(H), scale=0.25)
         dma("s", T.oq[:, C * t:C * t + C], T["oq%d" % t][0:128:16, :], [], [V("oq%d" % t)])
+        if t == 0:
+            dma("s", T.vb[:], T.v[:], [V("vb")], [])
         xn, tn, sn = "x%d" % (t + 1), "t%d" % (t + 1), "s%d" % (t + 1)
-        mix(0, H)
-        mix(H, H + 32)
+        mix(0, 128)
+        mix(128, 256)
         layer(0)
-        mix(H + 32, C)
-        layer_sum(xn, 0, 0, H)
+        mix(256, C)
         layer(1)
+        layer_sum(xn, 0, 0, 128)
+        layer(2)
         for b in (1, 2, 3):
-            layer_sum(xn, b, 0, H)
-        layer_sum(xn, 0, H, C)
-        for b in (1, 2, 3):
-            layer_sum(xn, b, H, M)
-        layer_sum(xn, 1, M, C - 32)
+            layer_sum(xn, b, 0, 128)
         if t + 1 < R:
+            for b in range(4):
+                layer_sum(xn, b, 128, M)
+            layer_sum(xn, 0, M, C)
+            layer_sum(xn, 1, M, C - 32)
             quant_state(t + 1, 0, M)
             send(t + 1, V("lt%d" % (t + 1), 0, M), V(tn, 0, M), "rt%d" % (t + 1), codes=True)
             scores(t + 1, 0)
@@ -496,20 +505,22 @@ def rank_program(g, core, T, topo):
             mask(0)
             hold("mh", "ma", 0, M // 3)
             continue
-        for h, (c0, c1) in enumerate(PIECE):
-            if h:
-                layer_sum(xn, 1, C - 32, C)
-                for b in (2, 3):
-                    layer_sum(xn, b, c0, c1)
+        for h in range(3):
+            c0, c1 = 128 * h, 128 * h + 128
+            for b in (1, 2, 3) if h else ():
+                layer_sum(xn, b, c0, c1)
+            if h < 2:
+                layer_sum(xn, 0, c1, c1 + 128)
             quant_state(t + 1, c0, c1)
-            mm(V("ps%d" % h, 0, c1 - c0), V("vq"), V("vs"), V(tn, c0, c1), V(sn, c0, c1))
+            ps = V("ps%d" % (4 + h), 0, 128)
+            mm(ps, V("vq"), V("vs"), V(tn, c0, c1), V(sn, c0, c1))
             dma("s", T.oc[:, 4 * c0:4 * c1], T[tn][:, c0:c1].bitcast(dt.uint8), [], [V(tn, c0, c1)])
-            if h == 0:
-                act(V("ysb", c0, c1), V("ps0", 0, c1 - c0), F.Copy)
+            if h < 2:
+                act(V("ysb", c0, c1), ps, F.Copy)
             else:
                 for k in range(4):
                     dma("a" if k % 2 else "s", T.osc[4 * k:4 * k + 4, :], T[sn][32 * k:32 * k + 4, :], [], [V(sn)])
-                cp(V("ysb", c0, c1), V("ps1", 0, c1 - c0))
+                cp(V("ysb", c0, c1), ps)
             dma("a", T.y[:, c0:c1], T.ysb[:, c0:c1], [], [V("ysb", c0, c1)])
 
     emit(ops, eng, T)

@@ -6,25 +6,25 @@ H = C // 2
 M = 240
 PIECE = ((0, M), (M, C))
 NC = 3 * K
-STEP = 512.0
+PLAIN = (("pa", 0, 1024), ("pa", 400, 0), ("pb", 0, 4))
+STEP = 256.0
 BIG = 131072.0
 F32, BF, U16, I32, Q4, U8 = "float32", "bfloat16", "uint16", "int32", "float8_e4m3fn_x4", "uint8"
 SCRATCH = {}
 for _n, _w, _d in [
-    ("x0", 4 * C, BF), ("x1", 4 * C, BF), ("x2", 4 * C, BF), ("xh", 4 * C, BF), ("gg", 4 * C, BF), ("yh", 4 * C, BF),
+    ("x0", 4 * C, BF), ("x1", 4 * C, BF), ("x2", 4 * C, BF), ("xh", 4 * C, BF), ("gg", 4 * C, BF), ("yh", 4 * C, BF), ("yg", 4 * H, BF),
     ("rl", 4 * C, F32), ("ub", 512, BF), ("vb", 512, BF), ("eb", 516, BF), ("one", 520, BF),
     ("t0", C, Q4), ("t1", C, Q4), ("t2", C, Q4), ("s0", C, U8), ("s1", C, U8), ("s2", C, U8),
     ("lt0", C, Q4), ("lt1", C, Q4), ("ls0", C, U8), ("ls1", C, U8), ("zq", C, Q4), ("zs", C, U8),
     ("uq", 128, Q4), ("us", 128, U8), ("up", 128, Q4), ("ups", 128, U8), ("vq", 128, Q4), ("vs", 128, U8),
     ("wq", 512, Q4), ("wsp", 512, U8), ("eq", 512, Q4), ("es", 512, U8),
     ("iot", NC, F32), ("c16", NC, F32), ("c4", C, BF), ("pi", 4, I32), ("pj", 16, I32), ("col", 32, F32), ("i16", 8, F32),
-    ("dm", NC, F32), ("sg", NC, F32), ("rs3", M, BF), ("dw", C, BF), ("flg", NC, BF), ("uo", 8, U16),
+    ("dm", NC, F32), ("sg", NC, F32), ("rs3", M, BF), ("dw", C, BF), ("flg", 128, BF), ("uo", 8, U16),
     ("psb", C, F32), ("m3", C, F32), ("ma", NC, F32), ("mh", NC, F32), ("junk", 480, BF),
-    ("rk", 10, F32), ("rko", 10, U16), ("sel", NC, BF), ("pos", NC, BF), ("cn", 3 * NC, F32), ("co", 4, U16),
+    ("rk", 10, F32), ("rko", 10, U16), ("sel", NC, BF), ("pos", NC, BF), ("cn", 3 * NC, BF), ("co", 4, U16),
     ("cand", NC, F32), ("crow", NC, BF), ("h0", NC, BF), ("h1", NC, BF), ("lh0", K, BF), ("lh1", K, BF),
-    ("rr", NC, BF), ("eo", 4, U16), ("cm", 4, F32),
-    ("oa", K, F32), ("oh", K, F32), ("kw", 4, U16), ("a4", K, F32), ("ao", 10, U16),
-    ("ba", K, F32), ("bh", K, F32), ("brow", K, F32), ("sn", 4, F32), ("fo", 12, U16), ("lf", 8, F32), ("lo", 8, U16),
+    ("rr", NC + 2, BF), ("zt", NC, BF), ("cm", 4, F32), ("oa", K, F32), ("kw", 4, U16), ("a4", K, F32), ("ao", 10, U16),
+    ("ba", K, F32), ("bh", K, F32), ("brow", K, F32), ("sn", 4, F32), ("fo", 20, U16), ("lf", 8, F32), ("lo", 8, U16),
     ("fc", 64, BF), ("fs", 64, BF), ("fl", 64, BF), ("val", 160, BF), ("cv", K, F32),
     ("tf0", 16 * W, BF), ("tf1", 16 * W, BF), ("tm0", 16 * W, BF), ("tm1", 16 * W, BF), ("ff", 17 * W, BF), ("fm", 17 * W, BF),
     ("l4", K, F32), ("cl", K, F32), ("pm", 56, F32), ("on", K, F32),
@@ -117,12 +117,15 @@ def rank_program(g, core, T, topo):
     def dma(q, o, a, writes, reads):
         op(q, lambda: eng[q].dma_start(o, a), writes, reads, kind="d", n=16)
 
-    def send(t, land, src, sem, codes=False, behind=()):
+    def turn(i):
+        return (None, ("turn", i, i + 1))
+
+    def send(t, land, src, sem, codes=False, first=(), behind=()):
         dst = T.cores[rank ^ (1 << t)]
         rid, pid = topo.addr(dst)[:2]
         m = topo.mask(core, dst)
         o, a = (land[0].bitcast(dt.uint8), src[0].bitcast(dt.uint8)) if codes else (land[0], src[0])
-        op("g", lambda s: g.remote_dma(o, a, T.sem[sem], s, pid, rid, m), list(behind), [src], kind="r", n=len(topo.engines(core, dst)))
+        op("g", lambda s: g.remote_dma(o, a, T.sem[sem], s, pid, rid, m), list(behind), [src] + list(first), kind="r", n=len(topo.engines(core, dst)))
 
     def arrive(t, sem, lands, calls):
         src = T.cores[rank ^ (1 << t)]
@@ -251,6 +254,7 @@ def rank_program(g, core, T, topo):
         places1(0, 4)
         twice1(7, 1)
         chosen = lambda k, z: (V("sel", 16 * k, 16 * z), IND(V("flg"), V("rko", k, z)))
+        slot()
         places1(4, 6)
         places1(6, 8, True)
         act(*chosen(4, 6), F.Copy)
@@ -267,25 +271,31 @@ def rank_program(g, core, T, topo):
     iota(V("iot"), [[1, NC]])
     ms(V("one"), 1.0)
     op("g", lambda: g.affine_select(T.eb[:], T.one[:, 0:516], [[-1, 516]], A.is_equal, 0.0, 3, 4), [V("eb")], [V("one")])
+    gfill("fs", 0, 64, 1)
+    gfill("fc", 0, 64, BIG)
+    gfill("flg", 0, K, -STEP)
+    gfill("flg", K, 128, 0)
+    iota(V("zt", 0, K), [[1, K]], int(-STEP))
+    iota(V("zt", K, NC), [[1, NC - K]], K)
+    gfill("ff", 0, W, 0)
+    gfill("fm", 0, W, 0)
     iota(V("c4"), [[0, 96], [1, 4]])
     zero = lambda name, k: act(V(name, 512 * k, 512 * k + 512), V("one", 0, 512), F.Copy, scale=0.0)
     zero("tf0", 0)
     zero("tf0", 1)
     ms(V("rs3"), 0.0)
     ts(V("pi", 1, 2), V("pi", 0, 1), 15, A.bitwise_and)
-    ms(V("fs"), 1.0)
-    ms(V("fc"), BIG)
-    ms(V("rs3", 0, M, 3), -1e29)
     cp(V("uo"), V("i16"))
+    ms(V("rs3", 0, M, 3), -1e29)
     cp(col(0), V("pi", 1, 2))
     ts(V("pj", 0, 1), V("pi", 1, 2), 2, A.arith_shift_right)
     ts(V("pj", 1, 2), V("pi", 1, 2), 3, A.bitwise_and)
-    ts(V("sg"), V("c16"), 0.0, A.is_equal, -3e29, A.mult)
-    ts(V("dm"), V("c16"), col(0), A.not_equal, -1e29, A.mult)
-    quant(V("uq"), V("us"), V("ub"))
     ts(V("col", 1, 4), V("i16", 0, 3), col(0), A.add, 0.5, A.add)
-    ts(col(7), col(0), -STEP, A.mult, 16.0 * STEP, A.add)
     ts(col(11), col(0), -1.0, A.add)
+    ts(V("sg"), V("c16"), 0.0, A.is_equal, -3e29, A.mult)
+    quant(V("uq"), V("us"), V("ub"))
+    ts(V("dm"), V("c16"), col(0), A.not_equal, -1e29, A.mult)
+    ts(col(7), col(0), -STEP, A.mult, 16.0 * STEP, A.add)
     op("v", lambda: g.vector.tensor_copy(T.up[:, 0:128].bitcast(dt.uint32), T.uq[:, 0:128].bitcast(dt.uint32).indirect(T.uo[:, 0:8])),
        [V("up")], [V("uq"), V("uo")])
     op("a", lambda: g.scalar.activation(T.ups[:, 0:128], T.us[:, 0:128].indirect(T.uo[:, 0:8]), F.Copy), [V("ups")], [V("us"), V("uo")])
@@ -297,25 +307,21 @@ def rank_program(g, core, T, topo):
         lambda: (ts(V("pj", 12, 15), V("col", 1, 4), -0.5, A.add, 1.0 / 3.0, A.mult),
                  cp(V("col", 4, 6), V("pj", 0, 2)),
                  ms(V("val"), BIG)),
-        lambda: ts(V("flg"), V("iot"), float(K), A.is_lt, -STEP, A.mult),
         lambda: (ms(V("fs", 0, 64, 4), 0.0), ms(V("fs", 3, 64, 4), -BIG), ts(col(6), col(5), 4.0 * H, A.add)),
         lambda: (ts(V("col", 8, 11), V("pj", 8, 11), float(W), A.mult, 48.0, A.add),
                  ts(V("col", 12, 15), V("pj", 12, 15), float(-W), A.mult, 16.0 * W + 48.0, A.add)),
         lambda: [ts(V("col", 20 + i, 26, 2), V("pj", 4, 7), float(W), A.mult, 47.0 + i, A.add) for i in range(2)],
         lambda: [ts(V("col", 26 + i, 32, 2), V("pj", 4, 7), float(-W), A.mult, 5.0 * W + 47.0 + i, A.add) for i in range(2)],
-        lambda: (ms(V("ff", 0, W), 0.0), ms(V("fm", 0, W), 0.0)),
+        lambda: (ts(V("col", 16, 18), V("col", 1, 3), 0.5, A.add, STEP, A.mult), ms(V("rr", 0, NC + 2, NC + 1), 0.0)),
         lambda: [ms(V("cv", k, K, 3), c) for k, c in enumerate((2048.0, -BIG, 0.0))],
         lambda: (ms(V("val", 16, 64, 3), -BIG), ms(V("val", 18, 64, 3), 0.0)),
         lambda: (ms(V("val", 96, NC, 3), 0.0), ms(V("val", 98, NC, 3), -BIG)),
-        lambda: ms(V("pa0", 0, 400), 1024.0),
-        lambda: ms(V("pa0", 400, 800), 0.0),
-        lambda: ms(V("pb0"), 4.0),
         lambda: ts(V("dw"), V("c4"), col(4), A.is_equal, 4096.0, A.mult),
     ] + [(lambda b: lambda: quant(V("eq", 128 * b, 128 * b + 128), V("es", 128 * b, 128 * b + 128), V("eb", 3 - b, 515 - b)))(b) for b in range(4)]
-    slot()
     quant_state(0, 0, M)
     scores(0, 0)
-    slot()
+    slot(2)
+    spare.pop()()
     top(0)
     quant_state(0, M, C)
     send(0, V("ls0"), V("s0"), "rt0")
@@ -331,18 +337,20 @@ def rank_program(g, core, T, topo):
         tq, hb, lh, xs, lt = "t%d" % t, "h%d" % t, "lh%d" % t, "x%d" % t, "lt%d" % t
         tf, tm, pa, pb = "tf%d" % t, "tm%d" % t, "pa%d" % t, "pb%d" % t
         rank_triples()
+        if t + 1 == R:
+            spare.append(lambda: quant(V("vq"), V("vs"), V("vb")))
         slot()
         invert("co", 128)
-        slot()
+        for a, e in ((2, 3), (0, 2)):
+            for i in range(3):
+                tt(V("ma", K * a + i, K * e, 3), IND(V("psb", 128 * i, 128 * i + 128), V("co", a, e)), V("dm", i, K * (e - a), 3), A.add)
         for i in range(3):
-            tt(V("ma", i, NC, 3), IND(V("psb", 128 * i, 128 * i + 128), V("co", 0, 3)), V("dm", i, NC, 3), A.add)
             act(V("cand", i, NC, 3), IND(V("psb", 128 * i, 128 * i + 128), V("co", 0, 3)), F.Copy)
-        for i in range(3):
+        for i in range(2):
             act(V("crow", i, NC, 3), IND(V("iot"), V("co", 0, 3)), F.Copy, bias=float(i - H), scale=3.0)
-        slot()
-        hold("mh", "ma", 64, NC)
-        hold("mh", "ma", 0, 64)
-        slot()
+        hold("mh", "ma", 96, NC)
+        ts(V("crow", 2, NC, 3), IND(V("iot"), V("co", 0, 3)), 3.0, A.mult, 2.0 - H, A.add)
+        hold("mh", "ma", 0, 96)
         for k in (8, 7, 6, 5):
             low2(k, True)
         fix2(6, 9)
@@ -362,93 +370,99 @@ def rank_program(g, core, T, topo):
             high2(k)
         for k in range(3):
             twice2(k, k)
+        slot()
         places2(3, 9)
         places2(0, 3, True)
         slot()
         scat(V(hb), V("rko", 0, 9), V("crow"))
-        send(t, V(lh), V(hb, 0, K), "rh%d" % t)
-        send(t, V(lt, M, C), V(tq, M, C), "rt%d" % t, codes=True, behind=[V(hb, 0, K)])
+        send(t, V(lh), V(hb, 0, K), "rh%d" % t, first=[turn(2 * t)])
+        send(t, V(lt, M, C), V(tq, M, C), "rt%d" % t, codes=True, first=[turn(2 * t + 1)], behind=[turn(2 * t)])
         if t + 1 < R:
             gfill("tf1", 0, 16 * W, 0)
             gfill("tm1", 0, 16 * W, 0)
-            gfill("pa1", 0, 400, 1024)
-            gfill("pa1", 400, 800, 0)
-            gfill("pb1", 0, 400, 4)
-        act(V("sel"), IND(V("flg"), V("rko", 0, 9)), F.Copy)
-        act(V("rr"), IND(V("iot"), V("rko", 0, 9)), F.Copy)
-        invert("eo", NC)
+            for name, a, c in PLAIN:
+                gfill(name + "1", a, a + 400, c)
+        act(V("sel"), IND(V("zt"), V("rko", 0, 9)), F.Copy)
+        act(V("rr", 1, NC + 1), IND(V("iot"), V("rko", 0, 9)), F.Copy)
         slot()
-        tt(V("oa"), IND(V("rr"), V("eo", 0, 3)), V("dm", 0, K), A.add)
-        act(V("a4"), IND(V("crow"), V("eo", 0, 3)), F.Copy, bias=2048.0 + 4.0 * (H + 1), scale=4.0)
+        for k in range(2):
+            scan(V("cn", NC * k, NC * k + 112 + 16 * k), V("sel", 0, 112 + 16 * k), V("rr", 0, 112 + 16 * k), col(16 + k), A.add, A.subtract)
+        scan(V("cn", 3 * NC - 1, 2 * NC + 31, -1), V("sel", NC - 1, 31, -1), V("rr", NC + 1, 33, -1), col(7), A.add, A.subtract)
+        for k in range(3):
+            reduce(V("cm", k, k + 1), V("cn", (NC + 16) * k, (NC + 16) * k + 112), A.min, True)
         slot()
-        hold("oh", "oa", 0, K)
-        slot()
-        cp(V("kw", 0, 3), V("oh", 15, K, 16))
+        cp(V("kw", 0, 3), V("cm", 0, 3))
         slot(2)
         arrive(t, "rh%d" % t, [V(lh)], 1)
         if t == 0:
-            dma("s", T.wq[:].bitcast(dt.uint8), T.wc[:], [V("wq"), V(tq, M, C)], [])
+            dma("s", T.wq[:].bitcast(dt.uint8), T.wc[:], [V("wq"), turn(1)], [])
             dma("s", T.wsp[:], T.ws[:], [V("wsp")], [])
         act(V("brow"), IND(V(lh), V("kw", 0, 3)), F.Copy)
         tt(V("ba"), IND(V(lh), V("kw", 0, 3)), V("dm", 0, K), A.add)
-        slot()
+        tt(V("ma", 0, K), IND(V(hb, 0, K), V("kw", 0, 3)), V("dm", 0, K), A.add)
         hold("bh", "ba", 0, K)
         count(lambda k: V("sn", k, k + 1), V(lh), K, lambda k: V("bh", 16 * k + 15, 16 * k + 16), (0, 2, 1))
         for k in range(3):
             tt(V("fc", k, 64, 4), V("brow", k, K, 3), V("brow", (k + 1) % 3, K, 3), A.is_gt)
+        hold("mh", "ma", 0, K)
         slot(len(spare))
         scan(V("fl"), V("fs"), V("fc"), 0.0, A.mult, A.add)
 
-        def slots(m, c, out, later=0.0):
+        def slots(m, c, out):
             i = 20 + 6 * m + 2 * c
-            ts(out, V("col", i, i + 2), V("sn", c, c + 1), A.subtract if m else A.add, later, A.add)
+            ts(out, V("col", i, i + 2), V("sn", c, c + 1), A.subtract if m else A.add)
 
-        def table(name, a, e, i, v):
-            scat(V(name, W * a, W * e), V("fo", i, i + 2), V("val", v, v + 32))
+        def table(name, a, i, v, n=1):
+            scat(V(name, W * a, W * a + 6 * W), V("fo", i, i + n), V("val", v, v + 16 * n))
 
         slots(0, 0, V("fo", 1, -1, -1))
-        slots(1, 2, V("fo", 10, 12))
+        slots(1, 2, V("fo", 2, 4))
         for a in (16, 96):
             cp(V("val", a + 1, a + K, 3), V("fl", 3, 64, 4))
-        slots(0, 1, V("fo", 2, 6, 2))
-        slots(1, 1, V("fo", 7, 10, 2))
-        table(tf, 0, 6, 0, 0)
-        table(tm, 0, 6, 10, 128)
-        slots(0, 2, V("fo", 3, 6, 2), 5.0 * W)
+        slots(0, 1, V("fo", 4, 8, 2))
+        slots(1, 1, V("fo", 8, 12, 2))
+        table(tf, 0, 0, 0, 2)
+        table(tm, 0, 2, 128, 2)
+        slots(0, 2, V("fo", 12, 16, 2))
         act(V("bz"), V("brow"), F.Copy, bias=2048.0, scale=4.0)
+        act(V("a4"), IND(V(hb, 0, K), V("kw", 0, 3)), F.Copy, bias=2048.0 + 4.0 * (H + 1), scale=4.0)
         for h in range(2):
             act(V("xh", 4 * H * h, 4 * H * h + 4 * H), V(xs, 4 * H * h, 4 * H * h + 4 * H), F.Copy, scale=0.5)
         arrive(t, "rt%d" % t, [V(lt), V("ls%d" % t)], 3)
         for b in range(4):
             mm(V("ps%d" % b, 0, C), V("eq", 128 * b, 128 * b + 128), V("es", 128 * b, 128 * b + 128), V(lt), V("ls%d" % t))
             act(V("yh", b, 4 * C, 4), V("ps%d" % b, 0, C), F.Copy, scale=0.5)
+        if t == 0:
+            for name, a, c in PLAIN:
+                act(V(name + "0", a, a + 400), V("one", 0, 400), F.Copy, scale=float(c))
 
         def where(k):
             ts(V("ao", 3 * k, 3 * k + 3), V("mh", 15, K, 16), H + 400.0 * (k % 2), A.add)
 
         between = {
-            0: lambda: table(tf, 5, 16, 2, 32),
-            1: lambda: table(tm, 5, 16, 6, 96),
-            2: lambda: table(tf, 5, 16, 4, 64),
-            3: lambda: table(tm, 5, 16, 8, 64),
-            4: lambda: tt(V("ma", 0, K), IND(V("crow"), V("eo", 0, 3)), V("dm", 0, K), A.add),
-            5: lambda: (tt(V("lf", 0, 3), V("col", 8, 11), V("sn", 0, 3), A.add), tt(V("lf", 3, 6), V("col", 12, 15), V("sn", 0, 3), A.subtract)),
-            6: lambda: (hold("mh", "ma", 0, K), tt(V("d1"), V("bz"), V("a4"), A.subtract)),
-            7: lambda: (cp(V("lo", 0, 3), V("lf", 0, 3)), cp(V("lo", 4, 5), V("lf", 3, 4))),
-            8: lambda: (cp(V("lo", 6, 8), V("lf", 4, 6)), ts(V("dl"), V("d1"), 1.0 / 2048.0, A.mult)),
-            9: lambda: (where(0), where(1)),
-            10: lambda: (where(2), quant(V("vq"), V("vs"), V("vb")) if t + 1 == R else None),
+            0: lambda: table(tf, 5, 4, 32),
+            1: lambda: table(tm, 5, 8, 112),
+            2: lambda: table(tf, 5, 6, 64),
+            3: lambda: table(tm, 5, 10, 64),
+            4: lambda: table(tf, 10, 12, 48),
+            5: lambda: table(tm, 10, 16, 96),
+            6: lambda: table(tf, 10, 14, 64),
+            7: lambda: table(tm, 10, 18, 64),
+            8: lambda: (tt(V("lf", 0, 3), V("col", 8, 11), V("sn", 0, 3), A.add), tt(V("lf", 3, 6), V("col", 12, 15), V("sn", 0, 3), A.subtract)),
+            9: lambda: (cp(V("lo", 0, 3), V("lf", 0, 3)), cp(V("lo", 6, 8), V("lf", 4, 6))),
+            10: lambda: (tt(V("d1"), V("bz"), V("a4"), A.subtract), act(V("dl"), V("d1"), F.Copy, scale=1.0 / 2048.0)),
             11: lambda: ts(V("l4", 0, 32), IND(V("ff", 0, 12 * W), V("lo", 0, 2)), 1.0 + 2048.0 / BIG, A.mult),
             12: lambda: tt(V("oa", 16, K), IND(V("fm", 0, 12 * W), V("lo", 6, 8)), V("cv", 16, K), A.add),
-            13: lambda: tt(V("oa", 0, 16), V("l4", 0, 16), V("cv", 0, 16), A.add),
-            14: lambda: tt(V("cl", 16, 32), V("l4", 16, 32), V("oa", 16, 32), A.add),
+            13: lambda: (tt(V("oa", 0, 16), V("l4", 0, 16), V("cv", 0, 16), A.add), cp(V("lo", 4, 5), V("lf", 3, 4))),
+            14: lambda: (tt(V("cl", 16, 32), V("l4", 16, 32), V("oa", 16, 32), A.add), where(0)),
+            15: lambda: (where(1), where(2)),
         }
         for s in range(16):
             a = W * s
             for f, tab in (("ff", tf), ("fm", tm)):
                 scan(V(f, a + W, a + 2 * W), V(f, a, a + W), V(tab, a, a + W), 0.0, A.max, A.add)
                 if s == 0 and tab == tf:
-                    slots(1, 0, V("fo", 6, 10, 2), 5.0 * W)
+                    slots(1, 0, V("fo", 16, 20, 2))
             if s in between:
                 between[s]()
         ts(V("l4", 32, K), IND(V("ff"), V("lo", 2, 3)), 1.0 + 2048.0 / BIG, A.mult)
@@ -477,10 +491,13 @@ def rank_program(g, core, T, topo):
         if t == 0:
             dma("s", T.vb[:], T.v[:], [V("vb")], [])
         xn, tn, sn = "x%d" % (t + 1), "t%d" % (t + 1), "s%d" % (t + 1)
+        for a, e in ((H, 256), (256, C)):
+            act(V("yg", 4 * (a - H), 4 * (e - H)), IND(V("yh"), V("qo", a // 4, e // 4)), F.Copy)
         mix(0, 128)
-        mix(128, 256)
+        mix(128, H)
         layer(0)
-        mix(256, C)
+        for a, e in ((H, 256), (256, C)):
+            tt(V("gg", 4 * a, 4 * e), V("yg", 4 * (a - H), 4 * (e - H)), V("xh", 4 * a, 4 * e), A.add)
         layer(1)
         layer_sum(xn, 0, 0, 128)
         layer(2)

from concourse.mybir import dt, AxisListType, AluOpType as A, ActivationFunctionType as F

C, K, R = 384, 48, 2
W = 2 * K
H = C // 2
M = 240
PIECE = ((0, M), (M, C))
NC = 3 * K
PLAIN = (("pa", 0, 1024), ("pa", 400, 0), ("pb", 0, 4))
STEP = 256.0
BIG = 131072.0
F32, BF, U16, I32, Q4, U8 = "float32", "bfloat16", "uint16", "int32", "float8_e4m3fn_x4", "uint8"
SCRATCH = {}
for _n, _w, _d in [
    ("x0", 4 * C, BF), ("x1", 4 * C, BF), ("x2", 4 * C, BF), ("xh", 4 * C, BF), ("gg", 4 * C, BF), ("yh", 4 * C, BF), ("yg", 4 * H, BF),
    ("rl", 4 * C, F32), ("ub", 512, BF), ("vb", 512, BF), ("eb", 516, BF), ("one", 520, BF),
    ("t0", C, Q4), ("t1", C, Q4), ("t2", C, Q4), ("s0", C, U8), ("s1", C, U8), ("s2", C, U8),
    ("lt0", C, Q4), ("lt1", C, Q4), ("ls0", C, U8), ("ls1", C, U8), ("zq", C, Q4), ("zs", C, U8),
    ("uq", 128, Q4), ("us", 128, U8), ("up", 128, Q4), ("ups", 128, U8), ("vq", 128, Q4), ("vs", 128, U8),
    ("wq", 512, Q4), ("wsp", 512, U8), ("eq", 512, Q4), ("es", 512, U8),
    ("iot", NC, F32), ("c16", NC, F32), ("c4", C, BF), ("pi", 4, I32), ("pj", 16, I32), ("col", 32, F32), ("i16", 8, F32),
    ("dm", NC, F32), ("sg", NC, F32), ("rs3", M, BF), ("dw", C, BF), ("flg", 128, BF), ("uo", 8, U16),
    ("psb", C, F32), ("m3", C, F32), ("ma", NC, F32), ("mh", NC, F32), ("junk", 480, BF),
    ("rk", 10, F32), ("rko", 10, U16), ("sel", NC, BF), ("pos", NC, BF), ("cn", 3 * NC, BF), ("co", 4, U16),
    ("cand", NC, F32), ("crow", NC, BF), ("h0", NC, BF), ("h1", NC, BF), ("lh0", K, BF), ("lh1", K, BF),
    ("rr", NC + 2, BF), ("zt", NC, BF), ("cm", 4, F32), ("oa", K, F32), ("kw", 4, U16), ("a4", K, F32), ("ao", 10, U16),
    ("ba", K, F32), ("bh", K, F32), ("brow", K, F32), ("sn", 4, F32), ("fo", 20, U16), ("lf", 8, F32), ("lo", 8, U16),
    ("fc", 64, BF), ("fs", 64, BF), ("fl", 64, BF), ("val", 160, BF), ("cv", K, F32),
    ("tf0", 16 * W, BF), ("tf1", 16 * W, BF), ("tm0", 16 * W, BF), ("tm1", 16 * W, BF), ("ff", 17 * W, BF), ("fm", 17 * W, BF),
    ("l4", K, F32), ("cl", K, F32), ("pm", 56, F32), ("on", K, F32),
    ("bz", K, F32), ("dl", K, F32), ("nn", K, F32), ("od", K, F32), ("d1", K, F32), ("pv", NC, BF),
    ("pa0", 800, BF), ("pa1", 800, BF), ("pb0", 400, BF), ("pb1", 400, BF),
    ("cap", C, BF), ("qf", H, BF), ("qr", C, BF), ("qh", C, BF), ("qo", 96, U16),
    ("oq0", C, F32), ("oq1", C, F32), ("ysb", C, F32),
]:
    SCRATCH[_n] = ("sbuf", [128, _w], _d)
SCRATCH["tb8"] = ("sbuf", [128, 8, 144], BF)
SCRATCH["tb9"] = ("sbuf", [128, 9, 160], BF)
for _i in range(8):
    SCRATCH["ps%d" % _i] = ("psum", [128, 512], F32)
SEMAPHORES = ["v", "a", "p", "g"] + ["d%d" % _i for _i in range(40)] + ["rt0", "rt1", "rh0", "rh1"]


def rank_program(g, core, T, topo):
    rank = T.rank_of(core)
    if rank is None:
        return
    ops = []

    def V(name, a=0, b=None, s=1):
        b = T[name].shape[1] if b is None else b
        if s == 1:
            return (T[name][:, a:b], (name, a, b))
        if s > 1:
            return (T[name][:, a:b:s], (name, a, b, s))
        return (T[name][:, a:(b if b >= 0 else None):s], (name, b + 1, a + 1))

    def IND(win, off):
        return (win[0].indirect(off[0]), win[1], off[1])

    def regs(vs):
        return [r for x in vs if isinstance(x, tuple) for r in x[1:]]

    def ap(x):
        return x[0] if isinstance(x, tuple) else x

    def op(q, fn, writes, reads, kind="c", n=1, arrive=None):
        ops.append({"q": q, "fn": fn, "w": regs(writes), "r": regs(reads), "kind": kind, "n": n, "arrive": arrive})

    def tt(o, a, b, f):
        op("v", lambda: g.vector.tensor_tensor(o[0], a[0], b[0], f), [o], [a, b])

    def ts(o, a, s1, f0, s2=None, f1=None):
        if f1 is None:
            op("v", lambda: g.vector.tensor_scalar(o[0], a[0], ap(s1), None, f0), [o], [a, s1])
        else:
            op("v", lambda: g.vector.tensor_scalar(o[0], a[0], ap(s1), ap(s2), f0, f1), [o], [a, s1, s2])

    def cp(o, a):
        op("v", lambda: g.vector.tensor_copy(o[0], a[0]), [o], [a])

    def scat(win, off, a):
        op("v", lambda: g.vector.tensor_copy(win[0].indirect(off[0]), a[0]), [win], [a, off])

    def scan(o, d0, d1, init, f0, f1):
        op("v", lambda: g.vector.tensor_tensor_scan(o[0], d0[0], d1[0], ap(init), f0, f1), [o], [d0, d1, init])

    def reduce(o, a, f, size=False):
        op("v", lambda: g.vector.tensor_reduce(o[0], a[0], AxisListType.X, f, apply_absolute_value=size), [o], [a])

    def ms(o, c):
        op("v", lambda: g.vector.memset(o[0], c), [o], [])

    def act(o, a, f, bias=0.0, scale=1.0, acc=None):
        if acc is None:
            op("a", lambda: g.scalar.activation(o[0], a[0], f, bias=ap(bias), scale=scale), [o], [a, bias])
        else:
            op("a", lambda: g.scalar.activation(o[0], a[0], f, bias=ap(bias), scale=scale, accum_out=acc[0]), [o, acc], [a, bias])

    def quant(q, s, a):
        op("v", lambda: g.vector.quantize_mx(q[0], s[0], a[0]), [q, s], [a])

    def mm(o, wq, ws, xq, xs):
        op("p", lambda: g.tensor.matmul_mx(o[0], wq[0], ws[0], xq[0], xs[0], True, True), [o], [wq, ws, xq, xs])

    def iota(o, pat, base=0, cm=0):
        if SCRATCH[o[1][0]][2] == I32:
            op("g", lambda: g.iota(o[0], pat, base, cm), [o], [])
        else:
            op("g", lambda: g.iota(o[0], pat, base, cm, allow_small_or_imprecise_dtypes=True), [o], [])

    def gfill(name, a, b, c):
        iota(V(name, a, b), [[0, b - a]], int(c))

    eng = {"v": g.vector, "a": g.scalar, "p": g.tensor, "g": g, "s": g.sync}

    def dma(q, o, a, writes, reads):
        op(q, lambda: eng[q].dma_start(o, a), writes, reads, kind="d", n=16)

    def turn(i):
        return (None, ("turn", i, i + 1))

    def send(t, land, src, sem, codes=False, first=(), behind=()):
        dst = T.cores[rank ^ (1 << t)]
        rid, pid = topo.addr(dst)[:2]
        m = topo.mask(core, dst)
        o, a = (land[0].bitcast(dt.uint8), src[0].bitcast(dt.uint8)) if codes else (land[0], src[0])
        op("g", lambda s: g.remote_dma(o, a, T.sem[sem], s, pid, rid, m), list(behind), [src] + list(first), kind="r", n=len(topo.engines(core, dst)))

    def arrive(t, sem, lands, calls):
        src = T.cores[rank ^ (1 << t)]
        op(None, None, lands, [], kind="x", n=calls * len(topo.engines(src, core)), arrive=sem)

    def col(i):
        return V("col", i, i + 1)

    spare = []

    def slot(n=1):
        for _ in range(n):
            if spare:
                spare.pop(0)()

    def hold(h, a, i, j):
        scan(V(h, i, j), V("sg", 0, j - i), V(a, i, j), 0.0, A.add, A.max)

    def count(out, row, n, bias, ks, scale=-1.0):
        for k in ks:
            act(V("junk", NC * k, NC * k + n), row, F.Sign, bias=bias(k), scale=scale, acc=out(k))

    def invert(out, n):
        sel = V("sel", 0, n - 16)
        scan(V("pos", 0, n - 16), sel, sel, 0.0, A.add, A.min)
        scan(V("cn", n - 1, 31, -1), V("sel", n - 1, 31, -1), V("one", 0, n - 32), col(7), A.add, A.add)
        count(lambda k: V("cm", k, k + 1), V("pos", 0, n - 16), n - 16, lambda k: col(1 + k), (0, 1), 1.0 / STEP)
        slot()
        reduce(V("cm", 2, 3), V("cn", 32, n), A.min, True)
        slot()
        ts(V(out, 2, 3), V("cm", 2, 3), -1.0, A.mult, float(n), A.add)
        ts(V(out, 0, 2), V("cm", 0, 2), 0.5, A.mult, (n - 16) / 2.0, A.add)

    def ranker(name, a, s, n):
        row = lambda i, j: V(name, a + s * i, a + s * (j - 1) + 1, s)
        nb, w = n // 16, n + 16
        tb = "tb%d" % nb
        seg = lambda k, i, j: (T[tb][:, k, i:j], (tb, w * k + i, w * k + j))
        m = lambda k: V("mh", 16 * k + 15, 16 * k + 16)

        def low(k, scalar=False):
            if scalar:
                act(seg(k, 0, 16 * k + 16), row(0, 16 * k + 16), F.Sign, bias=m(k), scale=-1.0)
            else:
                ts(seg(k, 0, 16 * k + 16), row(0, 16 * k + 16), m(k), A.is_lt)

        def fix(k, z):
            tt((T[tb][:, k:z, n:w],) + tuple((tb, w * i + n, w * i + w) for i in range(k, z)), row(16 * k, 16 * z), V("mh", 16 * k, 16 * z), A.is_equal)

        def high(k):
            ts(seg(k, 16 * k + 16, n), row(16 * k + 16, n), m(k), A.is_le)

        def total(k):
            act(seg(k, 0, w), seg(k, 0, w), F.Relu, acc=V("rk", k, k + 1))

        def twice(k, i):
            scan(V("junk", w * i, w * i + w), seg(k, 0, w), seg(k, 0, w), 0.0, A.add, A.add)

        def places(k, z, vector=False):
            if vector:
                ts(V("rko", k, z), V("junk", w - 1, w * (z - k), w), -0.5, A.mult, float(n), A.add)
            else:
                ts(V("rko", k, z), V("rk", k, z), -1.0, A.mult, float(n), A.add)
        return low, fix, high, total, twice, places

    def quant_state(t, a, e):
        quant(V("t%d" % t, a, e), V("s%d" % t, a, e), V("x%d" % t, 4 * a, 4 * e))

    def scores(t, h):
        a, e = PIECE[h]
        for i in (2 * h, 2 * h + 1):
            mm(V("ps%d" % i, 0, e - a), V("up"), V("ups"), V("t%d" % t, a, e), V("s%d" % t, a, e))

    def top(h):
        a, e = PIECE[h]
        scan(V("m3", a, e), V("rs3", 0, e - a), V("ps%d" % (2 * h), 0, e - a), 0.0, A.add, A.max)

    def planes(h):
        a, e = PIECE[h]
        for i in range(3):
            act(V("psb", 128 * i + a // 3, 128 * i + e // 3), V("ps%d" % (2 * h + 1), i, e - a, 3), F.Copy)

    def mask(h):
        a, e = PIECE[h]
        tt(V("ma", a // 3, e // 3), V("m3", a + 2, e, 3), V("dm", 0, (e - a) // 3), A.add)

    def layer_sum(xn, b, a, e):
        tt(V(xn, 4 * a + b, 4 * e, 4), V("gg", 4 * a + b, 4 * e, 4), V("rl", 4 * a + b, 4 * e, 4), A.add)

    def mix(a, e):
        tt(V("gg", 4 * a, 4 * e), IND(V("yh"), V("qo", a // 4, e // 4)), V("xh", 4 * a, 4 * e), A.add)

    def layer(h):
        a, e = 128 * h, 128 * h + 128
        quant(V("zq", a, e), V("zs", a, e), V("gg", 4 * a, 4 * e))
        for b in range(4):
            ps = V("ps%d" % (4 * (h % 2) + b), 0, e - a)
            mm(ps, V("wq", 128 * b, 128 * b + 128), V("wsp", 128 * b, 128 * b + 128), V("zq", a, e), V("zs", a, e))
            act(V("rl", 4 * a + b, 4 * e, 4), ps, F.Relu, scale=0.015625)

    low1, fix1, high1, total1, twice1, places1 = ranker("m3", 2, 3, 128)
    low2, fix2, high2, total2, twice2, places2 = ranker("cand", 0, 1, NC)

    def rank_triples():
        for k in (2, 3, 4):
            low1(k, True)
        top(1)
        low1(0)
        fix1(0, 2)
        low1(1)
        mask(1)
        for k in range(5):
            high1(k)
            if k == 1:
                fix1(2, 5)
                hold("mh", "ma", M // 3, 128)
            total1(k)
        fix1(5, 8)
        low1(5)
        high1(5)
        total1(5)
        low1(6)
        high1(6)
        low1(7)
        twice1(6, 0)
        places1(0, 4)
        twice1(7, 1)
        chosen = lambda k, z: (V("sel", 16 * k, 16 * z), IND(V("flg"), V("rko", k, z)))
        slot()
        places1(4, 6)
        places1(6, 8, True)
        act(*chosen(4, 6), F.Copy)
        planes(1)
        cp(*chosen(0, 4))
        cp(*chosen(6, 8))

    dma("s", T.ub[:], T.u[:], [V("ub")], [])
    dma("s", T.x0[:, 0:4 * M], T.x[:, 0:4 * M], [V("x0", 0, 4 * M)], [])
    dma("s", T.x0[:, 4 * M:4 * C], T.x[:, 4 * M:4 * C], [V("x0", 4 * M, 4 * C)], [])
    iota(V("pi", 0, 1), [[0, 1]], 0, 1)
    iota(V("i16"), [[16, 8]])
    iota(V("c16"), [[0, 9], [1, 16]])
    iota(V("iot"), [[1, NC]])
    ms(V("one"), 1.0)
    op("g", lambda: g.affine_select(T.eb[:], T.one[:, 0:516], [[-1, 516]], A.is_equal, 0.0, 3, 4), [V("eb")], [V("one")])
    gfill("fs", 0, 64, 1)
    gfill("fc", 0, 64, BIG)
    gfill("flg", 0, K, -STEP)
    gfill("flg", K, 128, 0)
    iota(V("zt", 0, K), [[1, K]], int(-STEP))
    iota(V("zt", K, NC), [[1, NC - K]], K)
    gfill("ff", 0, W, 0)
    gfill("fm", 0, W, 0)
    iota(V("c4"), [[0, 96], [1, 4]])
    zero = lambda name, k: act(V(name, 512 * k, 512 * k + 512), V("one", 0, 512), F.Copy, scale=0.0)
    zero("tf0", 0)
    zero("tf0", 1)
    ms(V("rs3"), 0.0)
    ts(V("pi", 1, 2), V("pi", 0, 1), 15, A.bitwise_and)
    cp(V("uo"), V("i16"))
    ms(V("rs3", 0, M, 3), -1e29)
    cp(col(0), V("pi", 1, 2))
    ts(V("pj", 0, 1), V("pi", 1, 2), 2, A.arith_shift_right)
    ts(V("pj", 1, 2), V("pi", 1, 2), 3, A.bitwise_and)
    ts(V("col", 1, 4), V("i16", 0, 3), col(0), A.add, 0.5, A.add)
    ts(col(11), col(0), -1.0, A.add)
    ts(V("sg"), V("c16"), 0.0, A.is_equal, -3e29, A.mult)
    quant(V("uq"), V("us"), V("ub"))
    ts(V("dm"), V("c16"), col(0), A.not_equal, -1e29, A.mult)
    ts(col(7), col(0), -STEP, A.mult, 16.0 * STEP, A.add)
    op("v", lambda: g.vector.tensor_copy(T.up[:, 0:128].bitcast(dt.uint32), T.uq[:, 0:128].bitcast(dt.uint32).indirect(T.uo[:, 0:8])),
       [V("up")], [V("uq"), V("uo")])
    op("a", lambda: g.scalar.activation(T.ups[:, 0:128], T.us[:, 0:128].indirect(T.uo[:, 0:8]), F.Copy), [V("ups")], [V("us"), V("uo")])
    zero("tf0", 2)
    zero("tm0", 0)
    spare += [
        lambda: (ts(V("pj", 4, 7), V("iot", 0, 3), col(11), A.add, 1.0 / 3.0, A.mult),
                 ts(V("pj", 8, 11), V("col", 1, 4), 0.5, A.add, 1.0 / 3.0, A.mult)),
        lambda: (ts(V("pj", 12, 15), V("col", 1, 4), -0.5, A.add, 1.0 / 3.0, A.mult),
                 cp(V("col", 4, 6), V("pj", 0, 2)),
                 ms(V("val"), BIG)),
        lambda: (ms(V("fs", 0, 64, 4), 0.0), ms(V("fs", 3, 64, 4), -BIG), ts(col(6), col(5), 4.0 * H, A.add)),
        lambda: (ts(V("col", 8, 11), V("pj", 8, 11), float(W), A.mult, 48.0, A.add),
                 ts(V("col", 12, 15), V("pj", 12, 15), float(-W), A.mult, 16.0 * W + 48.0, A.add)),
        lambda: [ts(V("col", 20 + i, 26, 2), V("pj", 4, 7), float(W), A.mult, 47.0 + i, A.add) for i in range(2)],
        lambda: [ts(V("col", 26 + i, 32, 2), V("pj", 4, 7), float(-W), A.mult, 5.0 * W + 47.0 + i, A.add) for i in range(2)],
        lambda: (ts(V("col", 16, 18), V("col", 1, 3), 0.5, A.add, STEP, A.mult), ms(V("rr", 0, NC + 2, NC + 1), 0.0)),
        lambda: [ms(V("cv", k, K, 3), c) for k, c in enumerate((2048.0, -BIG, 0.0))],
        lambda: (ms(V("val", 16, 64, 3), -BIG), ms(V("val", 18, 64, 3), 0.0)),
        lambda: (ms(V("val", 96, NC, 3), 0.0), ms(V("val", 98, NC, 3), -BIG)),
        lambda: ts(V("dw"), V("c4"), col(4), A.is_equal, 4096.0, A.mult),
    ] + [(lambda b: lambda: quant(V("eq", 128 * b, 128 * b + 128), V("es", 128 * b, 128 * b + 128), V("eb", 3 - b, 515 - b)))(b) for b in range(4)]
    quant_state(0, 0, M)
    scores(0, 0)
    slot(2)
    spare.pop()()
    top(0)
    quant_state(0, M, C)
    send(0, V("ls0"), V("s0"), "rt0")
    send(0, V("lt0", 0, M), V("t0", 0, M), "rt0", codes=True)
    gfill("tm0", 512, 16 * W, 0)
    scores(0, 1)
    planes(0)
    mask(0)
    slot()
    hold("mh", "ma", 0, M // 3)

    for t in range(R):
        tq, hb, lh, xs, lt = "t%d" % t, "h%d" % t, "lh%d" % t, "x%d" % t, "lt%d" % t
        tf, tm, pa, pb = "tf%d" % t, "tm%d" % t, "pa%d" % t, "pb%d" % t
        rank_triples()
        if t + 1 == R:
            spare.append(lambda: quant(V("vq"), V("vs"), V("vb")))
        slot()
        invert("co", 128)
        for a, e in ((2, 3), (0, 2)):
            for i in range(3):
                tt(V("ma", K * a + i, K * e, 3), IND(V("psb", 128 * i, 128 * i + 128), V("co", a, e)), V("dm", i, K * (e - a), 3), A.add)
        for i in range(3):
            act(V("cand", i, NC, 3), IND(V("psb", 128 * i, 128 * i + 128), V("co", 0, 3)), F.Copy)
        for i in range(2):
            act(V("crow", i, NC, 3), IND(V("iot"), V("co", 0, 3)), F.Copy, bias=float(i - H), scale=3.0)
        hold("mh", "ma", 96, NC)
        ts(V("crow", 2, NC, 3), IND(V("iot"), V("co", 0, 3)), 3.0, A.mult, 2.0 - H, A.add)
        hold("mh", "ma", 0, 96)
        for k in (8, 7, 6, 5):
            low2(k, True)
        fix2(6, 9)
        high2(7)
        high2(6)
        fix2(3, 6)
        high2(5)
        for k in (8, 7, 6, 5):
            total2(k)
        for k in (4, 3):
            low2(k)
            high2(k)
            total2(k)
        fix2(0, 3)
        for k in range(3):
            low2(k)
            high2(k)
        for k in range(3):
            twice2(k, k)
        slot()
        places2(3, 9)
        places2(0, 3, True)
        slot()
        scat(V(hb), V("rko", 0, 9), V("crow"))
        send(t, V(lh), V(hb, 0, K), "rh%d" % t, first=[turn(2 * t)])
        send(t, V(lt, M, C), V(tq, M, C), "rt%d" % t, codes=True, first=[turn(2 * t + 1)], behind=[turn(2 * t)])
        if t + 1 < R:
            gfill("tf1", 0, 16 * W, 0)
            gfill("tm1", 0, 16 * W, 0)
            for name, a, c in PLAIN:
                gfill(name + "1", a, a + 400, c)
        act(V("sel"), IND(V("zt"), V("rko", 0, 9)), F.Copy)
        act(V("rr", 1, NC + 1), IND(V("iot"), V("rko", 0, 9)), F.Copy)
        slot()
        for k in range(2):
            scan(V("cn", NC * k, NC * k + 112 + 16 * k), V("sel", 0, 112 + 16 * k), V("rr", 0, 112 + 16 * k), col(16 + k), A.add, A.subtract)
        scan(V("cn", 3 * NC - 1, 2 * NC + 31, -1), V("sel", NC - 1, 31, -1), V("rr", NC + 1, 33, -1), col(7), A.add, A.subtract)
        for k in range(3):
            reduce(V("cm", k, k + 1), V("cn", (NC + 16) * k, (NC + 16) * k + 112), A.min, True)
        slot()
        cp(V("kw", 0, 3), V("cm", 0, 3))
        slot(2)
        arrive(t, "rh%d" % t, [V(lh)], 1)
        if t == 0:
            dma("s", T.wq[:].bitcast(dt.uint8), T.wc[:], [V("wq"), turn(1)], [])
            dma("s", T.wsp[:], T.ws[:], [V("wsp")], [])
        act(V("brow"), IND(V(lh), V("kw", 0, 3)), F.Copy)
        tt(V("ba"), IND(V(lh), V("kw", 0, 3)), V("dm", 0, K), A.add)
        tt(V("ma", 0, K), IND(V(hb, 0, K), V("kw", 0, 3)), V("dm", 0, K), A.add)
        hold("bh", "ba", 0, K)
        count(lambda k: V("sn", k, k + 1), V(lh), K, lambda k: V("bh", 16 * k + 15, 16 * k + 16), (0, 2, 1))
        for k in range(3):
            tt(V("fc", k, 64, 4), V("brow", k, K, 3), V("brow", (k + 1) % 3, K, 3), A.is_gt)
        hold("mh", "ma", 0, K)
        slot(len(spare))
        scan(V("fl"), V("fs"), V("fc"), 0.0, A.mult, A.add)

        def slots(m, c, out):
            i = 20 + 6 * m + 2 * c
            ts(out, V("col", i, i + 2), V("sn", c, c + 1), A.subtract if m else A.add)

        def table(name, a, i, v, n=1):
            scat(V(name, W * a, W * a + 6 * W), V("fo", i, i + n), V("val", v, v + 16 * n))

        slots(0, 0, V("fo", 1, -1, -1))
        slots(1, 2, V("fo", 2, 4))
        for a in (16, 96):
            cp(V("val", a + 1, a + K, 3), V("fl", 3, 64, 4))
        slots(0, 1, V("fo", 4, 8, 2))
        slots(1, 1, V("fo", 8, 12, 2))
        table(tf, 0, 0, 0, 2)
        table(tm, 0, 2, 128, 2)
        slots(0, 2, V("fo", 12, 16, 2))
        act(V("bz"), V("brow"), F.Copy, bias=2048.0, scale=4.0)
        act(V("a4"), IND(V(hb, 0, K), V("kw", 0, 3)), F.Copy, bias=2048.0 + 4.0 * (H + 1), scale=4.0)
        for h in range(2):
            act(V("xh", 4 * H * h, 4 * H * h + 4 * H), V(xs, 4 * H * h, 4 * H * h + 4 * H), F.Copy, scale=0.5)
        arrive(t, "rt%d" % t, [V(lt), V("ls%d" % t)], 3)
        for b in range(4):
            mm(V("ps%d" % b, 0, C), V("eq", 128 * b, 128 * b + 128), V("es", 128 * b, 128 * b + 128), V(lt), V("ls%d" % t))
            act(V("yh", b, 4 * C, 4), V("ps%d" % b, 0, C), F.Copy, scale=0.5)
        if t == 0:
            for name, a, c in PLAIN:
                act(V(name + "0", a, a + 400), V("one", 0, 400), F.Copy, scale=float(c))

        def where(k):
            ts(V("ao", 3 * k, 3 * k + 3), V("mh", 15, K, 16), H + 400.0 * (k % 2), A.add)

        between = {
            0: lambda: table(tf, 5, 4, 32),
            1: lambda: table(tm, 5, 8, 112),
            2: lambda: table(tf, 5, 6, 64),
            3: lambda: table(tm, 5, 10, 64),
            4: lambda: table(tf, 10, 12, 48),
            5: lambda: table(tm, 10, 16, 96),
            6: lambda: table(tf, 10, 14, 64),
            7: lambda: table(tm, 10, 18, 64),
            8: lambda: (tt(V("lf", 0, 3), V("col", 8, 11), V("sn", 0, 3), A.add), tt(V("lf", 3, 6), V("col", 12, 15), V("sn", 0, 3), A.subtract)),
            9: lambda: (cp(V("lo", 0, 3), V("lf", 0, 3)), cp(V("lo", 6, 8), V("lf", 4, 6))),
            10: lambda: (tt(V("d1"), V("bz"), V("a4"), A.subtract), act(V("dl"), V("d1"), F.Copy, scale=1.0 / 2048.0)),
            11: lambda: ts(V("l4", 0, 32), IND(V("ff", 0, 12 * W), V("lo", 0, 2)), 1.0 + 2048.0 / BIG, A.mult),
            12: lambda: tt(V("oa", 16, K), IND(V("fm", 0, 12 * W), V("lo", 6, 8)), V("cv", 16, K), A.add),
            13: lambda: (tt(V("oa", 0, 16), V("l4", 0, 16), V("cv", 0, 16), A.add), cp(V("lo", 4, 5), V("lf", 3, 4))),
            14: lambda: (tt(V("cl", 16, 32), V("l4", 16, 32), V("oa", 16, 32), A.add), where(0)),
            15: lambda: (where(1), where(2)),
        }
        for s in range(16):
            a = W * s
            for f, tab in (("ff", tf), ("fm", tm)):
                scan(V(f, a + W, a + 2 * W), V(f, a, a + W), V(tab, a, a + W), 0.0, A.max, A.add)
                if s == 0 and tab == tf:
                    slots(1, 0, V("fo", 16, 20, 2))
            if s in between:
                between[s]()
        ts(V("l4", 32, K), IND(V("ff"), V("lo", 2, 3)), 1.0 + 2048.0 / BIG, A.mult)
        tt(V("cl", 0, 16), IND(V("fm"), V("lo", 4, 5)), V("oa", 0, 16), A.add)
        cp(V("pm", 0, 1), V("ff", 17 * W - 1, 17 * W))
        tt(V("cl", 32, K), V("l4", 32, K), V("oa", 32, K), A.add)
        scan(V("pm", 1, K + 1), V("cl"), V("cl"), V("pm", 0, 1), A.max, A.max)
        tt(V("on"), V("pm", 1, K + 1), V("pm", 0, K), A.subtract)
        tt(V("pv", 0, K), V("bz"), V("on"), A.subtract)
        act(V("pv", K, 96), V("on"), F.Copy, scale=-1.0 / 512.0)
        act(V("nn"), V("on"), F.Copy, bias=1.0, scale=-1.0 / 2048.0)
        tt(V("od"), V("on"), V("dl"), A.mult)
        ts(V("pv", 96, NC), V("on"), 4.0, A.add)
        scat(V(pa), V("ao", 0, 6), V("pv", 0, 96))
        scan(V("d1", K - 1, -1, -1), V("nn", K - 1, -1, -1), V("od", K - 1, -1, -1), 0.0, A.mult, A.add)
        scat(V(pb), V("ao", 6, 9), V("pv", 96, NC))
        scan(V("cap", C - 1, -1, -1), V(pa, 400 + C, 400, -1), V(pa, C - 1, -1, -1), 4.0 * (C - 1 - H), A.add, A.min)
        for name, e in (("qf", H), ("qr", C)):
            scan(V(name, 0, e), V(pb, 0, e), V("cap", 0, e), V("d1", 0, 1), A.add, A.min)
        for name, a, e in (("qf", 0, H), ("qr", H, C)):
            scan(V("qh", a, e), V("dw", a, e), V(name, a, e), 0.0, A.add, A.min)
        for a, e in ((0, H), (H, C)):
            ts(V("qo", a // 4, e // 4), V("qh", a + 3, e, 4), col(6), A.add, col(5), A.max)
        act(V("oq%d" % t), V("qr"), F.Relu, bias=float(H), scale=0.25)
        dma("s", T.oq[:, C * t:C * t + C], T["oq%d" % t][0:128:16, :], [], [V("oq%d" % t)])
        if t == 0:
            dma("s", T.vb[:], T.v[:], [V("vb")], [])
        xn, tn, sn = "x%d" % (t + 1), "t%d" % (t + 1), "s%d" % (t + 1)
        for a, e in ((H, 256), (256, C)):
            act(V("yg", 4 * (a - H), 4 * (e - H)), IND(V("yh"), V("qo", a // 4, e // 4)), F.Copy)
        mix(0, 128)
        mix(128, H)
        layer(0)
        for a, e in ((H, 256), (256, C)):
            tt(V("gg", 4 * a, 4 * e), V("yg", 4 * (a - H), 4 * (e - H)), V("xh", 4 * a, 4 * e), A.add)
        layer(1)
        layer_sum(xn, 0, 0, 128)
        layer(2)
        for b in (1, 2, 3):
            layer_sum(xn, b, 0, 128)
        if t + 1 < R:
            for b in range(4):
                layer_sum(xn, b, 128, M)
            layer_sum(xn, 0, M, C)
            layer_sum(xn, 1, M, C - 32)
            quant_state(t + 1, 0, M)
            send(t + 1, V("lt%d" % (t + 1), 0, M), V(tn, 0, M), "rt%d" % (t + 1), codes=True)
            scores(t + 1, 0)
            layer_sum(xn, 1, C - 32, C)
            layer_sum(xn, 2, M, C)
            layer_sum(xn, 3, M, C)
            top(0)
            quant_state(t + 1, M, C)
            send(t + 1, V("ls%d" % (t + 1)), V(sn), "rt%d" % (t + 1))
            scores(t + 1, 1)
            planes(0)
            mask(0)
            hold("mh", "ma", 0, M // 3)
            continue
        for h in range(3):
            c0, c1 = 128 * h, 128 * h + 128
            for b in (1, 2, 3) if h else ():
                layer_sum(xn, b, c0, c1)
            if h < 2:
                layer_sum(xn, 0, c1, c1 + 128)
            quant_state(t + 1, c0, c1)
            ps = V("ps%d" % (4 + h), 0, 128)
            mm(ps, V("vq"), V("vs"), V(tn, c0, c1), V(sn, c0, c1))
            dma("s", T.oc[:, 4 * c0:4 * c1], T[tn][:, c0:c1].bitcast(dt.uint8), [], [V(tn, c0, c1)])
            if h < 2:
                act(V("ysb", c0, c1), ps, F.Copy)
            else:
                for k in range(4):
                    dma("a" if k % 2 else "s", T.osc[4 * k:4 * k + 4, :], T[sn][32 * k:32 * k + 4, :], [], [V(sn)])
                cp(V("ysb", c0, c1), ps)
            dma("a", T.y[:, c0:c1], T.ysb[:, c0:c1], [], [V("ysb", c0, c1)])

    emit(ops, eng, T)


def emit(ops, eng, T):
    def bank(x):
        return x[0].startswith("ps") and x[0][2:].isdigit()

    def apart(x, y):
        return len(x) > 3 and len(y) > 3 and x[3] == y[3] and (x[1] - y[1]) % x[3] != 0

    def hit(x, y):
        return x[0] == y[0] and (bank(x) or (x[1] < y[2] and y[1] < x[2] and not apart(x, y)))

    deps = []
    for i, o in enumerate(ops):
        d = set()
        for j in range(i):
            p = ops[j]
            if any(hit(x, y) for x in o["r"] for y in p["w"]) or any(hit(x, y) for x in o["w"] for y in p["w"] + p["r"]):
                d.add(j)
            elif p["q"] != o["q"] and any(bank(x) and hit(x, y) for x in o["r"] for y in p["r"]):
                d.add(j)
        deps.append(d)
    known, done_at, waits = {q: set() for q in eng}, [], []
    for i, o in enumerate(ops):
        q = o["q"]
        if q is None:
            done_at.append({i})
            waits.append([])
            continue
        need = []
        for j in sorted(deps[i], reverse=True):
            if j not in known[q]:
                need.append(j)
                known[q] |= done_at[j]
        waits.append(need)
        mine = set(known[q]) | {i}
        if o["kind"] == "c":
            mine |= {j for j in range(i) if ops[j]["q"] == q and ops[j]["kind"] == "c"}
        done_at.append(mine)
    target = {j for w in waits for j in w}
    count, token, nd = {q: 0 for q in eng}, {}, 0
    for i, o in enumerate(ops):
        q = o["q"]
        if q is None:
            token[i] = (T.sem[o["arrive"]], o["n"])
            continue
        for j in waits[i]:
            eng[q].wait_ge(*token[j])
        if o["kind"] == "c":
            ins = o["fn"]()
            if i in target:
                count[q] += 1
                ins.then_inc(T.sem[q], 1)
                token[i] = (T.sem[q], count[q])
        else:
            s = T.sem["d%d" % nd]
            nd += 1
            token[i] = (s, o["n"])
            if o["kind"] == "d":
                o["fn"]().then_inc(s, 16)
            else:
                o["fn"](s)
    for i, o in enumerate(ops):
        if o["kind"] in "dr" and i not in target:
            eng["g" if o["kind"] == "r" else o["q"]].wait_ge(*token[i])
